import numpy as np
import ml_dtypes


def mxq(x, axis, fmt="e4m3"):
    dtype, down = {"e4m3": (ml_dtypes.float8_e4m3fn, 7), "e5m2": (ml_dtypes.float8_e5m2, 14)}[fmt]
    v = np.moveaxis(np.asarray(x, np.float32).astype(ml_dtypes.bfloat16).astype(np.float64), axis, -1)
    blocks = v.reshape(v.shape[:-1] + (-1, 32))
    amax = np.abs(blocks).max(-1, keepdims=True)
    byte = np.maximum(np.where(amax > 0, np.frexp(amax)[1] - 1 + 127, 0) - down, 1)
    scale = np.exp2(byte - 127.0)
    codes = (blocks / scale).astype(np.float32).astype(dtype).astype(np.float64)
    return np.moveaxis((codes * scale).reshape(v.shape), -1, axis)


WIDE = False


def mx_kscale(k):
    if not WIDE:
        return np.ones(k)
    levels = np.array([10, -10, 5, -5, 0])
    if k % 512:
        return np.exp2(np.random.permutation(np.resize(levels, k // 32))).repeat(32)
    a = np.empty((k // 512, 16))
    for p in range(k // 512):
        a[p, :8] = np.random.permutation(np.resize(levels, 8))
        for g in range(8):
            far = levels[np.abs(levels - a[p, g]) >= 10]
            a[p, g + 8] = far[np.random.randint(len(far))]
    return np.exp2(a.ravel()).repeat(32)


def f64(x):
    return np.asarray(x).astype(np.float64)


def striped(idx):
    return np.tile(idx.reshape(-1, 16).T, (8, 1)).astype(np.uint16)


def unstriped(offs):
    return offs[:16].T.reshape(-1).astype(np.int64)


def pack_weight(w):
    k, n = w.shape
    w = f64(np.asarray(w, np.float32).astype(ml_dtypes.bfloat16)).reshape(k // 32, 32, n)
    amax = np.abs(w).max(1)
    byte = np.clip(np.where(amax > 0, np.frexp(amax)[1] - 1 + 127 - 7, 1), 1, 254)
    scaled = (w * np.exp2(127.0 - byte)[:, None, :]).reshape(k, n).astype(np.float32)
    words = np.ascontiguousarray(scaled.reshape(k // 512, 128, 4, n).transpose(0, 1, 3, 2)).astype(ml_dtypes.float8_e4m3fn).view(np.uint8)
    return words, np.ascontiguousarray(byte.astype(np.uint8).reshape(k // 512, 16, n))


def unpack_weight(words, scales):
    g, p, n, _ = words.shape
    vals = np.ascontiguousarray(words).view(ml_dtypes.float8_e4m3fn).astype(np.float64) * np.repeat(np.exp2(scales.astype(np.float64) - 127.0), 8, axis=1)[..., None]
    return vals.transpose(0, 1, 3, 2).reshape(g * 512, n)


def silu(v):
    return v / (1.0 + np.exp(-np.maximum(v, -700.0)))


K, T, E, C, N = 1024, 1024, 16, 256, 128
TOP = 4


def by_expert(wq, xq):
    return np.concatenate([wq[e].T @ xq[:, e * C:(e + 1) * C] for e in range(E)], axis=1)


def setup_inputs():
    n = np.random.standard_normal
    s = mx_kscale(K)[:, None]
    deal = np.repeat(np.arange(E), C).reshape(TOP, T)[:, np.random.permutation(T)]
    deal = np.take_along_axis(deal, np.argsort(np.random.rand(TOP, T), axis=0), axis=0)
    for _ in range(8):
        s_, t_ = np.random.permutation(T).reshape(2, -1); r = np.random.randint(TOP, size=T // 2); x, y = deal[r, s_].copy(), deal[r, t_].copy()
        ok = ~((deal[:, s_] == y).any(0) | (deal[:, t_] == x).any(0)); deal[r[ok], s_[ok]] = y[ok]; deal[r[ok], t_[ok]] = x[ok]
    order = np.lexsort((np.random.rand(TOP * T), deal.reshape(-1)))
    slot_token = order % T; pos = np.empty(TOP * T, np.int64); pos[order] = np.arange(TOP * T); pos = pos.reshape(TOP, T)
    g = np.random.uniform(0.5, 1.5, (TOP, T)); g = g / g.sum(0)
    packed = [pack_weight(m) for m in n((E, K, N)) / np.sqrt(K) / s[None]]
    w_slot = np.empty(E * C)
    for r in range(TOP): w_slot[pos[r]] = g[r]
    return {
        "xT": (n((K, T)) * s).astype(np.float32),
        "w_words": np.stack([m[0] for m in packed]),
        "w_scales": np.stack([m[1] for m in packed]),
        "b": (0.3 * n((N, E))).astype(np.float32),
        "gate": np.tile(w_slot, (K, 1)).astype(np.float32),
        "offs": striped(slot_token),
        "pos1": striped(pos[0]),
        "pos2": striped(pos[1]),
        "pos3": striped(pos[2]),
        "pos4": striped(pos[3]),
    }


def reference(xT, w_words, w_scales, b, gate, offs, pos1, pos2, pos3, pos4):
    idx = unstriped(offs)
    w = np.stack([unpack_weight(w_words[e], w_scales[e]) for e in range(E)])
    xq = mxq(f64(gate) * f64(xT)[:, idx], 0, "e4m3")
    y = by_expert(w, xq)
    y = silu(y + np.repeat(f64(b), C, axis=1))
    return y[:, unstriped(pos1)] + y[:, unstriped(pos2)] + y[:, unstriped(pos3)] + y[:, unstriped(pos4)]

@@ -1,0 +1,160 @@
+from contextlib import ExitStack
+
+import concourse.mybir as mybir
+
+K, T, E, C, N = 1024, 1024, 16, 256, 128
+TOP = 4
+S = E * C
+P = 128
+PACK = 4
+K_PASS = P * PACK
+PASSES = K // K_PASS
+LIST = 16
+SPARE = 16
+
+F32 = mybir.dt.float32
+BF16 = mybir.dt.bfloat16
+I32 = mybir.dt.int32
+U32 = mybir.dt.uint32
+U16 = mybir.dt.uint16
+U8 = mybir.dt.uint8
+FP8X4 = mybir.dt.float8_e4m3fn_x4
+MULT = mybir.AluOpType.mult
+ADD = mybir.AluOpType.add
+SILU = mybir.ActivationFunctionType.Silu
+
+FLOPS = 2 * K * S * N
+BYTES = K * T * 4 + E * K * N + E * K * N // 32 + N * E * 4 + S * 4 + P * (S + TOP * T) // LIST * 2 + N * T * 4
+
+CHUNKS = [1024, 1024, 1024, 512, 256, 128, 128]
+GATE_TILE = 1024
+FIRST_GATHER = 256
+LAST_SUMS = [(0, 512), (512, 768), (768, 1024)]
+W_GROUP = 4
+TOKEN_HALF = T // 2
+
+
+def tile_moe_pre_lin_silu_kernel(
+    tc, xT, w_words, w_scales, b, gate, offs, pos1, pos2, pos3, pos4, out
+):
+    nc = tc.nc
+    with ExitStack() as ctx:
+        lists = ctx.enter_context(tc.tile_pool(name="lists", bufs=1))
+        keep = ctx.enter_context(tc.tile_pool(name="keep", bufs=1))
+        ring = ctx.enter_context(tc.tile_pool(name="ring", bufs=3))
+        psum = ctx.enter_context(tc.psum_pool(name="psum", bufs=4))
+
+        planes = [keep.tile([P, T + SPARE], F32, name=f"plane{i}") for i in range(PASSES * PACK)]
+        for plane in planes:
+            nc.vector.memset(plane[:, T:], 0.0)
+        w_scale = keep.tile([P, E * PASSES, N], U8, align_bytes=64)
+        nc.vector.memset(w_scale[:].bitcast(I32), 0)
+
+        def load_plane(i):
+            a, r = divmod(i, PACK)
+            rows = xT[a * K_PASS : (a + 1) * K_PASS, :].rearrange("(p r) t -> p r t", r=PACK)
+            nc.sync.dma_start(planes[i][:, :T], rows[:, r, :])
+
+        gates = [keep.tile([P, GATE_TILE], F32, name=f"gate{g}") for g in range(S // GATE_TILE)]
+
+        def load_gate(lo, hi):
+            g, start = divmod(lo, GATE_TILE)
+            nc.sync.dma_start(gates[g][:, start : start + hi - lo], gate[:P, lo:hi])
+
+        w_codes = []
+
+        def load_weights():
+            e0 = len(w_codes) * W_GROUP
+            group = keep.tile([P, W_GROUP * PASSES, N * PACK], U8, align_bytes=64, name=f"w{e0}")
+            words = w_words[e0 : e0 + W_GROUP].rearrange("e a p n r -> p (e a) (n r)")
+            nc.sync.dma_start(group[:].bitcast(I32), words.bitcast(I32))
+            w_codes.append(group)
+
+        slot_tokens = lists.tile([P, S // LIST], U16)
+        nc.sync.dma_start(slot_tokens[:], offs)
+        load_plane(0)
+        load_gate(0, FIRST_GATHER)
+        load_gate(FIRST_GATHER, GATE_TILE)
+        for i in range(1, 5):
+            load_plane(i)
+        scale_rows = w_scales.rearrange("e a (q r) n -> r q (e a) n", r=4)
+        for r in range(4):
+            nc.sync.dma_start(w_scale[r:P:32, :, :].bitcast(I32), scale_rows[r].bitcast(I32))
+        for i in range(5, 8):
+            load_plane(i)
+        bias = keep.tile([N, E], F32)
+        nc.sync.dma_start(bias[:], b)
+        load_weights()
+        load_gate(GATE_TILE, 2 * GATE_TILE)
+        for g in range(1, E // W_GROUP):
+            load_weights()
+        for g in range(2, S // GATE_TILE):
+            load_gate(g * GATE_TILE, (g + 1) * GATE_TILE)
+        token_slots = []
+        for j, pos in enumerate((pos1, pos2, pos3, pos4)):
+            slots = lists.tile([P, T // LIST], U16, name=f"pos{j}")
+            nc.sync.dma_start(slots[:], pos)
+            token_slots.append(slots)
+
+        y = keep.tile([N, S], F32)
+
+        s0 = 0
+        for ci, width in enumerate(CHUNKS):
+            s1 = s0 + width
+            quantised = []
+            for a in range(PASSES):
+                gated = ring.tile([P, PACK, width], F32, tag="gated")
+                for r in range(PACK):
+                    cuts = [s0, FIRST_GATHER, s1] if (s0, a, r) == (0, 0, 0) else [s0, s1]
+                    for lo, hi in zip(cuts, cuts[1:]):
+                        g, start = divmod(lo, GATE_TILE)
+                        nc.vector.tensor_tensor(
+                            gated[:, r, lo - s0 : hi - s0],
+                            planes[a * PACK + r][:].indirect(slot_tokens[:, lo // LIST : hi // LIST]),
+                            gates[g][:, start : start + hi - lo],
+                            MULT,
+                        )
+                woven = ring.tile([P, width, PACK], BF16, tag="woven", align_bytes=64)
+                nc.scalar.copy(
+                    woven[:].rearrange("p (c i) r -> p c r i", i=4),
+                    gated[:].rearrange("p r (c i) -> p c r i", i=4),
+                )
+                codes = keep.tile([P, width], U32, align_bytes=64, name=f"codes{ci}_{a}")
+                scales = keep.tile([P, width], U8, align_bytes=64, name=f"scales{ci}_{a}")
+                nc.vector.quantize_mx(
+                    out=codes[:].bitcast(FP8X4), scales=scales[:], in_=woven[:].rearrange("p c r -> p (c r)")
+                )
+                quantised.append((codes, scales))
+            run = min(width, C)
+            for c0 in range(0, width, run):
+                e = (s0 + c0) // C
+                acc = psum.tile([N, run], F32, tag="acc")
+                for a, (codes, scales) in enumerate(quantised):
+                    nc.tensor.matmul_mx(
+                        out=acc[:],
+                        lhsT=w_codes[e // W_GROUP][:, (e % W_GROUP) * PASSES + a, :].bitcast(FP8X4),
+                        lhsT_scale=w_scale[:, e * PASSES + a, :],
+                        rhs=codes[:, c0 : c0 + run].bitcast(FP8X4),
+                        rhs_scale=scales[:, c0 : c0 + run],
+                        start=(a == 0),
+                        stop=(a == PASSES - 1),
+                    )
+                nc.scalar.activation(y[:, s0 + c0 : s0 + c0 + run], acc[:], SILU, bias=bias[:, e : e + 1])
+            s0 = s1
+
+        sums = {}
+        for j, slots in enumerate(token_slots[:-1]):
+            for t0 in range(0, T, TOKEN_HALF):
+                picked = y[:].indirect(slots[:, t0 // LIST : (t0 + TOKEN_HALF) // LIST])
+                total = keep.tile([N, TOKEN_HALF], F32, name=f"sum{j}_{t0}")
+                if j == 0:
+                    nc.vector.tensor_copy(total[:], picked)
+                else:
+                    nc.vector.tensor_tensor(total[:], picked, sums[t0][:], ADD)
+                sums[t0] = total
+        for t0, t1 in LAST_SUMS:
+            half = t0 // TOKEN_HALF * TOKEN_HALF
+            result = keep.tile([N, t1 - t0], F32, name=f"result{t0}")
+            picked = y[:].indirect(token_slots[-1][:, t0 // LIST : t1 // LIST])
+            nc.vector.tensor_tensor(result[:], picked, sums[half][:, t0 - half : t1 - half], ADD)
+            nc.sync.dma_start(out[:, t0:t1], result[:])

@@ -26,7 +26,8 @@ SILU = mybir.ActivationFunctionType.Silu
 FLOPS = 2 * K * S * N
 BYTES = K * T * 4 + E * K * N + E * K * N // 32 + N * E * 4 + S * 4 + P * (S + TOP * T) // LIST * 2 + N * T * 4
 
-CHUNKS = [1024, 1024, 1024, 512, 256, 128, 128]
+UNITS = [(a, lo, lo + 1024) for lo in (0, 1024, 2048) for a in (0, 1)] + [
+    (0, 3072, 4096), (1, 3072, 3584), (1, 3584, 3840), (1, 3840, 3968), (1, 3968, 4096)]
 GATE_TILE = 1024
 FIRST_GATHER = 256
 LAST_SUMS = [(0, 512), (512, 768), (768, 1024)]
@@ -42,20 +43,21 @@ def tile_moe_pre_lin_silu_kernel(
         lists = ctx.enter_context(tc.tile_pool(name="lists", bufs=1))
         keep = ctx.enter_context(tc.tile_pool(name="keep", bufs=1))
         ring = ctx.enter_context(tc.tile_pool(name="ring", bufs=3))
+        ring4 = ctx.enter_context(tc.tile_pool(name="ring4", bufs=2))
         psum = ctx.enter_context(tc.psum_pool(name="psum", bufs=4))
 
         planes = [keep.tile([P, T + SPARE], F32, name=f"plane{i}") for i in range(PASSES * PACK)]
         for plane in planes:
-            nc.vector.memset(plane[:, T:], 0.0)
+            nc.gpsimd.memset(plane[:, T:], 0.0)
         w_scale = keep.tile([P, E * PASSES, N], U8, align_bytes=64)
-        nc.vector.memset(w_scale[:].bitcast(I32), 0)
+        nc.gpsimd.memset(w_scale[:].bitcast(I32), 0)
 
         def load_plane(i):
             a, r = divmod(i, PACK)
             rows = xT[a * K_PASS : (a + 1) * K_PASS, :].rearrange("(p r) t -> p r t", r=PACK)
             nc.sync.dma_start(planes[i][:, :T], rows[:, r, :])
 
-        gates = [keep.tile([P, GATE_TILE], F32, name=f"gate{g}") for g in range(S // GATE_TILE)]
+        gates = [keep.tile([P, GATE_TILE], F32, align_bytes=64, tag=f"gate{g}", name=f"gate{g}") for g in range(S // GATE_TILE)]
 
         def load_gate(lo, hi):
             g, start = divmod(lo, GATE_TILE)
@@ -75,21 +77,17 @@ def tile_moe_pre_lin_silu_kernel(
         load_plane(0)
         load_gate(0, FIRST_GATHER)
         load_gate(FIRST_GATHER, GATE_TILE)
-        for i in range(1, 5):
+        for i in range(1, 8):
             load_plane(i)
+        for g in range(1, S // GATE_TILE):
+            load_gate(g * GATE_TILE, (g + 1) * GATE_TILE)
         scale_rows = w_scales.rearrange("e a (q r) n -> r q (e a) n", r=4)
         for r in range(4):
             nc.sync.dma_start(w_scale[r:P:32, :, :].bitcast(I32), scale_rows[r].bitcast(I32))
-        for i in range(5, 8):
-            load_plane(i)
         bias = keep.tile([N, E], F32)
         nc.sync.dma_start(bias[:], b)
-        load_weights()
-        load_gate(GATE_TILE, 2 * GATE_TILE)
-        for g in range(1, E // W_GROUP):
+        for g in range(E // W_GROUP):
             load_weights()
-        for g in range(2, S // GATE_TILE):
-            load_gate(g * GATE_TILE, (g + 1) * GATE_TILE)
         token_slots = []
         for j, pos in enumerate((pos1, pos2, pos3, pos4)):
             slots = lists.tile([P, T // LIST], U16, name=f"pos{j}")
@@ -98,38 +96,12 @@ def tile_moe_pre_lin_silu_kernel(
 
         y = keep.tile([N, S], F32)
 
-        s0 = 0
-        for ci, width in enumerate(CHUNKS):
-            s1 = s0 + width
-            quantised = []
-            for a in range(PASSES):
-                gated = ring.tile([P, PACK, width], F32, tag="gated")
-                for r in range(PACK):
-                    cuts = [s0, FIRST_GATHER, s1] if (s0, a, r) == (0, 0, 0) else [s0, s1]
-                    for lo, hi in zip(cuts, cuts[1:]):
-                        g, start = divmod(lo, GATE_TILE)
-                        nc.vector.tensor_tensor(
-                            gated[:, r, lo - s0 : hi - s0],
-                            planes[a * PACK + r][:].indirect(slot_tokens[:, lo // LIST : hi // LIST]),
-                            gates[g][:, start : start + hi - lo],
-                            MULT,
-                        )
-                woven = ring.tile([P, width, PACK], BF16, tag="woven", align_bytes=64)
-                nc.scalar.copy(
-                    woven[:].rearrange("p (c i) r -> p c r i", i=4),
-                    gated[:].rearrange("p r (c i) -> p c r i", i=4),
-                )
-                codes = keep.tile([P, width], U32, align_bytes=64, name=f"codes{ci}_{a}")
-                scales = keep.tile([P, width], U8, align_bytes=64, name=f"scales{ci}_{a}")
-                nc.vector.quantize_mx(
-                    out=codes[:].bitcast(FP8X4), scales=scales[:], in_=woven[:].rearrange("p c r -> p (c r)")
-                )
-                quantised.append((codes, scales))
-            run = min(width, C)
-            for c0 in range(0, width, run):
-                e = (s0 + c0) // C
+        def multiply(base, span, operands):
+            run = min(span, C)
+            for c0 in range(0, span, run):
+                e = (base + c0) // C
                 acc = psum.tile([N, run], F32, tag="acc")
-                for a, (codes, scales) in enumerate(quantised):
+                for a, (codes, scales) in enumerate(operands):
                     nc.tensor.matmul_mx(
                         out=acc[:],
                         lhsT=w_codes[e // W_GROUP][:, (e % W_GROUP) * PASSES + a, :].bitcast(FP8X4),
@@ -139,8 +111,47 @@ def tile_moe_pre_lin_silu_kernel(
                         start=(a == 0),
                         stop=(a == PASSES - 1),
                     )
-                nc.scalar.activation(y[:, s0 + c0 : s0 + c0 + run], acc[:], SILU, bias=bias[:, e : e + 1])
-            s0 = s1
+                nc.scalar.activation(y[:, base + c0 : base + c0 + run], acc[:], SILU, bias=bias[:, e : e + 1])
+
+        made = {}
+
+        def quantise(a, lo, hi, woven):
+            width = hi - lo
+            if a == 0 and hi < S:
+                codes = keep.tile([P, width], U32, align_bytes=64, tag=f"gate{lo // GATE_TILE}", name=f"codes{a}_{lo}")
+            else:
+                codes = keep.tile([P, width], U32, align_bytes=64, name=f"codes{a}_{lo}")
+            scales = keep.tile([P, width], U8, align_bytes=64, name=f"scales{a}_{lo}")
+            nc.vector.quantize_mx(
+                out=codes[:].bitcast(FP8X4), scales=scales[:], in_=woven[:].rearrange("p c r -> p (c r)")
+            )
+            made[a] = (lo, codes, scales)
+            if a == PASSES - 1:
+                multiply(lo, width, [(c[:, lo - at : hi - at], s[:, lo - at : hi - at]) for at, c, s in (made[0], made[1])])
+
+        due = []
+        for a, s0, s1 in UNITS:
+            width = s1 - s0
+            gated = ring4.tile([P, PACK, width], F32, tag="gated")
+            for r in range(PACK):
+                cuts = [s0, FIRST_GATHER, s1] if (s0, a, r) == (0, 0, 0) else [s0, s1]
+                for lo, hi in zip(cuts, cuts[1:]):
+                    g, start = divmod(lo, GATE_TILE)
+                    nc.vector.tensor_tensor(
+                        gated[:, r, lo - s0 : hi - s0],
+                        planes[a * PACK + r][:].indirect(slot_tokens[:, lo // LIST : hi // LIST]),
+                        gates[g][:, start : start + hi - lo],
+                        MULT,
+                    )
+            woven = ring.tile([P, width, PACK], BF16, tag="woven", align_bytes=64)
+            nc.scalar.copy(
+                woven[:].rearrange("p (c i) r -> p c r i", i=4),
+                gated[:].rearrange("p r (c i) -> p c r i", i=4),
+            )
+            if due:
+                quantise(*due.pop())
+            due.append((a, s0, s1, woven))
+        quantise(*due.pop())
 
         sums = {}
         for j, slots in enumerate(token_slots[:-1]):

@@ -29,9 +29,10 @@ BYTES = K * T * 4 + E * K * N + E * K * N // 32 + N * E * 4 + S * 4 + P * (S + T
 UNITS = [(a, lo, lo + 1024) for lo in (0, 1024, 2048) for a in (0, 1)] + [
     (0, 3072, 4096), (1, 3072, 3584), (1, 3584, 3840), (1, 3840, 3968), (1, 3968, 4096)]
 GATE_TILE = 1024
-FIRST_GATHER = 256
-LAST_SUMS = [(0, 512), (512, 768), (768, 1024)]
+FIRST_CUTS = [0, 128, 384, 1024]
+LAST_SUMS = [(0, 512), (512, 768), (768, 896), (896, 1024)]
 W_GROUP = 4
+LAG = 2
 TOKEN_HALF = T // 2
 
 
@@ -42,8 +43,8 @@ def tile_moe_pre_lin_silu_kernel(
     with ExitStack() as ctx:
         lists = ctx.enter_context(tc.tile_pool(name="lists", bufs=1))
         keep = ctx.enter_context(tc.tile_pool(name="keep", bufs=1))
-        ring = ctx.enter_context(tc.tile_pool(name="ring", bufs=3))
-        ring4 = ctx.enter_context(tc.tile_pool(name="ring4", bufs=2))
+        ring = ctx.enter_context(tc.tile_pool(name="ring", bufs=4))
+        ring4 = ctx.enter_context(tc.tile_pool(name="ring4", bufs=3))
         psum = ctx.enter_context(tc.psum_pool(name="psum", bufs=4))
 
         planes = [keep.tile([P, T + SPARE], F32, name=f"plane{i}") for i in range(PASSES * PACK)]
@@ -75,8 +76,8 @@ def tile_moe_pre_lin_silu_kernel(
         slot_tokens = lists.tile([P, S // LIST], U16)
         nc.sync.dma_start(slot_tokens[:], offs)
         load_plane(0)
-        load_gate(0, FIRST_GATHER)
-        load_gate(FIRST_GATHER, GATE_TILE)
+        for lo, hi in zip(FIRST_CUTS, FIRST_CUTS[1:]):
+            load_gate(lo, hi)
         for i in range(1, 8):
             load_plane(i)
         for g in range(1, S // GATE_TILE):
@@ -134,7 +135,7 @@ def tile_moe_pre_lin_silu_kernel(
             width = s1 - s0
             gated = ring4.tile([P, PACK, width], F32, tag="gated")
             for r in range(PACK):
-                cuts = [s0, FIRST_GATHER, s1] if (s0, a, r) == (0, 0, 0) else [s0, s1]
+                cuts = FIRST_CUTS if (s0, a, r) == (0, 0, 0) else [s0, s1]
                 for lo, hi in zip(cuts, cuts[1:]):
                     g, start = divmod(lo, GATE_TILE)
                     nc.vector.tensor_tensor(
@@ -148,10 +149,11 @@ def tile_moe_pre_lin_silu_kernel(
                 woven[:].rearrange("p (c i) r -> p c r i", i=4),
                 gated[:].rearrange("p r (c i) -> p c r i", i=4),
             )
-            if due:
-                quantise(*due.pop())
             due.append((a, s0, s1, woven))
-        quantise(*due.pop())
+            if len(due) > LAG:
+                quantise(*due.pop(0))
+        for unit in due:
+            quantise(*unit)
 
         sums = {}
         for j, slots in enumerate(token_slots[:-1]):

@@ -10,7 +10,6 @@ PACK = 4
 K_PASS = P * PACK
 PASSES = K // K_PASS
 LIST = 16
-SPARE = 16
 
 F32 = mybir.dt.float32
 BF16 = mybir.dt.bfloat16
@@ -26,14 +25,16 @@ SILU = mybir.ActivationFunctionType.Silu
 FLOPS = 2 * K * S * N
 BYTES = K * T * 4 + E * K * N + E * K * N // 32 + N * E * 4 + S * 4 + P * (S + TOP * T) // LIST * 2 + N * T * 4
 
-UNITS = [(a, lo, lo + 1024) for lo in (0, 1024, 2048) for a in (0, 1)] + [
-    (0, 3072, 4096), (1, 3072, 3584), (1, 3584, 3840), (1, 3840, 3968), (1, 3968, 4096)]
-GATE_TILE = 1024
-FIRST_CUTS = [0, 128, 384, 1024]
-LAST_SUMS = [(0, 512), (512, 768), (768, 896), (896, 1024)]
+WIDE = 2048
+WINDOW = WIDE + LIST
+QUANT = 1024
+UNITS = [(0, 0, 2048), (1, 0, 2048), (0, 2048, 4096), (1, 2048, 3072), (1, 3072, 3584), (1, 3584, 3840)]
+LAST_UNITS = [(1, 3840, 3968), (1, 3968, 4096)]
+FIRST_CUTS = [0, 128, 384, 960, 2048]
+TOKEN_SPLIT = 512
+LAST_SUMS = [(0, 512), (512, 896), (896, 1024)]
 W_GROUP = 4
-LAG = 2
-TOKEN_HALF = T // 2
+VECTOR_CLEARS = 2
 
 
 def tile_moe_pre_lin_silu_kernel(
@@ -43,13 +44,16 @@ def tile_moe_pre_lin_silu_kernel(
     with ExitStack() as ctx:
         lists = ctx.enter_context(tc.tile_pool(name="lists", bufs=1))
         keep = ctx.enter_context(tc.tile_pool(name="keep", bufs=1))
-        ring = ctx.enter_context(tc.tile_pool(name="ring", bufs=4))
-        ring4 = ctx.enter_context(tc.tile_pool(name="ring4", bufs=3))
+        two = ctx.enter_context(tc.tile_pool(name="two", bufs=2))
+        three = ctx.enter_context(tc.tile_pool(name="three", bufs=3))
         psum = ctx.enter_context(tc.psum_pool(name="psum", bufs=4))
 
-        planes = [keep.tile([P, T + SPARE], F32, name=f"plane{i}") for i in range(PASSES * PACK)]
-        for plane in planes:
-            nc.gpsimd.memset(plane[:, T:], 0.0)
+        planes = [
+            keep.tile([P, WINDOW], F32, align_bytes=64, tag=f"plane{i}", name=f"plane{i}") for i in range(PASSES * PACK)
+        ]
+        for i, plane in enumerate(planes):
+            engine = nc.vector if i < VECTOR_CLEARS else nc.gpsimd
+            engine.memset(plane[:, T:].bitcast(I32), 0)
         w_scale = keep.tile([P, E * PASSES, N], U8, align_bytes=64)
         nc.gpsimd.memset(w_scale[:].bitcast(I32), 0)
 
@@ -58,37 +62,31 @@ def tile_moe_pre_lin_silu_kernel(
             rows = xT[a * K_PASS : (a + 1) * K_PASS, :].rearrange("(p r) t -> p r t", r=PACK)
             nc.sync.dma_start(planes[i][:, :T], rows[:, r, :])
 
-        gates = [keep.tile([P, GATE_TILE], F32, align_bytes=64, tag=f"gate{g}", name=f"gate{g}") for g in range(S // GATE_TILE)]
+        gates = [keep.tile([P, WIDE], F32, name=f"gate{g}") for g in range(S // WIDE)]
 
         def load_gate(lo, hi):
-            g, start = divmod(lo, GATE_TILE)
+            g, start = divmod(lo, WIDE)
             nc.sync.dma_start(gates[g][:, start : start + hi - lo], gate[:P, lo:hi])
 
-        w_codes = []
-
-        def load_weights():
-            e0 = len(w_codes) * W_GROUP
-            group = keep.tile([P, W_GROUP * PASSES, N * PACK], U8, align_bytes=64, name=f"w{e0}")
-            words = w_words[e0 : e0 + W_GROUP].rearrange("e a p n r -> p (e a) (n r)")
-            nc.sync.dma_start(group[:].bitcast(I32), words.bitcast(I32))
-            w_codes.append(group)
-
         slot_tokens = lists.tile([P, S // LIST], U16)
-        nc.sync.dma_start(slot_tokens[:], offs)
         load_plane(0)
+        nc.sync.dma_start(slot_tokens[:], offs)
         for lo, hi in zip(FIRST_CUTS, FIRST_CUTS[1:]):
             load_gate(lo, hi)
-        for i in range(1, 8):
+        for i in range(1, PASSES * PACK):
             load_plane(i)
-        for g in range(1, S // GATE_TILE):
-            load_gate(g * GATE_TILE, (g + 1) * GATE_TILE)
+        load_gate(WIDE, S)
         scale_rows = w_scales.rearrange("e a (q r) n -> r q (e a) n", r=4)
         for r in range(4):
             nc.sync.dma_start(w_scale[r:P:32, :, :].bitcast(I32), scale_rows[r].bitcast(I32))
         bias = keep.tile([N, E], F32)
         nc.sync.dma_start(bias[:], b)
-        for g in range(E // W_GROUP):
-            load_weights()
+        w_codes = []
+        for e0 in range(0, E, W_GROUP):
+            group = keep.tile([P, W_GROUP * PASSES, N * PACK], U8, align_bytes=64, name=f"w{e0}")
+            words = w_words[e0 : e0 + W_GROUP].rearrange("e a p n r -> p (e a) (n r)")
+            nc.sync.dma_start(group[:].bitcast(I32), words.bitcast(I32))
+            w_codes.append(group)
         token_slots = []
         for j, pos in enumerate((pos1, pos2, pos3, pos4)):
             slots = lists.tile([P, T // LIST], U16, name=f"pos{j}")
@@ -96,78 +94,91 @@ def tile_moe_pre_lin_silu_kernel(
             token_slots.append(slots)
 
         y = keep.tile([N, S], F32)
+        first_pass = {}
 
-        def multiply(base, span, operands):
-            run = min(span, C)
-            for c0 in range(0, span, run):
-                e = (base + c0) // C
-                acc = psum.tile([N, run], F32, tag="acc")
-                for a, (codes, scales) in enumerate(operands):
-                    nc.tensor.matmul_mx(
-                        out=acc[:],
-                        lhsT=w_codes[e // W_GROUP][:, (e % W_GROUP) * PASSES + a, :].bitcast(FP8X4),
-                        lhsT_scale=w_scale[:, e * PASSES + a, :],
-                        rhs=codes[:, c0 : c0 + run].bitcast(FP8X4),
-                        rhs_scale=scales[:, c0 : c0 + run],
-                        start=(a == 0),
-                        stop=(a == PASSES - 1),
-                    )
-                nc.scalar.activation(y[:, base + c0 : base + c0 + run], acc[:], SILU, bias=bias[:, e : e + 1])
-
-        made = {}
-
-        def quantise(a, lo, hi, woven):
-            width = hi - lo
-            if a == 0 and hi < S:
-                codes = keep.tile([P, width], U32, align_bytes=64, tag=f"gate{lo // GATE_TILE}", name=f"codes{a}_{lo}")
-            else:
-                codes = keep.tile([P, width], U32, align_bytes=64, name=f"codes{a}_{lo}")
-            scales = keep.tile([P, width], U8, align_bytes=64, name=f"scales{a}_{lo}")
-            nc.vector.quantize_mx(
-                out=codes[:].bitcast(FP8X4), scales=scales[:], in_=woven[:].rearrange("p c r -> p (c r)")
-            )
-            made[a] = (lo, codes, scales)
-            if a == PASSES - 1:
-                multiply(lo, width, [(c[:, lo - at : hi - at], s[:, lo - at : hi - at]) for at, c, s in (made[0], made[1])])
-
-        due = []
-        for a, s0, s1 in UNITS:
-            width = s1 - s0
-            gated = ring4.tile([P, PACK, width], F32, tag="gated")
+        def gather(a, s0, s1, gated):
             for r in range(PACK):
                 cuts = FIRST_CUTS if (s0, a, r) == (0, 0, 0) else [s0, s1]
                 for lo, hi in zip(cuts, cuts[1:]):
-                    g, start = divmod(lo, GATE_TILE)
+                    g, start = divmod(lo, WIDE)
                     nc.vector.tensor_tensor(
                         gated[:, r, lo - s0 : hi - s0],
                         planes[a * PACK + r][:].indirect(slot_tokens[:, lo // LIST : hi // LIST]),
                         gates[g][:, start : start + hi - lo],
                         MULT,
                     )
-            woven = ring.tile([P, width, PACK], BF16, tag="woven", align_bytes=64)
-            nc.scalar.copy(
-                woven[:].rearrange("p (c i) r -> p c r i", i=4),
-                gated[:].rearrange("p r (c i) -> p c r i", i=4),
-            )
-            due.append((a, s0, s1, woven))
-            if len(due) > LAG:
-                quantise(*due.pop(0))
-        for unit in due:
-            quantise(*unit)
+            pieces = []
+            for lo in range(s0, s1, QUANT):
+                hi = min(lo + QUANT, s1)
+                woven = three.tile([P, hi - lo, PACK], BF16, tag="woven", align_bytes=64)
+                nc.scalar.copy(
+                    woven[:].rearrange("p (c i) r -> p c r i", i=4),
+                    gated[:, :, lo - s0 : hi - s0].rearrange("p r (c i) -> p c r i", i=4),
+                )
+                pieces.append((a, lo, hi, woven))
+            return pieces
 
-        sums = {}
-        for j, slots in enumerate(token_slots[:-1]):
-            for t0 in range(0, T, TOKEN_HALF):
-                picked = y[:].indirect(slots[:, t0 // LIST : (t0 + TOKEN_HALF) // LIST])
-                total = keep.tile([N, TOKEN_HALF], F32, name=f"sum{j}_{t0}")
-                if j == 0:
-                    nc.vector.tensor_copy(total[:], picked)
+        def multiply(lo, hi, codes, scales):
+            run = min(hi - lo, C)
+            for s0 in range(lo, hi, run):
+                e = s0 // C
+                codes0, scales0 = first_pass[s0 // QUANT]
+                operands = [
+                    (codes0[:, s0 % QUANT : s0 % QUANT + run], scales0[:, s0 % QUANT : s0 % QUANT + run]),
+                    (codes[:, s0 - lo : s0 - lo + run], scales[:, s0 - lo : s0 - lo + run]),
+                ]
+                acc = psum.tile([N, run], F32, tag="acc")
+                for a, (x_codes, x_scales) in enumerate(operands):
+                    nc.tensor.matmul_mx(
+                        out=acc[:],
+                        lhsT=w_codes[e // W_GROUP][:, (e % W_GROUP) * PASSES + a, :].bitcast(FP8X4),
+                        lhsT_scale=w_scale[:, e * PASSES + a, :],
+                        rhs=x_codes.bitcast(FP8X4),
+                        rhs_scale=x_scales,
+                        start=(a == 0),
+                        stop=(a == PASSES - 1),
+                    )
+                nc.scalar.activation(y[:, s0 : s0 + run], acc[:], SILU, bias=bias[:, e : e + 1])
+
+        def quantise(a, lo, hi, woven):
+            width = hi - lo
+            if a == 0:
+                if lo < WIDE:
+                    codes = keep.tile([P, width], U32, align_bytes=64, name=f"codes{lo}")
                 else:
-                    nc.vector.tensor_tensor(total[:], picked, sums[t0][:], ADD)
-                sums[t0] = total
-        for t0, t1 in LAST_SUMS:
-            half = t0 // TOKEN_HALF * TOKEN_HALF
-            result = keep.tile([N, t1 - t0], F32, name=f"result{t0}")
-            picked = y[:].indirect(token_slots[-1][:, t0 // LIST : t1 // LIST])
-            nc.vector.tensor_tensor(result[:], picked, sums[half][:, t0 - half : t1 - half], ADD)
-            nc.sync.dma_start(out[:, t0:t1], result[:])
+                    codes = keep.tile([P, width], U32, align_bytes=64, tag=f"plane{lo // QUANT - 2}", name=f"codes{lo}")
+                scales = keep.tile([P, width], U8, align_bytes=64, name=f"scales{lo}")
+                first_pass[lo // QUANT] = (codes, scales)
+            else:
+                codes = two.tile([P, width], U32, align_bytes=64, tag="codes")
+                scales = two.tile([P, width], U8, align_bytes=64, tag="scales")
+            nc.vector.quantize_mx(
+                out=codes[:].bitcast(FP8X4), scales=scales[:], in_=woven[:].rearrange("p c r -> p (c r)")
+            )
+            if a == PASSES - 1:
+                multiply(lo, hi, codes, scales)
+
+        due = []
+        for a, s0, s1 in UNITS:
+            gated = two.tile([P, PACK, s1 - s0], F32, tag="gated")
+            pieces = gather(a, s0, s1, gated)
+            for piece in due:
+                quantise(*piece)
+            due = pieces
+        last_gated = two.tile([P, len(LAST_UNITS), PACK, C // 2], F32, tag="gated")
+        for u, (a, s0, s1) in enumerate(LAST_UNITS):
+            due = due + gather(a, s0, s1, last_gated[:, u])
+        for piece in due:
+            quantise(*piece)
+
+        sums = two.tile([N, TOP, T], F32, tag="gated")
+        for j, slots in enumerate(token_slots):
+            parts = LAST_SUMS if j == TOP - 1 else [(0, TOKEN_SPLIT), (TOKEN_SPLIT, T)]
+            for t0, t1 in parts:
+                picked = y[:].indirect(slots[:, t0 // LIST : t1 // LIST])
+                if j == 0:
+                    nc.vector.tensor_copy(sums[:, j, t0:t1], picked)
+                else:
+                    nc.vector.tensor_tensor(sums[:, j, t0:t1], picked, sums[:, j - 1, t0:t1], ADD)
+                if j == TOP - 1:
+                    nc.sync.dma_start(out[:, t0:t1], sums[:, j, t0:t1])

@@ -34,7 +34,6 @@ FIRST_CUTS = [0, 128, 384, 960, 2048]
 TOKEN_SPLIT = 512
 LAST_SUMS = [(0, 512), (512, 896), (896, 1024)]
 W_GROUP = 4
-VECTOR_CLEARS = 2
 
 
 def tile_moe_pre_lin_silu_kernel(
@@ -51,9 +50,9 @@ def tile_moe_pre_lin_silu_kernel(
         planes = [
             keep.tile([P, WINDOW], F32, align_bytes=64, tag=f"plane{i}", name=f"plane{i}") for i in range(PASSES * PACK)
         ]
-        for i, plane in enumerate(planes):
-            engine = nc.vector if i < VECTOR_CLEARS else nc.gpsimd
-            engine.memset(plane[:, T:].bitcast(I32), 0)
+        nc.vector.memset(planes[0][:, T:].bitcast(I32), 0)
+        for plane in planes[1:]:
+            nc.scalar.copy(plane[:, T:], planes[0][:, T:])
         w_scale = keep.tile([P, E * PASSES, N], U8, align_bytes=64)
         nc.gpsimd.memset(w_scale[:].bitcast(I32), 0)
 

@@ -28,12 +28,12 @@ BYTES = K * T * 4 + E * K * N + E * K * N // 32 + N * E * 4 + S * 4 + P * (S + T
 WIDE = 2048
 WINDOW = WIDE + LIST
 QUANT = 1024
-UNITS = [(0, 0, 2048), (1, 0, 2048), (0, 2048, 4096), (1, 2048, 3072), (1, 3072, 3584), (1, 3584, 3840)]
-LAST_UNITS = [(1, 3840, 3968), (1, 3968, 4096)]
+UNITS = [(0, 0, 2048), (1, 0, 2048), (0, 2048, 4096), (1, 2048, 3072), (1, 3072, 3584), (1, 3584, 3840), (1, 3840, 4096)]
 FIRST_CUTS = [0, 128, 384, 960, 2048]
 TOKEN_SPLIT = 512
 LAST_SUMS = [(0, 512), (512, 896), (896, 1024)]
 W_GROUP = 4
+LAST_SLOTS = 128
 
 
 def tile_moe_pre_lin_silu_kernel(
@@ -45,7 +45,7 @@ def tile_moe_pre_lin_silu_kernel(
         keep = ctx.enter_context(tc.tile_pool(name="keep", bufs=1))
         two = ctx.enter_context(tc.tile_pool(name="two", bufs=2))
         three = ctx.enter_context(tc.tile_pool(name="three", bufs=3))
-        psum = ctx.enter_context(tc.psum_pool(name="psum", bufs=4))
+        psum = ctx.enter_context(tc.psum_pool(name="psum", bufs=8))
 
         planes = [
             keep.tile([P, WINDOW], F32, align_bytes=64, tag=f"plane{i}", name=f"plane{i}") for i in range(PASSES * PACK)
@@ -95,8 +95,11 @@ def tile_moe_pre_lin_silu_kernel(
         y = keep.tile([N, S], F32)
         first_pass = {}
 
-        def gather(a, s0, s1, gated):
+        def gather(a, s0, s1, gated, early):
             for r in range(PACK):
+                if r == PACK // 2:
+                    for piece in early:
+                        quantise(*piece)
                 cuts = FIRST_CUTS if (s0, a, r) == (0, 0, 0) else [s0, s1]
                 for lo, hi in zip(cuts, cuts[1:]):
                     g, start = divmod(lo, WIDE)
@@ -106,16 +109,14 @@ def tile_moe_pre_lin_silu_kernel(
                         gates[g][:, start : start + hi - lo],
                         MULT,
                     )
-            pieces = []
-            for lo in range(s0, s1, QUANT):
-                hi = min(lo + QUANT, s1)
+
+        def weave(copy, a, lo, hi, gated):
+            if hi - lo > C:
                 woven = three.tile([P, hi - lo, PACK], BF16, tag="woven", align_bytes=64)
-                nc.scalar.copy(
-                    woven[:].rearrange("p (c i) r -> p c r i", i=4),
-                    gated[:, :, lo - s0 : hi - s0].rearrange("p r (c i) -> p c r i", i=4),
-                )
-                pieces.append((a, lo, hi, woven))
-            return pieces
+            else:
+                woven = keep.tile([P, hi - lo, PACK], BF16, align_bytes=64, name=f"woven{lo}")
+            copy(woven[:].rearrange("p (c i) r -> p c r i", i=4), gated.rearrange("p r (c i) -> p c r i", i=4))
+            return (a, lo, hi, woven)
 
         def multiply(lo, hi, codes, scales):
             run = min(hi - lo, C)
@@ -148,6 +149,9 @@ def tile_moe_pre_lin_silu_kernel(
                     codes = keep.tile([P, width], U32, align_bytes=64, tag=f"plane{lo // QUANT - 2}", name=f"codes{lo}")
                 scales = keep.tile([P, width], U8, align_bytes=64, name=f"scales{lo}")
                 first_pass[lo // QUANT] = (codes, scales)
+            elif width < QUANT:
+                codes = keep.tile([P, width], U32, align_bytes=64, name=f"last_codes{lo}")
+                scales = keep.tile([P, width], U8, align_bytes=64, name=f"last_scales{lo}")
             else:
                 codes = two.tile([P, width], U32, align_bytes=64, tag="codes")
                 scales = two.tile([P, width], U8, align_bytes=64, tag="scales")
@@ -160,13 +164,20 @@ def tile_moe_pre_lin_silu_kernel(
         due = []
         for a, s0, s1 in UNITS:
             gated = two.tile([P, PACK, s1 - s0], F32, tag="gated")
-            pieces = gather(a, s0, s1, gated)
-            for piece in due:
-                quantise(*piece)
-            due = pieces
-        last_gated = two.tile([P, len(LAST_UNITS), PACK, C // 2], F32, tag="gated")
-        for u, (a, s0, s1) in enumerate(LAST_UNITS):
-            due = due + gather(a, s0, s1, last_gated[:, u])
+            early, due = (due, []) if s1 - s0 == WIDE else ([], due)
+            gather(a, s0, s1, gated, early)
+            woven_to = s1 - LAST_SLOTS if (a, s1) == (PASSES - 1, S) else s1
+            pieces = [
+                weave(nc.scalar.copy, a, lo, min(lo + QUANT, woven_to), gated[:, :, lo - s0 : min(lo + QUANT, woven_to) - s0])
+                for lo in range(s0, woven_to, QUANT)
+            ]
+            if s1 - s0 > C:
+                for piece in due:
+                    quantise(*piece)
+                due = []
+            due = due + pieces
+        quantise(*due.pop(0))
+        due.append(weave(nc.vector.tensor_copy, PASSES - 1, S - LAST_SLOTS, S, gated[:, :, C - LAST_SLOTS :]))
         for piece in due:
             quantise(*piece)
 

@@ -33,7 +33,7 @@ FIRST_CUTS = [0, 128, 384, 960, 2048]
 TOKEN_SPLIT = 512
 LAST_SUMS = [(0, 512), (512, 896), (896, 1024)]
 W_GROUP = 4
-LAST_SLOTS = 128
+SCALAR_SHARE = 192
 
 
 def tile_moe_pre_lin_silu_kernel(
@@ -54,7 +54,7 @@ def tile_moe_pre_lin_silu_kernel(
         for plane in planes[1:]:
             nc.scalar.copy(plane[:, T:], planes[0][:, T:])
         w_scale = keep.tile([P, E * PASSES, N], U8, align_bytes=64)
-        nc.gpsimd.memset(w_scale[:].bitcast(I32), 0)
+        nc.vector.memset(w_scale[:].bitcast(I32), 0)
 
         def load_plane(i):
             a, r = divmod(i, PACK)
@@ -110,13 +110,8 @@ def tile_moe_pre_lin_silu_kernel(
                         MULT,
                     )
 
-        def weave(copy, a, lo, hi, gated):
-            if hi - lo > C:
-                woven = three.tile([P, hi - lo, PACK], BF16, tag="woven", align_bytes=64)
-            else:
-                woven = keep.tile([P, hi - lo, PACK], BF16, align_bytes=64, name=f"woven{lo}")
-            copy(woven[:].rearrange("p (c i) r -> p c r i", i=4), gated.rearrange("p r (c i) -> p c r i", i=4))
-            return (a, lo, hi, woven)
+        def weave(copy, woven, gated):
+            copy(woven.rearrange("p (c i) r -> p c r i", i=4), gated.rearrange("p r (c i) -> p c r i", i=4))
 
         def multiply(lo, hi, codes, scales):
             run = min(hi - lo, C)
@@ -145,8 +140,10 @@ def tile_moe_pre_lin_silu_kernel(
             if a == 0:
                 if lo < WIDE:
                     codes = keep.tile([P, width], U32, align_bytes=64, name=f"codes{lo}")
+                elif hi < S:
+                    codes = keep.tile([P, width], U32, align_bytes=64, tag="plane0", name=f"codes{lo}")
                 else:
-                    codes = keep.tile([P, width], U32, align_bytes=64, tag=f"plane{lo // QUANT - 2}", name=f"codes{lo}")
+                    codes = three.tile([P, width], U32, align_bytes=64, tag="woven")
                 scales = keep.tile([P, width], U8, align_bytes=64, name=f"scales{lo}")
                 first_pass[lo // QUANT] = (codes, scales)
             elif width < QUANT:
@@ -156,7 +153,7 @@ def tile_moe_pre_lin_silu_kernel(
                 codes = two.tile([P, width], U32, align_bytes=64, tag="codes")
                 scales = two.tile([P, width], U8, align_bytes=64, tag="scales")
             nc.vector.quantize_mx(
-                out=codes[:].bitcast(FP8X4), scales=scales[:], in_=woven[:].rearrange("p c r -> p (c r)")
+                out=codes[:].bitcast(FP8X4), scales=scales[:], in_=woven.rearrange("p c r -> p (c r)")
             )
             if a == PASSES - 1:
                 multiply(lo, hi, codes, scales)
@@ -166,18 +163,32 @@ def tile_moe_pre_lin_silu_kernel(
             gated = two.tile([P, PACK, s1 - s0], F32, tag="gated")
             early, due = (due, []) if s1 - s0 == WIDE else ([], due)
             gather(a, s0, s1, gated, early)
-            woven_to = s1 - LAST_SLOTS if (a, s1) == (PASSES - 1, S) else s1
-            pieces = [
-                weave(nc.scalar.copy, a, lo, min(lo + QUANT, woven_to), gated[:, :, lo - s0 : min(lo + QUANT, woven_to) - s0])
-                for lo in range(s0, woven_to, QUANT)
-            ]
+            if (a, s1) == (PASSES - 1, S):
+                break
+            pieces = []
+            for lo in range(s0, s1, QUANT):
+                hi = min(lo + QUANT, s1)
+                if hi - lo > C:
+                    woven = three.tile([P, hi - lo, PACK], BF16, tag="woven", align_bytes=64)
+                else:
+                    woven = keep.tile([P, hi - lo, PACK], BF16, align_bytes=64, name=f"woven{lo}")
+                weave(nc.scalar.copy, woven[:], gated[:, :, lo - s0 : hi - s0])
+                pieces.append((a, lo, hi, woven[:]))
             if s1 - s0 > C:
                 for piece in due:
                     quantise(*piece)
                 due = []
+            else:
+                quantise(*held)
+            if (a, s1) == (0, S):
+                held = pieces.pop()
             due = due + pieces
+        last_woven = keep.tile([P, C, PACK], BF16, align_bytes=64)
+        weave(nc.scalar.copy, last_woven[:, :SCALAR_SHARE], gated[:, :, :SCALAR_SHARE])
         quantise(*due.pop(0))
-        due.append(weave(nc.vector.tensor_copy, PASSES - 1, S - LAST_SLOTS, S, gated[:, :, C - LAST_SLOTS :]))
+        weave(nc.vector.tensor_copy, last_woven[:, SCALAR_SHARE:], gated[:, :, SCALAR_SHARE:])
+        for lo in range(0, C, C // 2):
+            due.append((PASSES - 1, S - C + lo, S - C + lo + C // 2, last_woven[:, lo : lo + C // 2]))
         for piece in due:
             quantise(*piece)
 

@@ -50,9 +50,6 @@ def tile_moe_pre_lin_silu_kernel(
         planes = [
             keep.tile([P, WINDOW], F32, align_bytes=64, tag=f"plane{i}", name=f"plane{i}") for i in range(PASSES * PACK)
         ]
-        nc.vector.memset(planes[0][:, T:].bitcast(I32), 0)
-        for plane in planes[1:]:
-            nc.scalar.copy(plane[:, T:], planes[0][:, T:])
         w_scale = keep.tile([P, E * PASSES, N], U8, align_bytes=64)
         nc.vector.memset(w_scale[:].bitcast(I32), 0)
 

@@ -65,9 +65,10 @@ def tile_moe_pre_lin_silu_kernel(
             nc.sync.dma_start(gates[g][:, start : start + hi - lo], gate[:P, lo:hi])
 
         slot_tokens = lists.tile([P, S // LIST], U16)
-        load_plane(0)
         nc.sync.dma_start(slot_tokens[:], offs)
-        for lo, hi in zip(FIRST_CUTS, FIRST_CUTS[1:]):
+        load_gate(FIRST_CUTS[0], FIRST_CUTS[1])
+        load_plane(0)
+        for lo, hi in zip(FIRST_CUTS[1:], FIRST_CUTS[2:]):
             load_gate(lo, hi)
         for i in range(1, PASSES * PACK):
             load_plane(i)

@@ -28,7 +28,7 @@ BYTES = K * T * 4 + E * K * N + E * K * N // 32 + N * E * 4 + S * 4 + P * (S + T
 WIDE = 2048
 WINDOW = WIDE + LIST
 QUANT = 1024
-UNITS = [(0, 0, 2048), (1, 0, 2048), (0, 2048, 4096), (1, 2048, 3072), (1, 3072, 3584), (1, 3584, 3840), (1, 3840, 4096)]
+UNITS = [(0, 0, 2048), (1, 0, 2048), (0, 2048, 4096), (1, 2048, 3072), (1, 3072, 3584)]
 FIRST_CUTS = [0, 128, 384, 960, 2048]
 TOKEN_SPLIT = 512
 LAST_SUMS = [(0, 512), (512, 896), (896, 1024)]
@@ -44,7 +44,6 @@ def tile_moe_pre_lin_silu_kernel(
         lists = ctx.enter_context(tc.tile_pool(name="lists", bufs=1))
         keep = ctx.enter_context(tc.tile_pool(name="keep", bufs=1))
         two = ctx.enter_context(tc.tile_pool(name="two", bufs=2))
-        three = ctx.enter_context(tc.tile_pool(name="three", bufs=3))
         psum = ctx.enter_context(tc.psum_pool(name="psum", bufs=8))
 
         planes = [
@@ -93,20 +92,14 @@ def tile_moe_pre_lin_silu_kernel(
         y = keep.tile([N, S], F32)
         first_pass = {}
 
-        def gather(a, s0, s1, gated, early):
-            for r in range(PACK):
-                if r == PACK // 2:
-                    for piece in early:
-                        quantise(*piece)
-                cuts = FIRST_CUTS if (s0, a, r) == (0, 0, 0) else [s0, s1]
-                for lo, hi in zip(cuts, cuts[1:]):
-                    g, start = divmod(lo, WIDE)
-                    nc.vector.tensor_tensor(
-                        gated[:, r, lo - s0 : hi - s0],
-                        planes[a * PACK + r][:].indirect(slot_tokens[:, lo // LIST : hi // LIST]),
-                        gates[g][:, start : start + hi - lo],
-                        MULT,
-                    )
+        def gather(a, r, lo, hi, gated):
+            g, start = divmod(lo, WIDE)
+            nc.vector.tensor_tensor(
+                gated,
+                planes[a * PACK + r][:].indirect(slot_tokens[:, lo // LIST : hi // LIST]),
+                gates[g][:, start : start + hi - lo],
+                MULT,
+            )
 
         def weave(copy, woven, gated):
             copy(woven.rearrange("p (c i) r -> p c r i", i=4), gated.rearrange("p r (c i) -> p c r i", i=4))
@@ -141,7 +134,7 @@ def tile_moe_pre_lin_silu_kernel(
                 elif hi < S:
                     codes = keep.tile([P, width], U32, align_bytes=64, tag="plane0", name=f"codes{lo}")
                 else:
-                    codes = three.tile([P, width], U32, align_bytes=64, tag="woven")
+                    codes = keep.tile([P, width], U32, align_bytes=64, tag="woven_1024")
                 scales = keep.tile([P, width], U8, align_bytes=64, name=f"scales{lo}")
                 first_pass[lo // QUANT] = (codes, scales)
             elif width < QUANT:
@@ -159,28 +152,44 @@ def tile_moe_pre_lin_silu_kernel(
         due = []
         for a, s0, s1 in UNITS:
             gated = two.tile([P, PACK, s1 - s0], F32, tag="gated")
-            early, due = (due, []) if s1 - s0 == WIDE else ([], due)
-            gather(a, s0, s1, gated, early)
-            if (a, s1) == (PASSES - 1, S):
-                break
+            for r in range(PACK):
+                if r == PACK // 2 and s1 - s0 == WIDE:
+                    for piece in due:
+                        quantise(*piece)
+                    due = []
+                cuts = FIRST_CUTS if (s0, a, r) == (0, 0, 0) else [s0, s1]
+                if (a, s1, r) == (0, S, PACK - 1):
+                    cuts = [s0, s0 + QUANT]
+                for lo, hi in zip(cuts, cuts[1:]):
+                    gather(a, r, lo, hi, gated[:, r, lo - s0 : hi - s0])
             pieces = []
             for lo in range(s0, s1, QUANT):
                 hi = min(lo + QUANT, s1)
-                if hi - lo > C:
-                    woven = three.tile([P, hi - lo, PACK], BF16, tag="woven", align_bytes=64)
+                if (a, hi) == (0, S):
+                    gather(a, PACK - 1, lo, hi, gated[:, PACK - 1, lo - s0 :])
+                if (a, lo) == (1, WIDE):
+                    woven = keep.tile([P, hi - lo, PACK], BF16, tag="woven_1024", align_bytes=64)
                 else:
-                    woven = keep.tile([P, hi - lo, PACK], BF16, align_bytes=64, name=f"woven{lo}")
+                    woven = two.tile([P, hi - lo, PACK], BF16, tag="woven", align_bytes=64)
                 weave(nc.scalar.copy, woven[:], gated[:, :, lo - s0 : hi - s0])
                 pieces.append((a, lo, hi, woven[:]))
-            if s1 - s0 > C:
-                for piece in due:
-                    quantise(*piece)
-                due = []
-            else:
-                quantise(*held)
+            for piece in due:
+                quantise(*piece)
             if (a, s1) == (0, S):
                 held = pieces.pop()
-            due = due + pieces
+            due = pieces
+
+        s0 = S - 2 * C
+        both = two.tile([P, PACK, 2 * C], F32, tag="gated")
+        for r in range(PACK - 1):
+            gather(1, r, s0, S, both[:, r, :])
+        gather(1, PACK - 1, s0, S - C, both[:, PACK - 1, :C])
+        woven = keep.tile([P, C, PACK], BF16, align_bytes=64)
+        weave(nc.scalar.copy, woven[:], both[:, :, :C])
+        due.append((1, s0, S - C, woven[:]))
+        quantise(*held)
+        gather(1, PACK - 1, S - C, S, both[:, PACK - 1, C:])
+        gated = both[:, :, C:]
         last_woven = keep.tile([P, C, PACK], BF16, align_bytes=64)
         weave(nc.scalar.copy, last_woven[:, :SCALAR_SHARE], gated[:, :, :SCALAR_SHARE])
         quantise(*due.pop(0))

@@ -27,13 +27,15 @@ BYTES = K * T * 4 + E * K * N + E * K * N // 32 + N * E * 4 + S * 4 + P * (S + T
 
 WIDE = 2048
 WINDOW = WIDE + LIST
-QUANT = 1024
-UNITS = [(0, 0, 2048), (1, 0, 2048), (0, 2048, 4096), (1, 2048, 3072), (1, 3072, 3584)]
-FIRST_CUTS = [0, 128, 384, 960, 2048]
+FIRST_CUTS = [0, 128, 384, 960, WIDE]
+PIECES = [(lo, lo + 2 * C, C) for lo in range(0, S - 2 * C, 2 * C)] + [
+    (S - 2 * C, S - C, C),
+    (S - C, S - C // 2, C // 2),
+    (S - C // 2, S, C // 2),
+]
 TOKEN_SPLIT = 512
 LAST_SUMS = [(0, 512), (512, 896), (896, 1024)]
 W_GROUP = 4
-SCALAR_SHARE = 192
 
 
 def tile_moe_pre_lin_silu_kernel(
@@ -89,117 +91,68 @@ def tile_moe_pre_lin_silu_kernel(
             nc.sync.dma_start(slots[:], pos)
             token_slots.append(slots)
 
-        y = keep.tile([N, S], F32)
-        first_pass = {}
+        woven = {
+            lo: keep.tile([P, (hi - lo) // run, PASSES, run, PACK], BF16, align_bytes=64, name=f"woven{lo}")
+            for lo, hi, run in PIECES
+        }
 
-        def gather(a, r, lo, hi, gated):
-            g, start = divmod(lo, WIDE)
-            nc.vector.tensor_tensor(
-                gated,
-                planes[a * PACK + r][:].indirect(slot_tokens[:, lo // LIST : hi // LIST]),
-                gates[g][:, start : start + hi - lo],
-                MULT,
+        def gather_and_weave(a, s0, s1, gated, first_cuts, last_cuts):
+            g, start = divmod(s0, WIDE)
+            for r in range(PACK):
+                cuts = first_cuts if r == 0 else last_cuts if r == PACK - 1 else [s0, s1]
+                for lo, hi in zip(cuts, cuts[1:]):
+                    nc.vector.tensor_tensor(
+                        gated[:, r, lo - s0 : hi - s0],
+                        planes[a * PACK + r][:].indirect(slot_tokens[:, lo // LIST : hi // LIST]),
+                        gates[g][:, start + lo - s0 : start + hi - s0],
+                        MULT,
+                    )
+            for lo, hi, run in PIECES:
+                if s0 <= lo < s1:
+                    nc.scalar.copy(
+                        woven[lo][:, :, a].rearrange("p e (c i) r -> p e c r i", i=4),
+                        gated[:, :, lo - s0 : hi - s0].rearrange("p r (e c i) -> p e c r i", c=run // 4, i=4),
+                    )
+
+        for a, s0 in ((0, 0), (1, 0), (0, WIDE)):
+            gated = two.tile([P, PACK, WIDE], F32, tag="staging")
+            whole = [s0, s0 + WIDE]
+            gather_and_weave(a, s0, s0 + WIDE, gated, FIRST_CUTS if (a, s0) == (0, 0) else whole, whole)
+        halves = two.tile([P, 2, PACK, WIDE // 2], F32, tag="staging")
+        mid = S - WIDE // 2
+        gather_and_weave(1, WIDE, mid, halves[:, 0], [WIDE, mid], [WIDE, mid])
+        gather_and_weave(1, mid, S, halves[:, 1], [mid, S], [mid, S - 2 * C, S])
+
+        y = two.tile([N, S], F32, tag="staging")
+        codes = [
+            keep.tile([P, WIDE], U32, align_bytes=64, tag=f"plane{i}", name=f"codes{i}")
+            for i in range(PASSES * S // WIDE)
+        ]
+        scales = keep.tile([P, PASSES * S], U8, align_bytes=64, tag=f"plane{PASSES * PACK - 2}")
+        for lo, hi, run in PIECES:
+            tile, col = divmod(PASSES * lo, WIDE)
+            nc.vector.quantize_mx(
+                out=codes[tile][:, col : col + PASSES * (hi - lo)].bitcast(FP8X4),
+                scales=scales[:, PASSES * lo : PASSES * hi],
+                in_=woven[lo][:].rearrange("p e a c r -> p (e a c r)"),
             )
-
-        def weave(copy, woven, gated):
-            copy(woven.rearrange("p (c i) r -> p c r i", i=4), gated.rearrange("p r (c i) -> p c r i", i=4))
-
-        def multiply(lo, hi, codes, scales):
-            run = min(hi - lo, C)
             for s0 in range(lo, hi, run):
                 e = s0 // C
-                codes0, scales0 = first_pass[s0 // QUANT]
-                operands = [
-                    (codes0[:, s0 % QUANT : s0 % QUANT + run], scales0[:, s0 % QUANT : s0 % QUANT + run]),
-                    (codes[:, s0 - lo : s0 - lo + run], scales[:, s0 - lo : s0 - lo + run]),
-                ]
                 acc = psum.tile([N, run], F32, tag="acc")
-                for a, (x_codes, x_scales) in enumerate(operands):
+                for a in range(PASSES):
+                    word = PASSES * (s0 - lo) + a * run
                     nc.tensor.matmul_mx(
                         out=acc[:],
                         lhsT=w_codes[e // W_GROUP][:, (e % W_GROUP) * PASSES + a, :].bitcast(FP8X4),
                         lhsT_scale=w_scale[:, e * PASSES + a, :],
-                        rhs=x_codes.bitcast(FP8X4),
-                        rhs_scale=x_scales,
+                        rhs=codes[tile][:, col + word : col + word + run].bitcast(FP8X4),
+                        rhs_scale=scales[:, PASSES * lo + word : PASSES * lo + word + run],
                         start=(a == 0),
                         stop=(a == PASSES - 1),
                     )
                 nc.scalar.activation(y[:, s0 : s0 + run], acc[:], SILU, bias=bias[:, e : e + 1])
 
-        def quantise(a, lo, hi, woven):
-            width = hi - lo
-            if a == 0:
-                if lo < WIDE:
-                    codes = keep.tile([P, width], U32, align_bytes=64, name=f"codes{lo}")
-                elif hi < S:
-                    codes = keep.tile([P, width], U32, align_bytes=64, tag="plane0", name=f"codes{lo}")
-                else:
-                    codes = keep.tile([P, width], U32, align_bytes=64, tag="woven_1024")
-                scales = keep.tile([P, width], U8, align_bytes=64, name=f"scales{lo}")
-                first_pass[lo // QUANT] = (codes, scales)
-            elif width < QUANT:
-                codes = keep.tile([P, width], U32, align_bytes=64, name=f"last_codes{lo}")
-                scales = keep.tile([P, width], U8, align_bytes=64, name=f"last_scales{lo}")
-            else:
-                codes = two.tile([P, width], U32, align_bytes=64, tag="codes")
-                scales = two.tile([P, width], U8, align_bytes=64, tag="scales")
-            nc.vector.quantize_mx(
-                out=codes[:].bitcast(FP8X4), scales=scales[:], in_=woven.rearrange("p c r -> p (c r)")
-            )
-            if a == PASSES - 1:
-                multiply(lo, hi, codes, scales)
-
-        due = []
-        for a, s0, s1 in UNITS:
-            gated = two.tile([P, PACK, s1 - s0], F32, tag="gated")
-            for r in range(PACK):
-                if r == PACK // 2 and s1 - s0 == WIDE:
-                    for piece in due:
-                        quantise(*piece)
-                    due = []
-                cuts = FIRST_CUTS if (s0, a, r) == (0, 0, 0) else [s0, s1]
-                if (a, s1, r) == (0, S, PACK - 1):
-                    cuts = [s0, s0 + QUANT]
-                for lo, hi in zip(cuts, cuts[1:]):
-                    gather(a, r, lo, hi, gated[:, r, lo - s0 : hi - s0])
-            pieces = []
-            for lo in range(s0, s1, QUANT):
-                hi = min(lo + QUANT, s1)
-                if (a, hi) == (0, S):
-                    gather(a, PACK - 1, lo, hi, gated[:, PACK - 1, lo - s0 :])
-                if (a, lo) == (1, WIDE):
-                    woven = keep.tile([P, hi - lo, PACK], BF16, tag="woven_1024", align_bytes=64)
-                else:
-                    woven = two.tile([P, hi - lo, PACK], BF16, tag="woven", align_bytes=64)
-                weave(nc.scalar.copy, woven[:], gated[:, :, lo - s0 : hi - s0])
-                pieces.append((a, lo, hi, woven[:]))
-            for piece in due:
-                quantise(*piece)
-            if (a, s1) == (0, S):
-                held = pieces.pop()
-            due = pieces
-
-        s0 = S - 2 * C
-        both = two.tile([P, PACK, 2 * C], F32, tag="gated")
-        for r in range(PACK - 1):
-            gather(1, r, s0, S, both[:, r, :])
-        gather(1, PACK - 1, s0, S - C, both[:, PACK - 1, :C])
-        woven = keep.tile([P, C, PACK], BF16, align_bytes=64)
-        weave(nc.scalar.copy, woven[:], both[:, :, :C])
-        due.append((1, s0, S - C, woven[:]))
-        quantise(*held)
-        gather(1, PACK - 1, S - C, S, both[:, PACK - 1, C:])
-        gated = both[:, :, C:]
-        last_woven = keep.tile([P, C, PACK], BF16, align_bytes=64)
-        weave(nc.scalar.copy, last_woven[:, :SCALAR_SHARE], gated[:, :, :SCALAR_SHARE])
-        quantise(*due.pop(0))
-        weave(nc.vector.tensor_copy, last_woven[:, SCALAR_SHARE:], gated[:, :, SCALAR_SHARE:])
-        for lo in range(0, C, C // 2):
-            due.append((PASSES - 1, S - C + lo, S - C + lo + C // 2, last_woven[:, lo : lo + C // 2]))
-        for piece in due:
-            quantise(*piece)
-
-        sums = two.tile([N, TOP, T], F32, tag="gated")
+        sums = two.tile([N, TOP, T], F32, tag="staging")
         for j, slots in enumerate(token_slots):
             parts = LAST_SUMS if j == TOP - 1 else [(0, TOKEN_SPLIT), (TOKEN_SPLIT, T)]
             for t0, t1 in parts:

@@ -25,17 +25,18 @@ SILU = mybir.ActivationFunctionType.Silu
 FLOPS = 2 * K * S * N
 BYTES = K * T * 4 + E * K * N + E * K * N // 32 + N * E * 4 + S * 4 + P * (S + TOP * T) // LIST * 2 + N * T * 4
 
-WIDE = 2048
-WINDOW = WIDE + LIST
-FIRST_CUTS = [0, 128, 384, 960, WIDE]
-PIECES = [(lo, lo + 2 * C, C) for lo in range(0, S - 2 * C, 2 * C)] + [
-    (S - 2 * C, S - C, C),
-    (S - C, S - C // 2, C // 2),
-    (S - C // 2, S, C // 2),
-]
+SPLIT = (2048, 2816)
+FIRST_CUTS = [0, 128, 384, 960, SPLIT[0]]
+LAST_CUT = S - 3 * C
+CODES = 2048
+PIECES = (
+    [(lo, lo + 2 * C, C) for lo in range(0, S - 4 * C, 2 * C)]
+    + [(lo, lo + C, C) for lo in range(S - 4 * C, S - C, C)]
+    + [(lo, lo + C // 2, C // 2) for lo in range(S - C, S, C // 2)]
+)
 TOKEN_SPLIT = 512
 LAST_SUMS = [(0, 512), (512, 896), (896, 1024)]
-W_GROUP = 4
+W_GROUP = 8
 
 
 def tile_moe_pre_lin_silu_kernel(
@@ -45,11 +46,11 @@ def tile_moe_pre_lin_silu_kernel(
     with ExitStack() as ctx:
         lists = ctx.enter_context(tc.tile_pool(name="lists", bufs=1))
         keep = ctx.enter_context(tc.tile_pool(name="keep", bufs=1))
-        two = ctx.enter_context(tc.tile_pool(name="two", bufs=2))
         psum = ctx.enter_context(tc.psum_pool(name="psum", bufs=8))
 
         planes = [
-            keep.tile([P, WINDOW], F32, align_bytes=64, tag=f"plane{i}", name=f"plane{i}") for i in range(PASSES * PACK)
+            keep.tile([P, SPLIT[i // PACK] + LIST], F32, align_bytes=64, tag=f"plane{i}", name=f"plane{i}")
+            for i in range(PASSES * PACK)
         ]
         w_scale = keep.tile([P, E * PASSES, N], U8, align_bytes=64)
         nc.vector.memset(w_scale[:].bitcast(I32), 0)
@@ -59,11 +60,10 @@ def tile_moe_pre_lin_silu_kernel(
             rows = xT[a * K_PASS : (a + 1) * K_PASS, :].rearrange("(p r) t -> p r t", r=PACK)
             nc.sync.dma_start(planes[i][:, :T], rows[:, r, :])
 
-        gates = [keep.tile([P, WIDE], F32, name=f"gate{g}") for g in range(S // WIDE)]
+        gates = keep.tile([P, S], F32)
 
         def load_gate(lo, hi):
-            g, start = divmod(lo, WIDE)
-            nc.sync.dma_start(gates[g][:, start : start + hi - lo], gate[:P, lo:hi])
+            nc.sync.dma_start(gates[:, lo:hi], gate[:P, lo:hi])
 
         slot_tokens = lists.tile([P, S // LIST], U16)
         nc.sync.dma_start(slot_tokens[:], offs)
@@ -72,19 +72,14 @@ def tile_moe_pre_lin_silu_kernel(
         for lo, hi in zip(FIRST_CUTS[1:], FIRST_CUTS[2:]):
             load_gate(lo, hi)
         for i in range(1, PASSES * PACK):
+            if i == PACK:
+                load_gate(SPLIT[0], S)
             load_plane(i)
-        load_gate(WIDE, S)
         scale_rows = w_scales.rearrange("e a (q r) n -> r q (e a) n", r=4)
         for r in range(4):
             nc.sync.dma_start(w_scale[r:P:32, :, :].bitcast(I32), scale_rows[r].bitcast(I32))
         bias = keep.tile([N, E], F32)
         nc.sync.dma_start(bias[:], b)
-        w_codes = []
-        for e0 in range(0, E, W_GROUP):
-            group = keep.tile([P, W_GROUP * PASSES, N * PACK], U8, align_bytes=64, name=f"w{e0}")
-            words = w_words[e0 : e0 + W_GROUP].rearrange("e a p n r -> p (e a) (n r)")
-            nc.sync.dma_start(group[:].bitcast(I32), words.bitcast(I32))
-            w_codes.append(group)
         token_slots = []
         for j, pos in enumerate((pos1, pos2, pos3, pos4)):
             slots = lists.tile([P, T // LIST], U16, name=f"pos{j}")
@@ -96,46 +91,62 @@ def tile_moe_pre_lin_silu_kernel(
             for lo, hi, run in PIECES
         }
 
-        def gather_and_weave(a, s0, s1, gated, first_cuts, last_cuts):
-            g, start = divmod(s0, WIDE)
+        def gather_and_weave(a, s0, s1):
+            gated = keep.tile([P, PACK, s1 - s0], F32, tag=f"staging{a}", name="gated")
             for r in range(PACK):
-                cuts = first_cuts if r == 0 else last_cuts if r == PACK - 1 else [s0, s1]
+                cuts = [s0, s1]
+                if (a, s0, r) == (0, 0, 0):
+                    cuts = FIRST_CUTS
+                if (a, s1, r) == (PASSES - 1, S, PACK - 1):
+                    cuts = [s0, LAST_CUT, s1]
                 for lo, hi in zip(cuts, cuts[1:]):
                     nc.vector.tensor_tensor(
                         gated[:, r, lo - s0 : hi - s0],
                         planes[a * PACK + r][:].indirect(slot_tokens[:, lo // LIST : hi // LIST]),
-                        gates[g][:, start + lo - s0 : start + hi - s0],
+                        gates[:, lo:hi],
                         MULT,
                     )
-            for lo, hi, run in PIECES:
-                if s0 <= lo < s1:
+            for first, last, run in PIECES:
+                lo, hi = max(first, s0), min(last, s1)
+                if lo < hi:
                     nc.scalar.copy(
-                        woven[lo][:, :, a].rearrange("p e (c i) r -> p e c r i", i=4),
+                        woven[first][:, (lo - first) // run : (hi - first) // run, a].rearrange(
+                            "p e (c i) r -> p e c r i", i=4
+                        ),
                         gated[:, :, lo - s0 : hi - s0].rearrange("p r (e c i) -> p e c r i", c=run // 4, i=4),
                     )
 
-        for a, s0 in ((0, 0), (1, 0), (0, WIDE)):
-            gated = two.tile([P, PACK, WIDE], F32, tag="staging")
-            whole = [s0, s0 + WIDE]
-            gather_and_weave(a, s0, s0 + WIDE, gated, FIRST_CUTS if (a, s0) == (0, 0) else whole, whole)
-        halves = two.tile([P, 2, PACK, WIDE // 2], F32, tag="staging")
-        mid = S - WIDE // 2
-        gather_and_weave(1, WIDE, mid, halves[:, 0], [WIDE, mid], [WIDE, mid])
-        gather_and_weave(1, mid, S, halves[:, 1], [mid, S], [mid, S - 2 * C, S])
+        for a in range(PASSES):
+            gather_and_weave(a, 0, SPLIT[a])
+        for a in range(PASSES):
+            gather_and_weave(a, SPLIT[a], S)
 
-        y = two.tile([N, S], F32, tag="staging")
+        w_codes = []
+        for e0 in range(0, E, W_GROUP):
+            group = keep.tile(
+                [P, W_GROUP * PASSES, N * PACK], U8, align_bytes=64, tag=f"plane{e0 // W_GROUP}", name=f"w{e0}"
+            )
+            words = w_words[e0 : e0 + W_GROUP].rearrange("e a p n r -> p (e a) (n r)")
+            nc.sync.dma_start(group[:].bitcast(I32), words.bitcast(I32))
+            w_codes.append(group)
+
+        y = keep.tile([N, S], F32, tag="staging0")
         codes = [
-            keep.tile([P, WIDE], U32, align_bytes=64, tag=f"plane{i}", name=f"codes{i}")
-            for i in range(PASSES * S // WIDE)
+            keep.tile([P, CODES], U32, align_bytes=64, tag=f"plane{E // W_GROUP + i}", name=f"codes{i}")
+            for i in range(PASSES * S // CODES)
         ]
         scales = keep.tile([P, PASSES * S], U8, align_bytes=64, tag=f"plane{PASSES * PACK - 2}")
         for lo, hi, run in PIECES:
-            tile, col = divmod(PASSES * lo, WIDE)
-            nc.vector.quantize_mx(
-                out=codes[tile][:, col : col + PASSES * (hi - lo)].bitcast(FP8X4),
-                scales=scales[:, PASSES * lo : PASSES * hi],
-                in_=woven[lo][:].rearrange("p e a c r -> p (e a c r)"),
-            )
+            tile, col = divmod(PASSES * lo, CODES)
+            words = PASSES * (hi - lo)
+            step = run if hi == S else words
+            values = woven[lo][:].rearrange("p e a c r -> p (e a c r)")
+            for w0 in range(0, words, step):
+                nc.vector.quantize_mx(
+                    out=codes[tile][:, col + w0 : col + w0 + step].bitcast(FP8X4),
+                    scales=scales[:, PASSES * lo + w0 : PASSES * lo + w0 + step],
+                    in_=values[:, PACK * w0 : PACK * (w0 + step)],
+                )
             for s0 in range(lo, hi, run):
                 e = s0 // C
                 acc = psum.tile([N, run], F32, tag="acc")
@@ -152,7 +163,7 @@ def tile_moe_pre_lin_silu_kernel(
                     )
                 nc.scalar.activation(y[:, s0 : s0 + run], acc[:], SILU, bias=bias[:, e : e + 1])
 
-        sums = two.tile([N, TOP, T], F32, tag="staging")
+        sums = keep.tile([N, TOP, T], F32, tag="staging1")
         for j, slots in enumerate(token_slots):
             parts = LAST_SUMS if j == TOP - 1 else [(0, TOKEN_SPLIT), (TOKEN_SPLIT, T)]
             for t0, t1 in parts:

@@ -69,6 +69,8 @@ def tile_moe_pre_lin_silu_kernel(
         nc.sync.dma_start(slot_tokens[:], offs)
         load_gate(FIRST_CUTS[0], FIRST_CUTS[1])
         load_plane(0)
+        warm = keep.tile([P, 1], F32)
+        nc.scalar.activation(warm[:], gates[:, :1], SILU)
         for lo, hi in zip(FIRST_CUTS[1:], FIRST_CUTS[2:]):
             load_gate(lo, hi)
         for i in range(1, PASSES * PACK):

@@ -35,7 +35,7 @@ PIECES = (
     + [(lo, lo + C // 2, C // 2) for lo in range(S - C, S, C // 2)]
 )
 TOKEN_SPLIT = 512
-LAST_SUMS = [(0, 512), (512, 896), (896, 1024)]
+LAST_SUMS = [(0, 512), (512, 832), (832, 1024)]
 W_GROUP = 8
 
 

@@ -1,6 +1,7 @@
 from contextlib import ExitStack
 
 import concourse.mybir as mybir
+from concourse.masks import make_identity
 
 K, T, E, C, N = 1024, 1024, 16, 256, 128
 TOP = 4
@@ -21,12 +22,13 @@ FP8X4 = mybir.dt.float8_e4m3fn_x4
 MULT = mybir.AluOpType.mult
 ADD = mybir.AluOpType.add
 SILU = mybir.ActivationFunctionType.Silu
+COPY = mybir.ActivationFunctionType.Copy
 
 FLOPS = 2 * K * S * N
 BYTES = K * T * 4 + E * K * N + E * K * N // 32 + N * E * 4 + S * 4 + P * (S + TOP * T) // LIST * 2 + N * T * 4
 
 SPLIT = (2048, 2816)
-FIRST_CUTS = [0, 128, 384, 960, SPLIT[0]]
+BANK = 512
 LAST_CUT = S - 3 * C
 CODES = 2048
 PIECES = (
@@ -67,13 +69,16 @@ def tile_moe_pre_lin_silu_kernel(
 
         slot_tokens = lists.tile([P, S // LIST], U16)
         nc.sync.dma_start(slot_tokens[:], offs)
-        load_gate(FIRST_CUTS[0], FIRST_CUTS[1])
         load_plane(0)
+        identity = keep.tile([P, P], F32)
+        make_identity(nc, identity[:])
         warm = keep.tile([P, 1], F32)
-        nc.scalar.activation(warm[:], gates[:, :1], SILU)
-        for lo, hi in zip(FIRST_CUTS[1:], FIRST_CUTS[2:]):
-            load_gate(lo, hi)
+        nc.scalar.activation(warm[:], identity[:, :1], SILU)
+        load_gate(0, SPLIT[0])
+        gate_rows = keep.tile([P, P], F32)
         for i in range(1, PASSES * PACK):
+            if i == 2:
+                nc.sync.dma_start(gate_rows[:], gate[: P * P // S].rearrange("k (c q) -> (k c) q", q=P))
             if i == PACK:
                 load_gate(SPLIT[0], S)
             load_plane(i)
@@ -93,12 +98,35 @@ def tile_moe_pre_lin_silu_kernel(
             for lo, hi, run in PIECES
         }
 
+        turned = psum.tile([P, P], F32, tag="acc")
+        nc.tensor.transpose(turned[:], gate_rows[:], identity[:])
+        gate_cols = keep.tile([P, SPLIT[0] // P], F32)
+        nc.scalar.copy(gate_cols[:], turned[:, : SPLIT[0] // P])
+
+        def gather_before_the_gate(gated):
+            both = keep.tile([P, 2, SPLIT[0]], F32, tag="staging1")
+            raw, by_slot = both[:, 0], both[:, 1]
+            nc.vector.tensor_copy(raw, planes[0][:].indirect(slot_tokens[:, : SPLIT[0] // LIST]))
+            for lo in range(0, SPLIT[0], BANK):
+                there = psum.tile([P, BANK], F32, tag="acc")
+                back = psum.tile([P, BANK], F32, tag="acc")
+                blocks = range(lo, lo + BANK, P)
+                for c in blocks:
+                    nc.tensor.transpose(there[:, c - lo : c - lo + P], raw[:, c : c + P], identity[:])
+                for c in blocks:
+                    scale = gate_cols[:, c // P : c // P + 1]
+                    nc.scalar.activation(by_slot[:, c : c + P], there[:, c - lo : c - lo + P], COPY, scale=scale)
+                for c in blocks:
+                    nc.tensor.transpose(back[:, c - lo : c - lo + P], by_slot[:, c : c + P], identity[:])
+                nc.scalar.copy(gated[:, lo : lo + BANK], back[:])
+
         def gather_and_weave(a, s0, s1):
             gated = keep.tile([P, PACK, s1 - s0], F32, tag=f"staging{a}", name="gated")
             for r in range(PACK):
-                cuts = [s0, s1]
                 if (a, s0, r) == (0, 0, 0):
-                    cuts = FIRST_CUTS
+                    gather_before_the_gate(gated[:, 0])
+                    continue
+                cuts = [s0, s1]
                 if (a, s1, r) == (PASSES - 1, S, PACK - 1):
                     cuts = [s0, LAST_CUT, s1]
                 for lo, hi in zip(cuts, cuts[1:]):

@@ -1,7 +1,6 @@
 from contextlib import ExitStack
 
 import concourse.mybir as mybir
-from concourse.masks import make_identity
 
 K, T, E, C, N = 1024, 1024, 16, 256, 128
 TOP = 4
@@ -21,6 +20,7 @@ U8 = mybir.dt.uint8
 FP8X4 = mybir.dt.float8_e4m3fn_x4
 MULT = mybir.AluOpType.mult
 ADD = mybir.AluOpType.add
+EQUAL = mybir.AluOpType.is_equal
 SILU = mybir.ActivationFunctionType.Silu
 COPY = mybir.ActivationFunctionType.Copy
 
@@ -29,6 +29,7 @@ BYTES = K * T * 4 + E * K * N + E * K * N // 32 + N * E * 4 + S * 4 + P * (S + T
 
 SPLIT = (2048, 2816)
 BANK = 512
+QUAD = 32
 LAST_CUT = S - 3 * C
 CODES = 2048
 PIECES = (
@@ -70,10 +71,19 @@ def tile_moe_pre_lin_silu_kernel(
         slot_tokens = lists.tile([P, S // LIST], U16)
         nc.sync.dma_start(slot_tokens[:], offs)
         load_plane(0)
+        ones = keep.tile([P, QUAD], F32)
+        nc.vector.memset(ones[:], 1.0)
         identity = keep.tile([P, P], F32)
-        make_identity(nc, identity[:])
+        nc.vector.memset(identity[:], 0.0)
+        column = keep.tile([P, QUAD], F32, align_bytes=64)
+        nc.vector.tensor_tensor_scan(column[:], ones[:], ones[:], 0.0, MULT, ADD)
+        row = keep.tile([P, QUAD], F32, align_bytes=64)
+        nc.vector.transpose(row[:], column[:])
+        for q in range(0, P, QUAD):
+            part = slice(q, q + QUAD)
+            nc.vector.tensor_tensor(identity[part, part], column[part, :], row[part, :], EQUAL)
         warm = keep.tile([P, 1], F32)
-        nc.scalar.activation(warm[:], identity[:, :1], SILU)
+        nc.scalar.activation(warm[:], ones[:, :1], SILU)
         load_gate(0, SPLIT[0])
         gate_rows = keep.tile([P, P], F32)
         for i in range(1, PASSES * PACK):

@@ -55,7 +55,7 @@ def tile_moe_pre_lin_silu_kernel(
             keep.tile([P, SPLIT[i // PACK] + LIST], F32, align_bytes=64, tag=f"plane{i}", name=f"plane{i}")
             for i in range(PASSES * PACK)
         ]
-        w_scale = keep.tile([P, E * PASSES, N], U8, align_bytes=64)
+        w_scale = keep.tile([P, E * PASSES // 4, N], U8, align_bytes=64)
         nc.vector.memset(w_scale[:].bitcast(I32), 0)
 
         def load_plane(i):
@@ -92,9 +92,11 @@ def tile_moe_pre_lin_silu_kernel(
             if i == PACK:
                 load_gate(SPLIT[0], S)
             load_plane(i)
-        scale_rows = w_scales.rearrange("e a (q r) n -> r q (e a) n", r=4)
-        for r in range(4):
-            nc.sync.dma_start(w_scale[r:P:32, :, :].bitcast(I32), scale_rows[r].bitcast(I32))
+        scale_rows = w_scales.rearrange("(g h) a (q r) n -> h a r q g n", h=2, r=4)
+        for j in range(4):
+            for r in range(4):
+                rows = scale_rows[j // PASSES, j % PASSES, r]
+                nc.sync.dma_start(w_scale[4 * j + r : P : 32, :, :].bitcast(I32), rows.bitcast(I32))
         bias = keep.tile([N, E], F32)
         nc.sync.dma_start(bias[:], b)
         token_slots = []
@@ -195,7 +197,7 @@ def tile_moe_pre_lin_silu_kernel(
                     nc.tensor.matmul_mx(
                         out=acc[:],
                         lhsT=w_codes[e // W_GROUP][:, (e % W_GROUP) * PASSES + a, :].bitcast(FP8X4),
-                        lhsT_scale=w_scale[:, e * PASSES + a, :],
+                        lhsT_scale=w_scale[4 * ((e * PASSES + a) % 4) :, (e * PASSES + a) // 4, :],
                         rhs=codes[tile][:, col + word : col + word + run].bitcast(FP8X4),
                         rhs_scale=scales[:, PASSES * lo + word : PASSES * lo + word + run],
                         start=(a == 0),

@@ -169,7 +169,8 @@ def tile_moe_pre_lin_silu_kernel(
                 [P, W_GROUP * PASSES, N * PACK], U8, align_bytes=64, tag=f"plane{e0 // W_GROUP}", name=f"w{e0}"
             )
             words = w_words[e0 : e0 + W_GROUP].rearrange("e a p n r -> p (e a) (n r)")
-            nc.sync.dma_start(group[:].bitcast(I32), words.bitcast(I32))
+            for half in (slice(0, W_GROUP), slice(W_GROUP, 2 * W_GROUP)):
+                nc.sync.dma_start(group[:, half].bitcast(I32), words[:, half].bitcast(I32))
             w_codes.append(group)
 
         y = keep.tile([N, S], F32, tag="staging0")

@@ -20,26 +20,16 @@ U8 = mybir.dt.uint8
 FP8X4 = mybir.dt.float8_e4m3fn_x4
 MULT = mybir.AluOpType.mult
 ADD = mybir.AluOpType.add
-EQUAL = mybir.AluOpType.is_equal
 SILU = mybir.ActivationFunctionType.Silu
 COPY = mybir.ActivationFunctionType.Copy
 
 FLOPS = 2 * K * S * N
 BYTES = K * T * 4 + E * K * N + E * K * N // 32 + N * E * 4 + S * 4 + P * (S + TOP * T) // LIST * 2 + N * T * 4
 
-SPLIT = (2048, 2816)
+RUN = 1024
 BANK = 512
-QUAD = 32
-LAST_CUT = S - 3 * C
-CODES = 2048
-PIECES = (
-    [(lo, lo + 2 * C, C) for lo in range(0, S - 4 * C, 2 * C)]
-    + [(lo, lo + C, C) for lo in range(S - 4 * C, S - C, C)]
-    + [(lo, lo + C // 2, C // 2) for lo in range(S - C, S, C // 2)]
-)
-TOKEN_SPLIT = 512
-LAST_SUMS = [(0, 512), (512, 832), (832, 1024)]
-W_GROUP = 8
+PAIR = 2
+HALF = T // 2
 
 
 def tile_moe_pre_lin_silu_kernel(
@@ -49,54 +39,46 @@ def tile_moe_pre_lin_silu_kernel(
     with ExitStack() as ctx:
         lists = ctx.enter_context(tc.tile_pool(name="lists", bufs=1))
         keep = ctx.enter_context(tc.tile_pool(name="keep", bufs=1))
+        ring = ctx.enter_context(tc.tile_pool(name="ring", bufs=3))
         psum = ctx.enter_context(tc.psum_pool(name="psum", bufs=8))
 
-        planes = [
-            keep.tile([P, SPLIT[i // PACK] + LIST], F32, align_bytes=64, tag=f"plane{i}", name=f"plane{i}")
-            for i in range(PASSES * PACK)
-        ]
+        planes = [keep.tile([P, RUN + LIST], F32, tag=f"plane{i}", name=f"plane{i}") for i in range(PASSES * PACK)]
+        gates = [keep.tile([P, RUN], F32, name=f"gate{q}") for q in range(S // RUN)]
         w_scale = keep.tile([P, E * PASSES // 4, N], U8, align_bytes=64)
         nc.vector.memset(w_scale[:].bitcast(I32), 0)
+        warm_in = keep.tile([P, 1], F32)
+        nc.vector.memset(warm_in[:], 0.0)
+        warm_out = keep.tile([P, 1], F32)
+        nc.scalar.activation(warm_out[:], warm_in[:], SILU)
 
         def load_plane(i):
             a, r = divmod(i, PACK)
             rows = xT[a * K_PASS : (a + 1) * K_PASS, :].rearrange("(p r) t -> p r t", r=PACK)
             nc.sync.dma_start(planes[i][:, :T], rows[:, r, :])
 
-        gates = keep.tile([P, S], F32)
-
-        def load_gate(lo, hi):
-            nc.sync.dma_start(gates[:, lo:hi], gate[:P, lo:hi])
+        def load_gate(q):
+            nc.sync.dma_start(gates[q][:], gate[:P, q * RUN : (q + 1) * RUN])
 
         slot_tokens = lists.tile([P, S // LIST], U16)
         nc.sync.dma_start(slot_tokens[:], offs)
         load_plane(0)
-        ones = keep.tile([P, QUAD], F32)
-        nc.vector.memset(ones[:], 1.0)
-        identity = keep.tile([P, P], F32)
-        nc.vector.memset(identity[:], 0.0)
-        column = keep.tile([P, QUAD], F32, align_bytes=64)
-        nc.vector.tensor_tensor_scan(column[:], ones[:], ones[:], 0.0, MULT, ADD)
-        row = keep.tile([P, QUAD], F32, align_bytes=64)
-        nc.vector.transpose(row[:], column[:])
-        for q in range(0, P, QUAD):
-            part = slice(q, q + QUAD)
-            nc.vector.tensor_tensor(identity[part, part], column[part, :], row[part, :], EQUAL)
-        warm = keep.tile([P, 1], F32)
-        nc.scalar.activation(warm[:], ones[:, :1], SILU)
-        load_gate(0, SPLIT[0])
-        gate_rows = keep.tile([P, P], F32)
-        for i in range(1, PASSES * PACK):
-            if i == 2:
-                nc.sync.dma_start(gate_rows[:], gate[: P * P // S].rearrange("k (c q) -> (k c) q", q=P))
-            if i == PACK:
-                load_gate(SPLIT[0], S)
+        load_gate(0)
+        for i in range(1, PACK):
             load_plane(i)
+        load_gate(1)
+        for i in range(PACK, PASSES * PACK):
+            load_plane(i)
+        for q in range(2, S // RUN):
+            load_gate(q)
         scale_rows = w_scales.rearrange("(g h) a (q r) n -> h a r q g n", h=2, r=4)
         for j in range(4):
             for r in range(4):
                 rows = scale_rows[j // PASSES, j % PASSES, r]
                 nc.sync.dma_start(w_scale[4 * j + r : P : 32, :, :].bitcast(I32), rows.bitcast(I32))
+        w_codes = keep.tile([P, E * PASSES, N * PACK], U8, align_bytes=64)
+        words = w_words.rearrange("e a p n r -> p (e a) (n r)")
+        for lo in range(0, E * PASSES, 8):
+            nc.sync.dma_start(w_codes[:, lo : lo + 8].bitcast(I32), words[:, lo : lo + 8].bitcast(I32))
         bias = keep.tile([N, E], F32)
         nc.sync.dma_start(bias[:], b)
         token_slots = []
@@ -105,115 +87,103 @@ def tile_moe_pre_lin_silu_kernel(
             nc.sync.dma_start(slots[:], pos)
             token_slots.append(slots)
 
-        woven = {
-            lo: keep.tile([P, (hi - lo) // run, PASSES, run, PACK], BF16, align_bytes=64, name=f"woven{lo}")
-            for lo, hi, run in PIECES
-        }
+        codes = [keep.tile([P, S], U32, align_bytes=64, name=f"codes{a}") for a in range(PASSES)]
+        scales = [keep.tile([P, S], U8, align_bytes=64, name=f"scales{a}") for a in range(PASSES)]
 
-        turned = psum.tile([P, P], F32, tag="acc")
-        nc.tensor.transpose(turned[:], gate_rows[:], identity[:])
-        gate_cols = keep.tile([P, SPLIT[0] // P], F32)
-        nc.scalar.copy(gate_cols[:], turned[:, : SPLIT[0] // P])
+        def picked(a, r, lo, hi):
+            return planes[a * PACK + r][:].indirect(slot_tokens[:, lo // LIST : hi // LIST])
 
-        def gather_before_the_gate(gated):
-            both = keep.tile([P, 2, SPLIT[0]], F32, tag="staging1")
-            raw, by_slot = both[:, 0], both[:, 1]
-            nc.vector.tensor_copy(raw, planes[0][:].indirect(slot_tokens[:, : SPLIT[0] // LIST]))
-            for lo in range(0, SPLIT[0], BANK):
-                there = psum.tile([P, BANK], F32, tag="acc")
-                back = psum.tile([P, BANK], F32, tag="acc")
-                blocks = range(lo, lo + BANK, P)
-                for c in blocks:
-                    nc.tensor.transpose(there[:, c - lo : c - lo + P], raw[:, c : c + P], identity[:])
-                for c in blocks:
-                    scale = gate_cols[:, c // P : c // P + 1]
-                    nc.scalar.activation(by_slot[:, c : c + P], there[:, c - lo : c - lo + P], COPY, scale=scale)
-                for c in blocks:
-                    nc.tensor.transpose(back[:, c - lo : c - lo + P], by_slot[:, c : c + P], identity[:])
-                nc.scalar.copy(gated[:, lo : lo + BANK], back[:])
+        def by_pairs(tile, width):
+            return tile[:, :, :width].rearrange("p r (c i) -> p c r i", i=PAIR)
 
-        def gather_and_weave(a, s0, s1):
-            gated = keep.tile([P, PACK, s1 - s0], F32, tag=f"staging{a}", name="gated")
-            for r in range(PACK):
-                if (a, s0, r) == (0, 0, 0):
-                    gather_before_the_gate(gated[:, 0])
-                    continue
-                cuts = [s0, s1]
-                if (a, s1, r) == (PASSES - 1, S, PACK - 1):
-                    cuts = [s0, LAST_CUT, s1]
-                for lo, hi in zip(cuts, cuts[1:]):
-                    nc.vector.tensor_tensor(
-                        gated[:, r, lo - s0 : hi - s0],
-                        planes[a * PACK + r][:].indirect(slot_tokens[:, lo // LIST : hi // LIST]),
-                        gates[:, lo:hi],
-                        MULT,
-                    )
-            for first, last, run in PIECES:
-                lo, hi = max(first, s0), min(last, s1)
-                if lo < hi:
-                    nc.scalar.copy(
-                        woven[first][:, (lo - first) // run : (hi - first) // run, a].rearrange(
-                            "p e (c i) r -> p e c r i", i=4
-                        ),
-                        gated[:, :, lo - s0 : hi - s0].rearrange("p r (e c i) -> p e c r i", c=run // 4, i=4),
-                    )
-
-        for a in range(PASSES):
-            gather_and_weave(a, 0, SPLIT[a])
-        for a in range(PASSES):
-            gather_and_weave(a, SPLIT[a], S)
-
-        w_codes = []
-        for e0 in range(0, E, W_GROUP):
-            group = keep.tile(
-                [P, W_GROUP * PASSES, N * PACK], U8, align_bytes=64, tag=f"plane{e0 // W_GROUP}", name=f"w{e0}"
+        def quantise(a, lo, hi, woven):
+            nc.vector.quantize_mx(
+                out=codes[a][:, lo:hi].bitcast(FP8X4),
+                scales=scales[a][:, lo:hi],
+                in_=woven[:, : hi - lo].rearrange("p c r -> p (c r)"),
             )
-            words = w_words[e0 : e0 + W_GROUP].rearrange("e a p n r -> p (e a) (n r)")
-            for half in (slice(0, W_GROUP), slice(W_GROUP, 2 * W_GROUP)):
-                nc.sync.dma_start(group[:, half].bitcast(I32), words[:, half].bitcast(I32))
-            w_codes.append(group)
 
-        y = keep.tile([N, S], F32, tag="staging0")
-        codes = [
-            keep.tile([P, CODES], U32, align_bytes=64, tag=f"plane{E // W_GROUP + i}", name=f"codes{i}")
-            for i in range(PASSES * S // CODES)
-        ]
-        scales = keep.tile([P, PASSES * S], U8, align_bytes=64, tag=f"plane{PASSES * PACK - 2}")
-        for lo, hi, run in PIECES:
-            tile, col = divmod(PASSES * lo, CODES)
-            words = PASSES * (hi - lo)
-            step = run if hi == S else words
-            values = woven[lo][:].rearrange("p e a c r -> p (e a c r)")
-            for w0 in range(0, words, step):
-                nc.vector.quantize_mx(
-                    out=codes[tile][:, col + w0 : col + w0 + step].bitcast(FP8X4),
-                    scales=scales[:, PASSES * lo + w0 : PASSES * lo + w0 + step],
-                    in_=values[:, PACK * w0 : PACK * (w0 + step)],
+        def vector_run(a, lo, hi):
+            q, width = lo // RUN, hi - lo
+            gated = keep.tile([P, PACK, RUN], F32, tag="gated")
+            for r in range(PACK):
+                nc.vector.tensor_tensor(
+                    gated[:, r, :width], picked(a, r, lo, hi), gates[q][:, lo - q * RUN : hi - q * RUN], MULT
                 )
-            for s0 in range(lo, hi, run):
-                e = s0 // C
-                acc = psum.tile([N, run], F32, tag="acc")
-                for a in range(PASSES):
-                    word = PASSES * (s0 - lo) + a * run
-                    nc.tensor.matmul_mx(
-                        out=acc[:],
-                        lhsT=w_codes[e // W_GROUP][:, (e % W_GROUP) * PASSES + a, :].bitcast(FP8X4),
-                        lhsT_scale=w_scale[4 * ((e * PASSES + a) % 4) :, (e * PASSES + a) // 4, :],
-                        rhs=codes[tile][:, col + word : col + word + run].bitcast(FP8X4),
-                        rhs_scale=scales[:, PASSES * lo + word : PASSES * lo + word + run],
-                        start=(a == 0),
-                        stop=(a == PASSES - 1),
-                    )
-                nc.scalar.activation(y[:, s0 : s0 + run], acc[:], SILU, bias=bias[:, e : e + 1])
+            woven = ring.tile([P, RUN, PACK], BF16, align_bytes=64, tag="woven")
+            nc.vector.tensor_copy(woven[:, :width].rearrange("p (c i) r -> p c r i", i=PAIR), by_pairs(gated, width))
+            quantise(a, lo, hi, woven)
 
-        sums = keep.tile([N, TOP, T], F32, tag="staging1")
-        for j, slots in enumerate(token_slots):
-            parts = LAST_SUMS if j == TOP - 1 else [(0, TOKEN_SPLIT), (TOKEN_SPLIT, T)]
-            for t0, t1 in parts:
-                picked = y[:].indirect(slots[:, t0 // LIST : t1 // LIST])
-                if j == 0:
-                    nc.vector.tensor_copy(sums[:, j, t0:t1], picked)
-                else:
-                    nc.vector.tensor_tensor(sums[:, j, t0:t1], picked, sums[:, j - 1, t0:t1], ADD)
-                if j == TOP - 1:
-                    nc.sync.dma_start(out[:, t0:t1], sums[:, j, t0:t1])
+        def scalar_run(a, lo, hi):
+            q, width = lo // RUN, hi - lo
+            raw = ring.tile([P, PACK, RUN], F32, tag="raw")
+            for r in range(PACK):
+                nc.scalar.activation(raw[:, r, :width], picked(a, r, lo, hi), COPY)
+            woven = ring.tile([P, RUN, PACK], BF16, align_bytes=64, tag="woven")
+            weights = gates[q][:, lo - q * RUN : hi - q * RUN].rearrange("p (c i) -> p c i", i=PAIR)
+            nc.vector.tensor_tensor(
+                woven[:, :width].rearrange("p (c i) r -> p c r i", i=PAIR),
+                by_pairs(raw, width),
+                weights.unsqueeze(2).to_broadcast([P, width // PAIR, PACK, PAIR]),
+                MULT,
+            )
+            quantise(a, lo, hi, woven)
+
+        banks = []
+
+        def multiply(lo, hi):
+            for s0 in range(lo, hi, BANK):
+                bank = psum.tile([N, BANK], F32, tag="bank")
+                banks.append(bank)
+                for e in range(s0 // C, (s0 + BANK) // C):
+                    for a in range(PASSES):
+                        g = e * PASSES + a
+                        nc.tensor.matmul_mx(
+                            out=bank[:, e * C - s0 : (e + 1) * C - s0],
+                            lhsT=w_codes[:, g, :].bitcast(FP8X4),
+                            lhsT_scale=w_scale[4 * (g % 4) :, g // 4, :],
+                            rhs=codes[a][:, e * C : (e + 1) * C].bitcast(FP8X4),
+                            rhs_scale=scales[a][:, e * C : (e + 1) * C],
+                            start=(a == 0),
+                            stop=(a == PASSES - 1),
+                        )
+
+        vector_run(0, 0, RUN)
+        scalar_run(0, RUN, 2 * RUN)
+        vector_run(1, 0, RUN)
+        multiply(0, RUN)
+        scalar_run(0, 2 * RUN, 3 * RUN)
+        scalar_run(0, 3 * RUN, S)
+        scalar_run(1, RUN, 2 * RUN)
+        multiply(RUN, 2 * RUN)
+        scalar_run(1, 2 * RUN, 3 * RUN)
+        multiply(2 * RUN, 3 * RUN)
+        scalar_run(1, 3 * RUN, S - BANK)
+        multiply(3 * RUN, S - BANK)
+        scalar_run(1, S - BANK, S)
+        multiply(S - BANK, S)
+
+        y = keep.tile([N, S], F32, tag=f"plane{PASSES * PACK - 1}")
+        for e in range(E):
+            col = e * C % BANK
+            nc.scalar.activation(
+                y[:, e * C : (e + 1) * C], banks[e * C // BANK][:, col : col + C], SILU, bias=bias[:, e : e + 1]
+            )
+
+        def result(j, h):
+            return y[:].indirect(token_slots[j][:, h * HALF // LIST : (h + 1) * HALF // LIST])
+
+        fetched = ring.tile([N, 2, 2, HALF], F32, tag="raw")
+        for h in range(2):
+            for j in range(2):
+                nc.scalar.activation(fetched[:, h, j], result(j, h), COPY)
+        sums = ring.tile([N, 2, TOP, HALF], F32, tag="raw")
+        nc.vector.tensor_copy(sums[:, 1, 0], result(2, 1))
+        nc.vector.tensor_tensor(sums[:, 0, 0], result(2, 0), fetched[:, 0, 0], ADD)
+        nc.vector.tensor_tensor(sums[:, 1, 1], result(3, 1), sums[:, 1, 0], ADD)
+        nc.vector.tensor_tensor(sums[:, 0, 1], result(3, 0), sums[:, 0, 0], ADD)
+        nc.vector.tensor_tensor(sums[:, 1, 2], sums[:, 1, 1], fetched[:, 1, 0], ADD)
+        nc.vector.tensor_tensor(sums[:, 0, 2], sums[:, 0, 1], fetched[:, 0, 1], ADD)
+        nc.sync.dma_start(out[:, :HALF], sums[:, 0, 2])
+        nc.vector.tensor_tensor(sums[:, 1, 3], sums[:, 1, 2], fetched[:, 1, 1], ADD)
+        nc.sync.dma_start(out[:, HALF:], sums[:, 1, 3])

@@ -20,6 +20,7 @@ U8 = mybir.dt.uint8
 FP8X4 = mybir.dt.float8_e4m3fn_x4
 MULT = mybir.AluOpType.mult
 ADD = mybir.AluOpType.add
+EQUAL = mybir.AluOpType.is_equal
 SILU = mybir.ActivationFunctionType.Silu
 COPY = mybir.ActivationFunctionType.Copy
 
@@ -27,9 +28,10 @@ FLOPS = 2 * K * S * N
 BYTES = K * T * 4 + E * K * N + E * K * N // 32 + N * E * 4 + S * 4 + P * (S + TOP * T) // LIST * 2 + N * T * 4
 
 RUN = 1024
-BANK = 512
-PAIR = 2
+CELL = 512
+QUAD = 32
 HALF = T // 2
+RAW_BYTES = PACK * RUN * 4
 
 
 def tile_moe_pre_lin_silu_kernel(
@@ -39,37 +41,48 @@ def tile_moe_pre_lin_silu_kernel(
     with ExitStack() as ctx:
         lists = ctx.enter_context(tc.tile_pool(name="lists", bufs=1))
         keep = ctx.enter_context(tc.tile_pool(name="keep", bufs=1))
-        ring = ctx.enter_context(tc.tile_pool(name="ring", bufs=3))
-        psum = ctx.enter_context(tc.psum_pool(name="psum", bufs=8))
+        placed = ctx.enter_context(tc.tile_pool(name="placed", bufs=1))
+        psum = ctx.enter_context(tc.psum_pool(name="psum", bufs=1))
 
         planes = [keep.tile([P, RUN + LIST], F32, tag=f"plane{i}", name=f"plane{i}") for i in range(PASSES * PACK)]
-        gates = [keep.tile([P, RUN], F32, name=f"gate{q}") for q in range(S // RUN)]
         w_scale = keep.tile([P, E * PASSES // 4, N], U8, align_bytes=64)
         nc.vector.memset(w_scale[:].bitcast(I32), 0)
-        warm_in = keep.tile([P, 1], F32)
-        nc.vector.memset(warm_in[:], 0.0)
-        warm_out = keep.tile([P, 1], F32)
-        nc.scalar.activation(warm_out[:], warm_in[:], SILU)
+        ones = keep.tile([P, QUAD], F32)
+        nc.vector.memset(ones[:], 1.0)
+        warm = keep.tile([P, 1], F32)
+        nc.scalar.activation(warm[:], ones[:, :1], SILU)
+        identity = keep.tile([P, P], F32)
+        nc.vector.memset(identity[:], 0.0)
+        column = keep.tile([P, QUAD], F32, align_bytes=64)
+        nc.vector.tensor_tensor_scan(column[:], ones[:], ones[:], 0.0, MULT, ADD)
+        row = keep.tile([P, QUAD], F32, align_bytes=64)
+        nc.vector.transpose(row[:], column[:])
+        for q in range(0, P, QUAD):
+            part = slice(q, q + QUAD)
+            nc.vector.tensor_tensor(identity[part, part], column[part, :], row[part, :], EQUAL)
 
         def load_plane(i):
             a, r = divmod(i, PACK)
             rows = xT[a * K_PASS : (a + 1) * K_PASS, :].rearrange("(p r) t -> p r t", r=PACK)
             nc.sync.dma_start(planes[i][:, :T], rows[:, r, :])
 
-        def load_gate(q):
-            nc.sync.dma_start(gates[q][:], gate[:P, q * RUN : (q + 1) * RUN])
+        def load_gate(turn, lo, hi):
+            tile = keep.tile([P, hi - lo], F32, align_bytes=64, tag=f"gate{turn}", name=f"gate{turn}")
+            nc.sync.dma_start(tile[:], gate[:P, lo:hi])
+            return tile
 
         slot_tokens = lists.tile([P, S // LIST], U16)
         nc.sync.dma_start(slot_tokens[:], offs)
-        load_plane(0)
-        load_gate(0)
-        for i in range(1, PACK):
+        for i in range(PACK):
             load_plane(i)
-        load_gate(1)
+        gate1 = load_gate(1, 0, 512)
         for i in range(PACK, PASSES * PACK):
             load_plane(i)
-        for q in range(2, S // RUN):
-            load_gate(q)
+        gate_rows = keep.tile([P, P], F32, align_bytes=64, tag="rows")
+        nc.sync.dma_start(gate_rows[:], gate[: P * P // S].rearrange("k (c q) -> (k c) q", q=P))
+        gate2 = load_gate(2, 512, 1536)
+        gate3 = load_gate(3, 1536, 2560)
+        gate4 = load_gate(4, 3584, 4096)
         scale_rows = w_scales.rearrange("(g h) a (q r) n -> h a r q g n", h=2, r=4)
         for j in range(4):
             for r in range(4):
@@ -87,97 +100,144 @@ def tile_moe_pre_lin_silu_kernel(
             nc.sync.dma_start(slots[:], pos)
             token_slots.append(slots)
 
-        codes = [keep.tile([P, S], U32, align_bytes=64, name=f"codes{a}") for a in range(PASSES)]
-        scales = [keep.tile([P, S], U8, align_bytes=64, name=f"scales{a}") for a in range(PASSES)]
-
-        def picked(a, r, lo, hi):
-            return planes[a * PACK + r][:].indirect(slot_tokens[:, lo // LIST : hi // LIST])
-
-        def by_pairs(tile, width):
-            return tile[:, :, :width].rearrange("p r (c i) -> p c r i", i=PAIR)
-
-        def quantise(a, lo, hi, woven):
-            nc.vector.quantize_mx(
-                out=codes[a][:, lo:hi].bitcast(FP8X4),
-                scales=scales[a][:, lo:hi],
-                in_=woven[:, : hi - lo].rearrange("p c r -> p (c r)"),
-            )
-
-        def vector_run(a, lo, hi):
-            q, width = lo // RUN, hi - lo
-            gated = keep.tile([P, PACK, RUN], F32, tag="gated")
-            for r in range(PACK):
-                nc.vector.tensor_tensor(
-                    gated[:, r, :width], picked(a, r, lo, hi), gates[q][:, lo - q * RUN : hi - q * RUN], MULT
+        turned = psum.tile([P, P], F32, tag=f"bank{S // CELL - 1}")
+        nc.tensor.transpose(turned[:], gate_rows[:], identity[:])
+        gate_cols = keep.tile([P, S // P], F32)
+        nc.vector.tensor_copy(gate_cols[:], turned[:, : S // P])
+        gate_banks = []
+        for j in range(S // CELL):
+            bank = psum.tile([P, CELL], F32, tag=f"bank{j}", name=f"gate_bank{j}")
+            for c in range(CELL // P):
+                col = j * CELL // P + c
+                nc.tensor.transpose(
+                    bank[:, c * P : (c + 1) * P], gate_cols[:, col : col + 1].to_broadcast([P, P]), identity[:]
                 )
-            woven = ring.tile([P, RUN, PACK], BF16, align_bytes=64, tag="woven")
-            nc.vector.tensor_copy(woven[:, :width].rearrange("p (c i) r -> p c r i", i=PAIR), by_pairs(gated, width))
-            quantise(a, lo, hi, woven)
+            gate_banks.append(bank)
 
-        def scalar_run(a, lo, hi):
-            q, width = lo // RUN, hi - lo
-            raw = ring.tile([P, PACK, RUN], F32, tag="raw")
+        codes = [keep.tile([P, S], U32, align_bytes=64, name=f"codes{a}") for a in range(PASSES)]
+        scale_of = {}
+        sums_of = {}
+
+        def gather(engine, a, lo, hi, raw):
             for r in range(PACK):
-                nc.scalar.activation(raw[:, r, :width], picked(a, r, lo, hi), COPY)
-            woven = ring.tile([P, RUN, PACK], BF16, align_bytes=64, tag="woven")
-            weights = gates[q][:, lo - q * RUN : hi - q * RUN].rearrange("p (c i) -> p c i", i=PAIR)
-            nc.vector.tensor_tensor(
-                woven[:, :width].rearrange("p (c i) r -> p c r i", i=PAIR),
-                by_pairs(raw, width),
-                weights.unsqueeze(2).to_broadcast([P, width // PAIR, PACK, PAIR]),
+                picked = planes[a * PACK + r][:].indirect(slot_tokens[:, lo // LIST : hi // LIST])
+                if engine is nc.vector:
+                    nc.vector.tensor_copy(raw[:, r], picked)
+                else:
+                    nc.scalar.activation(raw[:, r], picked, COPY)
+            return raw
+
+        def staging(tag, lo, hi):
+            return keep.tile([P, PACK, hi - lo], F32, tag=tag, name=tag)
+
+        def weave(engine, woven, raw, weights, run):
+            width = weights.shape[1]
+            engine.tensor_tensor(
+                woven.rearrange("p (c i) r -> p c r i", i=run),
+                raw.rearrange("p r (c i) -> p c r i", i=run),
+                weights.rearrange("p (c i) -> p c i", i=run).unsqueeze(2).to_broadcast([P, width // run, PACK, run]),
                 MULT,
             )
-            quantise(a, lo, hi, woven)
 
-        banks = []
+        def multiply(e):
+            j, col = divmod(e * C, CELL)
+            if col == 0:
+                sums_of[j] = psum.tile([N, CELL], F32, tag=f"bank{j}", name=f"sums{j}")
+            for a in range(PASSES):
+                g = e * PASSES + a
+                nc.tensor.matmul_mx(
+                    out=sums_of[j][:, col : col + C],
+                    lhsT=w_codes[:, g, :].bitcast(FP8X4),
+                    lhsT_scale=w_scale[4 * (g % 4) :, g // 4, :],
+                    rhs=codes[a][:, e * C : (e + 1) * C].bitcast(FP8X4),
+                    rhs_scale=scale_of[a, e],
+                    start=(a == 0),
+                    stop=(a == PASSES - 1),
+                )
 
-        def multiply(lo, hi):
-            for s0 in range(lo, hi, BANK):
-                bank = psum.tile([N, BANK], F32, tag="bank")
-                banks.append(bank)
-                for e in range(s0 // C, (s0 + BANK) // C):
-                    for a in range(PASSES):
-                        g = e * PASSES + a
-                        nc.tensor.matmul_mx(
-                            out=bank[:, e * C - s0 : (e + 1) * C - s0],
-                            lhsT=w_codes[:, g, :].bitcast(FP8X4),
-                            lhsT_scale=w_scale[4 * (g % 4) :, g // 4, :],
-                            rhs=codes[a][:, e * C : (e + 1) * C].bitcast(FP8X4),
-                            rhs_scale=scales[a][:, e * C : (e + 1) * C],
-                            start=(a == 0),
-                            stop=(a == PASSES - 1),
-                        )
+        def quantise(a, lo, hi, woven, scales):
+            nc.vector.quantize_mx(
+                out=codes[a][:, lo:hi].bitcast(FP8X4), scales=scales, in_=woven.rearrange("p c r -> p (c r)")
+            )
+            for e in range(lo // C, hi // C):
+                scale_of[a, e] = scales[:, e * C - lo : (e + 1) * C - lo]
+                if (1 - a, e) in scale_of:
+                    multiply(e)
 
-        vector_run(0, 0, RUN)
-        scalar_run(0, RUN, 2 * RUN)
-        vector_run(1, 0, RUN)
-        multiply(0, RUN)
-        scalar_run(0, 2 * RUN, 3 * RUN)
-        scalar_run(0, 3 * RUN, S)
-        scalar_run(1, RUN, 2 * RUN)
-        multiply(RUN, 2 * RUN)
-        scalar_run(1, 2 * RUN, 3 * RUN)
-        multiply(2 * RUN, 3 * RUN)
-        scalar_run(1, 3 * RUN, S - BANK)
-        multiply(3 * RUN, S - BANK)
-        scalar_run(1, S - BANK, S)
-        multiply(S - BANK, S)
+        def vector_cells(cells):
+            woven = keep.tile([P, len(cells), CELL, PACK], BF16, align_bytes=64, tag="woven_v")
+            for n, (a, lo, raw) in enumerate(cells):
+                weave(nc.vector, woven[:, n], raw, gate_banks[lo // CELL][:], 2)
+            return [(a, lo, lo + CELL, woven[:, n]) for n, (a, lo, raw) in enumerate(cells)]
+
+        def batch(tag, pieces):
+            scales = keep.tile([P, sum(hi - lo for a, lo, hi, woven in pieces)], U8, align_bytes=64, tag=tag, name=tag)
+            col = 0
+            for a, lo, hi, woven in pieces:
+                quantise(a, lo, hi, woven, scales[:, col : col + hi - lo])
+                col = col + hi - lo
+
+        def gpsimd_turn(a, lo, hi, raw, weights, tag="woven_g", offset=RAW_BYTES):
+            woven = placed.tile([P, hi - lo, PACK], BF16, align_bytes=64, tag=tag, offset=offset, name=tag)
+            weave(nc.gpsimd, woven[:], raw[:], weights[:], 4)
+            return (a, lo, hi, woven[:])
+
+        v1 = gather(nc.vector, 0, 0, 512, staging("raw0", 0, 512))
+        s1 = gather(nc.scalar, 0, 512, 1536, staging("raw1", 512, 1536))
+        turn = gpsimd_turn(0, 0, 512, v1, gate1, "woven_first", RAW_BYTES - 2048)
+        v2 = gather(nc.vector, 1, 0, 512, staging("raw4", 0, 512))
+        s2 = gather(nc.scalar, 1, 512, 1536, staging("raw2", 512, 1536))
+        s3 = gather(nc.scalar, 1, 1536, 2560, staging("raw3", 1536, 2560))
+        batch("rows", [turn])
+
+        turn = gpsimd_turn(0, 512, 1536, s1, gate2)
+        v3 = gather(nc.vector, 0, 1536, 2560, placed.tile([P, PACK, RUN], F32, align_bytes=64, offset=0, name="v3"))
+        cells = vector_cells([(1, 0, v2[:])])
+        s4 = gather(nc.scalar, 0, 2560, 3584, staging("raw4", 2560, 3584))
+        batch("gate2", cells + [turn])
+
+        turn = gpsimd_turn(0, 1536, 2560, v3, gate3)
+        v4 = gather(nc.vector, 0, 3584, 4096, staging("raw1", 3584, 4096))
+        cells = vector_cells([(1, 512, s2[:, :, :CELL]), (1, 1024, s2[:, :, CELL:]), (1, 1536, s3[:, :, :CELL])])
+        s5 = gather(nc.scalar, 1, 2560, 3584, staging("raw2", 2560, 3584))
+        s6 = gather(nc.scalar, 1, 3584, 4096, staging("raw0", 3584, 4096))
+        batch("gate3", cells + [turn])
+
+        turn = gpsimd_turn(0, 3584, 4096, v4, gate4)
+        cells = vector_cells([(1, 2048, s3[:, :, CELL:]), (0, 2560, s4[:, :, :CELL]), (0, 3072, s4[:, :, CELL:])])
+        batch("gate4", cells + [turn])
+
+        woven = keep.tile([P, S - 2560, PACK], BF16, align_bytes=64, tag="woven_v")
+        scales = keep.tile([P, S - 2560], U8, align_bytes=64, tag="gate1")
+        pieces = [(2560, 3072, s5[:, :, :CELL]), (3072, 3584, s5[:, :, CELL:])]
+        pieces = pieces + [(3584, 3840, s6[:, :, :C]), (3840, 4096, s6[:, :, C:])]
+        for n in range(len(pieces) + 1):
+            if n < len(pieces):
+                lo, hi, raw = pieces[n]
+                weights = gate_banks[lo // CELL][:, lo % CELL : lo % CELL + hi - lo]
+                weave(nc.vector, woven[:, lo - 2560 : hi - 2560], raw, weights, 2)
+            if n > 0:
+                lo, hi, raw = pieces[n - 1]
+                if hi < 3840:
+                    quantise(1, lo, hi, woven[:, lo - 2560 : hi - 2560], scales[:, lo - 2560 : hi - 2560])
+        for lo, hi, raw in pieces[2:]:
+            quantise(1, lo, hi, woven[:, lo - 2560 : hi - 2560], scales[:, lo - 2560 : hi - 2560])
 
         y = keep.tile([N, S], F32, tag=f"plane{PASSES * PACK - 1}")
         for e in range(E):
-            col = e * C % BANK
+            j, col = divmod(e * C, CELL)
             nc.scalar.activation(
-                y[:, e * C : (e + 1) * C], banks[e * C // BANK][:, col : col + C], SILU, bias=bias[:, e : e + 1]
+                y[:, e * C : (e + 1) * C], sums_of[j][:, col : col + C], SILU, bias=bias[:, e : e + 1]
             )
 
         def result(j, h):
             return y[:].indirect(token_slots[j][:, h * HALF // LIST : (h + 1) * HALF // LIST])
 
-        fetched = ring.tile([N, 2, 2, HALF], F32, tag="raw")
+        fetched = keep.tile([N, 2, 2, HALF], F32, tag="raw1")
         for h in range(2):
             for j in range(2):
                 nc.scalar.activation(fetched[:, h, j], result(j, h), COPY)
-        sums = ring.tile([N, 2, TOP, HALF], F32, tag="raw")
+        sums = keep.tile([N, 2, TOP, HALF], F32, tag="raw2")
         nc.vector.tensor_copy(sums[:, 1, 0], result(2, 1))
         nc.vector.tensor_tensor(sums[:, 0, 0], result(2, 0), fetched[:, 0, 0], ADD)
         nc.vector.tensor_tensor(sums[:, 1, 1], result(3, 1), sums[:, 1, 0], ADD)

@@ -179,7 +179,12 @@ def tile_moe_pre_lin_silu_kernel(
 
         def gpsimd_turn(a, lo, hi, raw, weights, tag="woven_g", offset=RAW_BYTES):
             woven = placed.tile([P, hi - lo, PACK], BF16, align_bytes=64, tag=tag, offset=offset, name=tag)
-            weave(nc.gpsimd, woven[:], raw[:], weights[:], 4)
+            nc.gpsimd.tensor_tensor(
+                woven[:],
+                raw[:].rearrange("p r c -> p c r"),
+                weights[:].unsqueeze(2).to_broadcast([P, hi - lo, PACK]),
+                MULT,
+            )
             return (a, lo, hi, woven[:])
 
         v1 = gather(nc.vector, 0, 0, 512, staging("raw0", 0, 512))

@@ -30,8 +30,6 @@ BYTES = K * T * 4 + E * K * N + E * K * N // 32 + N * E * 4 + S * 4 + P * (S + T
 RUN = 1024
 CELL = 512
 QUAD = 32
-HALF = T // 2
-RAW_BYTES = PACK * RUN * 4
 
 
 def tile_moe_pre_lin_silu_kernel(
@@ -41,7 +39,6 @@ def tile_moe_pre_lin_silu_kernel(
     with ExitStack() as ctx:
         lists = ctx.enter_context(tc.tile_pool(name="lists", bufs=1))
         keep = ctx.enter_context(tc.tile_pool(name="keep", bufs=1))
-        placed = ctx.enter_context(tc.tile_pool(name="placed", bufs=1))
         psum = ctx.enter_context(tc.psum_pool(name="psum", bufs=1))
 
         planes = [keep.tile([P, RUN + LIST], F32, tag=f"plane{i}", name=f"plane{i}") for i in range(PASSES * PACK)]
@@ -118,8 +115,8 @@ def tile_moe_pre_lin_silu_kernel(
         scale_of = {}
         sums_of = {}
 
-        def gather(engine, a, lo, hi, raw):
-            for r in range(PACK):
+        def gather(engine, a, lo, hi, raw, rows=range(PACK)):
+            for r in rows:
                 picked = planes[a * PACK + r][:].indirect(slot_tokens[:, lo // LIST : hi // LIST])
                 if engine is nc.vector:
                     nc.vector.tensor_copy(raw[:, r], picked)
@@ -128,7 +125,7 @@ def tile_moe_pre_lin_silu_kernel(
             return raw
 
         def staging(tag, lo, hi):
-            return keep.tile([P, PACK, hi - lo], F32, tag=tag, name=tag)
+            return keep.tile([P, PACK, hi - lo], F32, align_bytes=64, tag=tag, name=tag)
 
         def weave(engine, woven, raw, weights, run):
             width = weights.shape[1]
@@ -165,10 +162,10 @@ def tile_moe_pre_lin_silu_kernel(
                     multiply(e)
 
         def vector_cells(cells):
-            woven = keep.tile([P, len(cells), CELL, PACK], BF16, align_bytes=64, tag="woven_v")
-            for n, (a, lo, raw) in enumerate(cells):
-                weave(nc.vector, woven[:, n], raw, gate_banks[lo // CELL][:], 2)
-            return [(a, lo, lo + CELL, woven[:, n]) for n, (a, lo, raw) in enumerate(cells)]
+            woven = keep.tile([P, len(cells) * CELL, PACK], BF16, align_bytes=64, tag="woven_v")
+            for n, (lo, raw) in enumerate(cells):
+                weave(nc.vector, woven[:, n * CELL : (n + 1) * CELL], raw, gate_banks[lo // CELL][:], 2)
+            return woven
 
         def batch(tag, pieces):
             scales = keep.tile([P, sum(hi - lo for a, lo, hi, woven in pieces)], U8, align_bytes=64, tag=tag, name=tag)
@@ -177,8 +174,8 @@ def tile_moe_pre_lin_silu_kernel(
                 quantise(a, lo, hi, woven, scales[:, col : col + hi - lo])
                 col = col + hi - lo
 
-        def gpsimd_turn(a, lo, hi, raw, weights, tag="woven_g", offset=RAW_BYTES):
-            woven = placed.tile([P, hi - lo, PACK], BF16, align_bytes=64, tag=tag, offset=offset, name=tag)
+        def gpsimd_turn(a, lo, hi, raw, weights, tag="woven_g"):
+            woven = keep.tile([P, hi - lo, PACK], BF16, align_bytes=64, tag=tag, name=tag)
             nc.gpsimd.tensor_tensor(
                 woven[:],
                 raw[:].rearrange("p r c -> p c r"),
@@ -189,44 +186,31 @@ def tile_moe_pre_lin_silu_kernel(
 
         v1 = gather(nc.vector, 0, 0, 512, staging("raw0", 0, 512))
         s1 = gather(nc.scalar, 0, 512, 1536, staging("raw1", 512, 1536))
-        turn = gpsimd_turn(0, 0, 512, v1, gate1, "woven_first", RAW_BYTES - 2048)
+        first = gpsimd_turn(0, 0, 512, v1, gate1, "woven_first")
         v2 = gather(nc.vector, 1, 0, 512, staging("raw4", 0, 512))
+        v3 = gather(nc.vector, 1, 1536, 2560, staging("raw3", 1536, 2560))
         s2 = gather(nc.scalar, 1, 512, 1536, staging("raw2", 512, 1536))
-        s3 = gather(nc.scalar, 1, 1536, 2560, staging("raw3", 1536, 2560))
-        batch("rows", [turn])
-
+        s3 = gather(nc.scalar, 0, 1536, 2560, staging("rows", 1536, 2560))
         turn = gpsimd_turn(0, 512, 1536, s1, gate2)
-        v3 = gather(nc.vector, 0, 1536, 2560, placed.tile([P, PACK, RUN], F32, align_bytes=64, offset=0, name="v3"))
-        cells = vector_cells([(1, 0, v2[:])])
+        woven = vector_cells([(0, v2[:]), (512, s2[:, :, :CELL]), (1024, s2[:, :, CELL:])])
         s4 = gather(nc.scalar, 0, 2560, 3584, staging("raw4", 2560, 3584))
-        batch("gate2", cells + [turn])
-
-        turn = gpsimd_turn(0, 1536, 2560, v3, gate3)
-        v4 = gather(nc.vector, 0, 3584, 4096, staging("raw1", 3584, 4096))
-        cells = vector_cells([(1, 512, s2[:, :, :CELL]), (1, 1024, s2[:, :, CELL:]), (1, 1536, s3[:, :, :CELL])])
+        v4 = gather(nc.scalar, 0, 3584, 4096, staging("raw1", 3584, 4096), [0])
         s5 = gather(nc.scalar, 1, 2560, 3584, staging("raw2", 2560, 3584))
-        s6 = gather(nc.scalar, 1, 3584, 4096, staging("raw0", 3584, 4096))
-        batch("gate3", cells + [turn])
+        batch("gate2", [(1, 0, 1024, woven[:, :1024]), (1, 1024, 1536, woven[:, 1024:]), first, turn])
+
+        turn = gpsimd_turn(1, 1536, 2560, v3, gate3)
+        gather(nc.vector, 0, 3584, 4096, v4, [1, 2, 3])
+        s6 = gather(nc.scalar, 1, 3584, 4096, staging("raw3", 3584, 4096))
+        woven = vector_cells(
+            [(1536, s3[:, :, :CELL]), (2048, s3[:, :, CELL:]), (2560, s4[:, :, :CELL]), (3072, s4[:, :, CELL:])]
+        )
+        batch("gate3", [(0, 1536, 2560, woven[:, :1024]), (0, 2560, 3584, woven[:, 1024:]), turn])
 
         turn = gpsimd_turn(0, 3584, 4096, v4, gate4)
-        cells = vector_cells([(1, 2048, s3[:, :, CELL:]), (0, 2560, s4[:, :, :CELL]), (0, 3072, s4[:, :, CELL:])])
-        batch("gate4", cells + [turn])
-
-        woven = keep.tile([P, S - 2560, PACK], BF16, align_bytes=64, tag="woven_v")
-        scales = keep.tile([P, S - 2560], U8, align_bytes=64, tag="gate1")
-        pieces = [(2560, 3072, s5[:, :, :CELL]), (3072, 3584, s5[:, :, CELL:])]
-        pieces = pieces + [(3584, 3840, s6[:, :, :C]), (3840, 4096, s6[:, :, C:])]
-        for n in range(len(pieces) + 1):
-            if n < len(pieces):
-                lo, hi, raw = pieces[n]
-                weights = gate_banks[lo // CELL][:, lo % CELL : lo % CELL + hi - lo]
-                weave(nc.vector, woven[:, lo - 2560 : hi - 2560], raw, weights, 2)
-            if n > 0:
-                lo, hi, raw = pieces[n - 1]
-                if hi < 3840:
-                    quantise(1, lo, hi, woven[:, lo - 2560 : hi - 2560], scales[:, lo - 2560 : hi - 2560])
-        for lo, hi, raw in pieces[2:]:
-            quantise(1, lo, hi, woven[:, lo - 2560 : hi - 2560], scales[:, lo - 2560 : hi - 2560])
+        woven = vector_cells([(2560, s5[:, :, :CELL]), (3072, s5[:, :, CELL:]), (3584, s6[:])])
+        cuts = [2560, 3072, 3584, 3840, 4096]
+        pieces = [(1, lo, hi, woven[:, lo - 2560 : hi - 2560]) for lo, hi in zip(cuts, cuts[1:])]
+        batch("gate4", pieces[:2] + [turn] + pieces[2:])
 
         y = keep.tile([N, S], F32, tag=f"plane{PASSES * PACK - 1}")
         for e in range(E):
@@ -235,20 +219,40 @@ def tile_moe_pre_lin_silu_kernel(
                 y[:, e * C : (e + 1) * C], sums_of[j][:, col : col + C], SILU, bias=bias[:, e : e + 1]
             )
 
-        def result(j, h):
-            return y[:].indirect(token_slots[j][:, h * HALF // LIST : (h + 1) * HALF // LIST])
+        def result(j, lo, hi):
+            return y[:].indirect(token_slots[j][:, lo // LIST : hi // LIST])
 
-        fetched = keep.tile([N, 2, 2, HALF], F32, tag="raw1")
-        for h in range(2):
-            for j in range(2):
-                nc.scalar.activation(fetched[:, h, j], result(j, h), COPY)
-        sums = keep.tile([N, 2, TOP, HALF], F32, tag="raw2")
-        nc.vector.tensor_copy(sums[:, 1, 0], result(2, 1))
-        nc.vector.tensor_tensor(sums[:, 0, 0], result(2, 0), fetched[:, 0, 0], ADD)
-        nc.vector.tensor_tensor(sums[:, 1, 1], result(3, 1), sums[:, 1, 0], ADD)
-        nc.vector.tensor_tensor(sums[:, 0, 1], result(3, 0), sums[:, 0, 0], ADD)
-        nc.vector.tensor_tensor(sums[:, 1, 2], sums[:, 1, 1], fetched[:, 1, 0], ADD)
-        nc.vector.tensor_tensor(sums[:, 0, 2], sums[:, 0, 1], fetched[:, 0, 1], ADD)
-        nc.sync.dma_start(out[:, :HALF], sums[:, 0, 2])
-        nc.vector.tensor_tensor(sums[:, 1, 3], sums[:, 1, 2], fetched[:, 1, 1], ADD)
-        nc.sync.dma_start(out[:, HALF:], sums[:, 1, 3])
+        fetched = keep.tile([N, TOP - 1, T], F32, align_bytes=64, tag="raw1")
+        sums = keep.tile([N, TOP, T], F32, align_bytes=64, tag="raw2")
+        own, narrow, wide = slice(0, 256), slice(256, 512), slice(512, T)
+        for j in range(TOP - 1):
+            for part in (narrow, wide):
+                nc.scalar.activation(fetched[:, j, part], result(j, part.start, part.stop), COPY)
+
+        def own_step(j):
+            picked = result(j, own.start, own.stop)
+            if j == 0:
+                nc.vector.tensor_copy(sums[:, 0, own], picked)
+            else:
+                nc.vector.tensor_tensor(sums[:, j, own], picked, sums[:, j - 1, own], ADD)
+
+        def shared_step(j, part):
+            if j == 0:
+                picked = result(TOP - 1, part.start, part.stop)
+                nc.vector.tensor_tensor(sums[:, 0, part], picked, fetched[:, 0, part], ADD)
+            else:
+                nc.vector.tensor_tensor(sums[:, j, part], sums[:, j - 1, part], fetched[:, j, part], ADD)
+
+        own_step(0)
+        shared_step(0, narrow)
+        own_step(1)
+        shared_step(0, wide)
+        own_step(2)
+        shared_step(1, narrow)
+        own_step(3)
+        nc.sync.dma_start(out[:, own], sums[:, TOP - 1, own])
+        shared_step(1, wide)
+        shared_step(2, narrow)
+        nc.sync.dma_start(out[:, narrow], sums[:, TOP - 2, narrow])
+        shared_step(2, wide)
+        nc.sync.dma_start(out[:, wide], sums[:, TOP - 2, wide])

@@ -87,8 +87,8 @@ def tile_moe_pre_lin_silu_kernel(
                 nc.sync.dma_start(w_scale[4 * j + r : P : 32, :, :].bitcast(I32), rows.bitcast(I32))
         w_codes = keep.tile([P, E * PASSES, N * PACK], U8, align_bytes=64)
         words = w_words.rearrange("e a p n r -> p (e a) (n r)")
-        for lo in range(0, E * PASSES, 8):
-            nc.sync.dma_start(w_codes[:, lo : lo + 8].bitcast(I32), words[:, lo : lo + 8].bitcast(I32))
+        for lo in range(0, E * PASSES, E):
+            nc.sync.dma_start(w_codes[:, lo : lo + E].bitcast(I32), words[:, lo : lo + E].bitcast(I32))
         bias = keep.tile([N, E], F32)
         nc.sync.dma_start(bias[:], b)
         token_slots = []
@@ -174,43 +174,59 @@ def tile_moe_pre_lin_silu_kernel(
                 quantise(a, lo, hi, woven, scales[:, col : col + hi - lo])
                 col = col + hi - lo
 
-        def gpsimd_turn(a, lo, hi, raw, weights, tag="woven_g"):
-            woven = keep.tile([P, hi - lo, PACK], BF16, align_bytes=64, tag=tag, name=tag)
-            nc.gpsimd.tensor_tensor(
-                woven[:],
-                raw[:].rearrange("p r c -> p c r"),
-                weights[:].unsqueeze(2).to_broadcast([P, hi - lo, PACK]),
-                MULT,
-            )
-            return (a, lo, hi, woven[:])
+        def gpsimd_turn(pieces):
+            woven = keep.tile([P, sum(raw.shape[2] for raw, weights in pieces), PACK], BF16, align_bytes=64, tag="woven_g")
+            col = 0
+            for raw, weights in pieces:
+                width = raw.shape[2]
+                nc.gpsimd.tensor_tensor(
+                    woven[:, col : col + width],
+                    raw.rearrange("p r c -> p c r"),
+                    weights.unsqueeze(2).to_broadcast([P, width, PACK]),
+                    MULT,
+                )
+                col = col + width
+            return woven
 
         v1 = gather(nc.vector, 0, 0, 512, staging("raw0", 0, 512))
         s1 = gather(nc.scalar, 0, 512, 1536, staging("raw1", 512, 1536))
-        first = gpsimd_turn(0, 0, 512, v1, gate1, "woven_first")
         v2 = gather(nc.vector, 1, 0, 512, staging("raw4", 0, 512))
         v3 = gather(nc.vector, 1, 1536, 2560, staging("raw3", 1536, 2560))
         s2 = gather(nc.scalar, 1, 512, 1536, staging("raw2", 512, 1536))
         s3 = gather(nc.scalar, 0, 1536, 2560, staging("rows", 1536, 2560))
-        turn = gpsimd_turn(0, 512, 1536, s1, gate2)
-        woven = vector_cells([(0, v2[:]), (512, s2[:, :, :CELL]), (1024, s2[:, :, CELL:])])
+        turn = gpsimd_turn([(v1[:], gate1[:]), (s1[:], gate2[:])])
+        woven = vector_cells([(0, v2[:])])
         s4 = gather(nc.scalar, 0, 2560, 3584, staging("raw4", 2560, 3584))
-        v4 = gather(nc.scalar, 0, 3584, 4096, staging("raw1", 3584, 4096), [0])
-        s5 = gather(nc.scalar, 1, 2560, 3584, staging("raw2", 2560, 3584))
-        batch("gate2", [(1, 0, 1024, woven[:, :1024]), (1, 1024, 1536, woven[:, 1024:]), first, turn])
+        batch("gate2", [(1, 0, 512, woven[:]), (0, 0, 512, turn[:, :512]), (0, 512, 1536, turn[:, 512:])])
 
-        turn = gpsimd_turn(1, 1536, 2560, v3, gate3)
-        gather(nc.vector, 0, 3584, 4096, v4, [1, 2, 3])
+        turn = gpsimd_turn([(v3[:], gate3[:]), (s3[:, :, :CELL], gate3[:, :CELL])])
+        v4 = gather(nc.vector, 0, 3584, 4096, staging("raw1", 3584, 4096))
+        woven = keep.tile([P, 5 * CELL, PACK], BF16, align_bytes=64, tag="woven_v")
+        for n in range(2):
+            weave(nc.vector, woven[:, n * CELL : (n + 1) * CELL], s2[:, :, n * CELL : (n + 1) * CELL], gate_banks[1 + n][:], 2)
+        s5 = staging("raw2", 2560, 3584)
+        gather(nc.vector, 1, 2560, 3072, s5[:, :, :CELL], [0])
+        for n, raw in enumerate((s3[:, :, CELL:], s4[:, :, :CELL], s4[:, :, CELL:])):
+            weave(nc.vector, woven[:, (2 + n) * CELL : (3 + n) * CELL], raw, gate_banks[4 + n][:], 2)
+        gather(nc.scalar, 1, 3072, 3584, s5[:, :, CELL:], [0])
+        gather(nc.scalar, 1, 2560, 3584, s5, [1, 2, 3])
         s6 = gather(nc.scalar, 1, 3584, 4096, staging("raw3", 3584, 4096))
-        woven = vector_cells(
-            [(1536, s3[:, :, :CELL]), (2048, s3[:, :, CELL:]), (2560, s4[:, :, :CELL]), (3072, s4[:, :, CELL:])]
+        batch(
+            "gate3",
+            [
+                (1, 512, 1536, woven[:, :1024]),
+                (0, 2048, 3072, woven[:, 1024:2048]),
+                (0, 3072, 3584, woven[:, 2048:]),
+                (0, 1536, 2048, turn[:, 1024:]),
+                (1, 1536, 2560, turn[:, :1024]),
+            ],
         )
-        batch("gate3", [(0, 1536, 2560, woven[:, :1024]), (0, 2560, 3584, woven[:, 1024:]), turn])
 
-        turn = gpsimd_turn(0, 3584, 4096, v4, gate4)
+        turn = gpsimd_turn([(v4[:], gate4[:])])
         woven = vector_cells([(2560, s5[:, :, :CELL]), (3072, s5[:, :, CELL:]), (3584, s6[:])])
         cuts = [2560, 3072, 3584, 3840, 4096]
         pieces = [(1, lo, hi, woven[:, lo - 2560 : hi - 2560]) for lo, hi in zip(cuts, cuts[1:])]
-        batch("gate4", pieces[:2] + [turn] + pieces[2:])
+        batch("gate4", pieces[:2] + [(0, 3584, 4096, turn[:])] + pieces[2:])
 
         y = keep.tile([N, S], F32, tag=f"plane{PASSES * PACK - 1}")
         for e in range(E):
@@ -226,7 +242,7 @@ def tile_moe_pre_lin_silu_kernel(
         sums = keep.tile([N, TOP, T], F32, align_bytes=64, tag="raw2")
         own, narrow, wide = slice(0, 256), slice(256, 512), slice(512, T)
         for j in range(TOP - 1):
-            for part in (narrow, wide):
+            for part in (narrow, wide) if j == 0 else (wide, narrow):
                 nc.scalar.activation(fetched[:, j, part], result(j, part.start, part.stop), COPY)
 
         def own_step(j):
@@ -248,11 +264,11 @@ def tile_moe_pre_lin_silu_kernel(
         own_step(1)
         shared_step(0, wide)
         own_step(2)
-        shared_step(1, narrow)
+        shared_step(1, wide)
         own_step(3)
         nc.sync.dma_start(out[:, own], sums[:, TOP - 1, own])
-        shared_step(1, wide)
-        shared_step(2, narrow)
-        nc.sync.dma_start(out[:, narrow], sums[:, TOP - 2, narrow])
+        shared_step(1, narrow)
         shared_step(2, wide)
         nc.sync.dma_start(out[:, wide], sums[:, TOP - 2, wide])
+        shared_step(2, narrow)
+        nc.sync.dma_start(out[:, narrow], sums[:, TOP - 2, narrow])

@@ -138,12 +138,15 @@ def tile_moe_pre_lin_silu_kernel(
 
         def multiply(e):
             j, col = divmod(e * C, CELL)
-            if col == 0:
-                sums_of[j] = psum.tile([N, CELL], F32, tag=f"bank{j}", name=f"sums{j}")
+            if e == E - 1:
+                sums_of[e] = psum.tile([N, C], F32, tag="bank0", name="last_sums")[:]
+            elif col == 0:
+                bank = psum.tile([N, CELL], F32, tag=f"bank{j}", name=f"sums{j}")
+                sums_of[e], sums_of[e + 1] = bank[:, :C], bank[:, C:]
             for a in range(PASSES):
                 g = e * PASSES + a
                 nc.tensor.matmul_mx(
-                    out=sums_of[j][:, col : col + C],
+                    out=sums_of[e],
                     lhsT=w_codes[:, g, :].bitcast(FP8X4),
                     lhsT_scale=w_scale[4 * (g % 4) :, g // 4, :],
                     rhs=codes[a][:, e * C : (e + 1) * C].bitcast(FP8X4),
@@ -196,44 +199,60 @@ def tile_moe_pre_lin_silu_kernel(
         s3 = gather(nc.scalar, 0, 1536, 2560, staging("rows", 1536, 2560))
         turn = gpsimd_turn([(v1[:], gate1[:]), (s1[:], gate2[:])])
         woven = vector_cells([(0, v2[:])])
-        s4 = gather(nc.scalar, 0, 2560, 3584, staging("raw4", 2560, 3584))
+        s4 = staging("raw4", 2560, 3584)
+        gather(nc.vector, 0, 2560, 3072, s4[:, :, :CELL], [0])
+        gather(nc.scalar, 0, 3072, 3584, s4[:, :, CELL:], [0])
+        gather(nc.scalar, 0, 2560, 3584, s4, [1, 2, 3])
         batch("gate2", [(1, 0, 512, woven[:]), (0, 0, 512, turn[:, :512]), (0, 512, 1536, turn[:, 512:])])
 
-        turn = gpsimd_turn([(v3[:], gate3[:]), (s3[:, :, :CELL], gate3[:, :CELL])])
-        v4 = gather(nc.vector, 0, 3584, 4096, staging("raw1", 3584, 4096))
-        woven = keep.tile([P, 5 * CELL, PACK], BF16, align_bytes=64, tag="woven_v")
+        turn = gpsimd_turn([(v3[:], gate3[:]), (s3[:, :, :C], gate3[:, :C])])
+        v4 = staging("raw1", 3584, 4096)
+        gather(nc.vector, 0, 3584, 4096, v4, [1, 2, 3])
+        gather(nc.scalar, 0, 3584, 4096, v4, [0])
+        woven = keep.tile([P, 5 * CELL + C, PACK], BF16, align_bytes=64, tag="woven_v")
         for n in range(2):
             weave(nc.vector, woven[:, n * CELL : (n + 1) * CELL], s2[:, :, n * CELL : (n + 1) * CELL], gate_banks[1 + n][:], 2)
-        s5 = staging("raw2", 2560, 3584)
-        gather(nc.vector, 1, 2560, 3072, s5[:, :, :CELL], [0])
+        weave(nc.vector, woven[:, 1024:1280], s3[:, :, C:CELL], gate_banks[3][:, C:], 2)
         for n, raw in enumerate((s3[:, :, CELL:], s4[:, :, :CELL], s4[:, :, CELL:])):
-            weave(nc.vector, woven[:, (2 + n) * CELL : (3 + n) * CELL], raw, gate_banks[4 + n][:], 2)
-        gather(nc.scalar, 1, 3072, 3584, s5[:, :, CELL:], [0])
-        gather(nc.scalar, 1, 2560, 3584, s5, [1, 2, 3])
-        s6 = gather(nc.scalar, 1, 3584, 4096, staging("raw3", 3584, 4096))
+            weave(nc.vector, woven[:, 1280 + n * CELL : 1280 + (n + 1) * CELL], raw, gate_banks[4 + n][:], 2)
+        s5 = gather(nc.scalar, 1, 2560, 3584, staging("raw2", 2560, 3584))
+        s6 = staging("rows", 3584, 4096)
+        gather(nc.scalar, 1, 3584, 3840, s6[:, :, :C])
+        gather(nc.scalar, 1, 3840, 4096, s6[:, :, C:])
         batch(
             "gate3",
             [
                 (1, 512, 1536, woven[:, :1024]),
-                (0, 2048, 3072, woven[:, 1024:2048]),
-                (0, 3072, 3584, woven[:, 2048:]),
-                (0, 1536, 2048, turn[:, 1024:]),
+                (0, 1792, 2816, woven[:, 1024:2048]),
+                (0, 2816, 3328, woven[:, 2048:2560]),
+                (0, 3328, 3584, woven[:, 2560:]),
+                (0, 1536, 1792, turn[:, 1024:]),
                 (1, 1536, 2560, turn[:, :1024]),
             ],
         )
 
-        turn = gpsimd_turn([(v4[:], gate4[:])])
-        woven = vector_cells([(2560, s5[:, :, :CELL]), (3072, s5[:, :, CELL:]), (3584, s6[:])])
-        cuts = [2560, 3072, 3584, 3840, 4096]
-        pieces = [(1, lo, hi, woven[:, lo - 2560 : hi - 2560]) for lo, hi in zip(cuts, cuts[1:])]
-        batch("gate4", pieces[:2] + [(0, 3584, 4096, turn[:])] + pieces[2:])
-
         y = keep.tile([N, S], F32, tag=f"plane{PASSES * PACK - 1}")
-        for e in range(E):
-            j, col = divmod(e * C, CELL)
-            nc.scalar.activation(
-                y[:, e * C : (e + 1) * C], sums_of[j][:, col : col + C], SILU, bias=bias[:, e : e + 1]
-            )
+
+        def activate(e):
+            nc.scalar.activation(y[:, e * C : (e + 1) * C], sums_of[e], SILU, bias=bias[:, e : e + 1])
+
+        for e in range(E - 6):
+            activate(e)
+        turn = gpsimd_turn([(v4[:], gate4[:])])
+        woven = keep.tile([P, 3 * CELL, PACK], BF16, align_bytes=64, tag="woven_v")
+        scales = keep.tile([P, 4 * CELL], U8, align_bytes=64, tag="gate4")
+        for n in range(2):
+            weave(nc.vector, woven[:, n * CELL : (n + 1) * CELL], s5[:, :, n * CELL : (n + 1) * CELL], gate_banks[5 + n][:], 2)
+        weave(nc.vector, woven[:, 1024:1280], s6[:, :, :C], gate_banks[7][:, :C], 2)
+        quantise(1, 2560, 3072, woven[:, :512], scales[:, :512])
+        quantise(1, 3072, 3584, woven[:, 512:1024], scales[:, 512:1024])
+        quantise(0, 3584, 4096, turn[:], scales[:, 1024:1536])
+        weave(nc.vector, woven[:, 1280:], s6[:, :, C:], gate_banks[7][:, C:], 2)
+        quantise(1, 3584, 3840, woven[:, 1024:1280], scales[:, 1536:1792])
+        quantise(1, 3840, 4096, woven[:, 1280:], scales[:, 1792:])
+
+        for e in range(E - 6, E):
+            activate(e)
 
         def result(j, lo, hi):
             return y[:].indirect(token_slots[j][:, lo // LIST : hi // LIST])

@@ -70,16 +70,17 @@ def tile_moe_pre_lin_silu_kernel(
 
         slot_tokens = lists.tile([P, S // LIST], U16)
         nc.sync.dma_start(slot_tokens[:], offs)
-        for i in range(PACK):
-            load_plane(i)
-        gate1 = load_gate(1, 0, 512)
-        for i in range(PACK, PASSES * PACK):
+        load_plane(0)
+        gate1 = keep.tile([P, 768], F32)
+        for lo, hi in ((0, 256), (256, 768)):
+            nc.sync.dma_start(gate1[:, lo:hi], gate[:P, lo:hi])
+        for i in range(1, PASSES * PACK):
             load_plane(i)
         gate_rows = keep.tile([P, P], F32, align_bytes=64, tag="rows")
         nc.sync.dma_start(gate_rows[:], gate[: P * P // S].rearrange("k (c q) -> (k c) q", q=P))
-        gate2 = load_gate(2, 512, 1536)
+        gate2 = load_gate(2, 768, 1792)
         gate3 = load_gate(3, 1536, 2560)
-        gate4 = load_gate(4, 3584, 4096)
+        gate4 = load_gate(4, 3648, 4096)
         scale_rows = w_scales.rearrange("(g h) a (q r) n -> h a r q g n", h=2, r=4)
         for j in range(4):
             for r in range(4):
@@ -87,8 +88,7 @@ def tile_moe_pre_lin_silu_kernel(
                 nc.sync.dma_start(w_scale[4 * j + r : P : 32, :, :].bitcast(I32), rows.bitcast(I32))
         w_codes = keep.tile([P, E * PASSES, N * PACK], U8, align_bytes=64)
         words = w_words.rearrange("e a p n r -> p (e a) (n r)")
-        for lo in range(0, E * PASSES, E):
-            nc.sync.dma_start(w_codes[:, lo : lo + E].bitcast(I32), words[:, lo : lo + E].bitcast(I32))
+        nc.sync.dma_start(w_codes[:].bitcast(I32), words.bitcast(I32))
         bias = keep.tile([N, E], F32)
         nc.sync.dma_start(bias[:], b)
         token_slots = []
@@ -177,44 +177,54 @@ def tile_moe_pre_lin_silu_kernel(
                 quantise(a, lo, hi, woven, scales[:, col : col + hi - lo])
                 col = col + hi - lo
 
-        def gpsimd_turn(pieces):
-            woven = keep.tile([P, sum(raw.shape[2] for raw, weights in pieces), PACK], BF16, align_bytes=64, tag="woven_g")
-            col = 0
-            for raw, weights in pieces:
-                width = raw.shape[2]
-                nc.gpsimd.tensor_tensor(
-                    woven[:, col : col + width],
-                    raw.rearrange("p r c -> p c r"),
-                    weights.unsqueeze(2).to_broadcast([P, width, PACK]),
-                    MULT,
-                )
-                col = col + width
-            return woven
+        def gpsimd_weave(woven, raw, weights):
+            nc.gpsimd.tensor_tensor(
+                woven, raw.rearrange("p r c -> p c r"), weights.unsqueeze(2).to_broadcast(woven.shape), MULT
+            )
 
-        v1 = gather(nc.vector, 0, 0, 512, staging("raw0", 0, 512))
-        s1 = gather(nc.scalar, 0, 512, 1536, staging("raw1", 512, 1536))
+        def turn_tile(width):
+            return keep.tile([P, width, PACK], BF16, align_bytes=64, tag="woven_g", name="turn")
+
+        v1 = staging("raw0", 0, 768)
+        for r in range(PACK):
+            for lo, hi in ((0, 256), (256, 768)) if r == 0 else ((0, 768),):
+                picked = planes[r][:].indirect(slot_tokens[:, lo // LIST : hi // LIST])
+                nc.vector.tensor_tensor(v1[:, r, lo:hi], picked, gate1[:, lo:hi], MULT)
+        s1 = gather(nc.scalar, 0, 768, 1792, staging("raw1", 768, 1792))
         v2 = gather(nc.vector, 1, 0, 512, staging("raw4", 0, 512))
         v3 = gather(nc.vector, 1, 1536, 2560, staging("raw3", 1536, 2560))
         s2 = gather(nc.scalar, 1, 512, 1536, staging("raw2", 512, 1536))
-        s3 = gather(nc.scalar, 0, 1536, 2560, staging("rows", 1536, 2560))
-        turn = gpsimd_turn([(v1[:], gate1[:]), (s1[:], gate2[:])])
+        s3 = gather(nc.scalar, 0, 1792, 2560, staging("rows", 1792, 2560))
+        turn = turn_tile(1792)
+        nc.gpsimd.tensor_scalar(turn[:, :768], v1[:].rearrange("p r c -> p c r"), 1.0, 0.0, MULT, ADD)
+        gpsimd_weave(turn[:, 768:], s1[:], gate2[:])
         woven = vector_cells([(0, v2[:])])
-        s4 = staging("raw4", 2560, 3584)
-        gather(nc.vector, 0, 2560, 3072, s4[:, :, :CELL], [0])
-        gather(nc.scalar, 0, 3072, 3584, s4[:, :, CELL:], [0])
-        gather(nc.scalar, 0, 2560, 3584, s4, [1, 2, 3])
-        batch("gate2", [(1, 0, 512, woven[:]), (0, 0, 512, turn[:, :512]), (0, 512, 1536, turn[:, 512:])])
+        s4 = gather(nc.scalar, 0, 2560, 3584, staging("raw4", 2560, 3584))
+        batch(
+            "gate2",
+            [
+                (1, 0, 512, woven[:]),
+                (0, 0, 1024, turn[:, :1024]),
+                (0, 1024, 1536, turn[:, 1024:1536]),
+                (0, 1536, 1792, turn[:, 1536:]),
+            ],
+        )
 
-        turn = gpsimd_turn([(v3[:], gate3[:]), (s3[:, :, :C], gate3[:, :C])])
+        turn = turn_tile(1280)
+        gpsimd_weave(turn[:, :1024], v3[:], gate3[:])
+        gpsimd_weave(turn[:, 1024:], s3[:, :, :C], gate3[:, C:CELL])
         v4 = staging("raw1", 3584, 4096)
         gather(nc.vector, 0, 3584, 4096, v4, [1, 2, 3])
         gather(nc.scalar, 0, 3584, 4096, v4, [0])
-        woven = keep.tile([P, 5 * CELL + C, PACK], BF16, align_bytes=64, tag="woven_v")
-        for n in range(2):
-            weave(nc.vector, woven[:, n * CELL : (n + 1) * CELL], s2[:, :, n * CELL : (n + 1) * CELL], gate_banks[1 + n][:], 2)
-        weave(nc.vector, woven[:, 1024:1280], s3[:, :, C:CELL], gate_banks[3][:, C:], 2)
-        for n, raw in enumerate((s3[:, :, CELL:], s4[:, :, :CELL], s4[:, :, CELL:])):
-            weave(nc.vector, woven[:, 1280 + n * CELL : 1280 + (n + 1) * CELL], raw, gate_banks[4 + n][:], 2)
+        woven = vector_cells(
+            [
+                (512, s2[:, :, :CELL]),
+                (1024, s2[:, :, CELL:]),
+                (2048, s3[:, :, C:]),
+                (2560, s4[:, :, :CELL]),
+                (3072, s4[:, :, CELL:]),
+            ]
+        )
         s5 = gather(nc.scalar, 1, 2560, 3584, staging("raw2", 2560, 3584))
         s6 = staging("rows", 3584, 4096)
         gather(nc.scalar, 1, 3584, 3840, s6[:, :, :C])
@@ -223,10 +233,9 @@ def tile_moe_pre_lin_silu_kernel(
             "gate3",
             [
                 (1, 512, 1536, woven[:, :1024]),
-                (0, 1792, 2816, woven[:, 1024:2048]),
-                (0, 2816, 3328, woven[:, 2048:2560]),
-                (0, 3328, 3584, woven[:, 2560:]),
-                (0, 1536, 1792, turn[:, 1024:]),
+                (0, 2048, 3072, woven[:, 1024:2048]),
+                (0, 3072, 3584, woven[:, 2048:]),
+                (0, 1792, 2048, turn[:, 1024:]),
                 (1, 1536, 2560, turn[:, :1024]),
             ],
         )
@@ -238,7 +247,9 @@ def tile_moe_pre_lin_silu_kernel(
 
         for e in range(E - 6):
             activate(e)
-        turn = gpsimd_turn([(v4[:], gate4[:])])
+        turn = turn_tile(CELL)
+        gpsimd_weave(turn[:, 64:], v4[:, :, 64:], gate4[:])
+        weave(nc.vector, turn[:, :64], v4[:, :, :64], gate_banks[7][:, :64], 2)
         woven = keep.tile([P, 3 * CELL, PACK], BF16, align_bytes=64, tag="woven_v")
         scales = keep.tile([P, 4 * CELL], U8, align_bytes=64, tag="gate4")
         for n in range(2):

@@ -10,6 +10,7 @@ PACK = 4
 K_PASS = P * PACK
 PASSES = K // K_PASS
 LIST = 16
+QUAD = 32
 
 F32 = mybir.dt.float32
 BF16 = mybir.dt.bfloat16
@@ -27,9 +28,18 @@ COPY = mybir.ActivationFunctionType.Copy
 FLOPS = 2 * K * S * N
 BYTES = K * T * 4 + E * K * N + E * K * N // 32 + N * E * 4 + S * 4 + P * (S + TOP * T) // LIST * 2 + N * T * 4
 
-RUN = 1024
 CELL = 512
-QUAD = 32
+RUN = 2 * CELL
+PAIR = 2
+W_PART = 8
+
+B1, B3, B4, B5, B6, B7 = (j * CELL for j in (1, 3, 4, 5, 6, 7))
+FUSED = 3 * C
+FIRST_GATE = C
+SECOND = FUSED + RUN
+SECOND_SHARE, LAST_SHARE = 32, 64
+SCALAR_SHARE = 128
+OWN, WIDE, MIDDLE, NARROW = slice(0, 288), slice(288, 672), slice(672, 896), slice(896, T)
 
 
 def tile_moe_pre_lin_silu_kernel(
@@ -42,7 +52,7 @@ def tile_moe_pre_lin_silu_kernel(
         psum = ctx.enter_context(tc.psum_pool(name="psum", bufs=1))
 
         planes = [keep.tile([P, RUN + LIST], F32, tag=f"plane{i}", name=f"plane{i}") for i in range(PASSES * PACK)]
-        w_scale = keep.tile([P, E * PASSES // 4, N], U8, align_bytes=64)
+        w_scale = keep.tile([P, E * PASSES, N], U8, align_bytes=64)
         nc.vector.memset(w_scale[:].bitcast(I32), 0)
         ones = keep.tile([P, QUAD], F32)
         nc.vector.memset(ones[:], 1.0)
@@ -54,16 +64,16 @@ def tile_moe_pre_lin_silu_kernel(
         nc.vector.tensor_tensor_scan(column[:], ones[:], ones[:], 0.0, MULT, ADD)
         row = keep.tile([P, QUAD], F32, align_bytes=64)
         nc.vector.transpose(row[:], column[:])
-        for q in range(0, P, QUAD):
-            part = slice(q, q + QUAD)
-            nc.vector.tensor_tensor(identity[part, part], column[part, :], row[part, :], EQUAL)
+        for start in range(0, P, QUAD):
+            quadrant = slice(start, start + QUAD)
+            nc.vector.tensor_tensor(identity[quadrant, quadrant], column[quadrant, :], row[quadrant, :], EQUAL)
 
         def load_plane(i):
             a, r = divmod(i, PACK)
             rows = xT[a * K_PASS : (a + 1) * K_PASS, :].rearrange("(p r) t -> p r t", r=PACK)
             nc.sync.dma_start(planes[i][:, :T], rows[:, r, :])
 
-        def load_gate(turn, lo, hi):
+        def load_turn_gate(turn, lo, hi):
             tile = keep.tile([P, hi - lo], F32, align_bytes=64, tag=f"gate{turn}", name=f"gate{turn}")
             nc.sync.dma_start(tile[:], gate[:P, lo:hi])
             return tile
@@ -71,24 +81,23 @@ def tile_moe_pre_lin_silu_kernel(
         slot_tokens = lists.tile([P, S // LIST], U16)
         nc.sync.dma_start(slot_tokens[:], offs)
         load_plane(0)
-        gate1 = keep.tile([P, 768], F32)
-        for lo, hi in ((0, 256), (256, 768)):
-            nc.sync.dma_start(gate1[:, lo:hi], gate[:P, lo:hi])
+        fused_gate = keep.tile([P, FUSED], F32)
+        for lo, hi in ((0, FIRST_GATE), (FIRST_GATE, FUSED)):
+            nc.sync.dma_start(fused_gate[:, lo:hi], gate[:P, lo:hi])
         for i in range(1, PASSES * PACK):
             load_plane(i)
-        gate_rows = keep.tile([P, P], F32, align_bytes=64, tag="rows")
+        gate_rows = keep.tile([P, P], F32, align_bytes=64, tag="staging5")
         nc.sync.dma_start(gate_rows[:], gate[: P * P // S].rearrange("k (c q) -> (k c) q", q=P))
-        gate2 = load_gate(2, 768, 1792)
-        gate3 = load_gate(3, 1536, 2560)
-        gate4 = load_gate(4, 3648, 4096)
-        scale_rows = w_scales.rearrange("(g h) a (q r) n -> h a r q g n", h=2, r=4)
-        for j in range(4):
-            for r in range(4):
-                rows = scale_rows[j // PASSES, j % PASSES, r]
-                nc.sync.dma_start(w_scale[4 * j + r : P : 32, :, :].bitcast(I32), rows.bitcast(I32))
+        gate1 = load_turn_gate(1, FUSED, SECOND)
+        gate2 = load_turn_gate(2, B3, B5)
+        gate3 = load_turn_gate(3, B7 + LAST_SHARE, S)
+        scale_rows = w_scales.rearrange("e a (q r) n -> r q (e a) n", r=PACK)
+        for r in range(PACK):
+            nc.sync.dma_start(w_scale[r:P:QUAD].bitcast(I32), scale_rows[r].bitcast(I32))
         w_codes = keep.tile([P, E * PASSES, N * PACK], U8, align_bytes=64)
         words = w_words.rearrange("e a p n r -> p (e a) (n r)")
-        nc.sync.dma_start(w_codes[:].bitcast(I32), words.bitcast(I32))
+        for lo in range(0, E * PASSES, W_PART):
+            nc.sync.dma_start(w_codes[:, lo : lo + W_PART].bitcast(I32), words[:, lo : lo + W_PART].bitcast(I32))
         bias = keep.tile([N, E], F32)
         nc.sync.dma_start(bias[:], b)
         token_slots = []
@@ -104,201 +113,199 @@ def tile_moe_pre_lin_silu_kernel(
         gate_banks = []
         for j in range(S // CELL):
             bank = psum.tile([P, CELL], F32, tag=f"bank{j}", name=f"gate_bank{j}")
-            for c in range(CELL // P):
-                col = j * CELL // P + c
-                nc.tensor.transpose(
-                    bank[:, c * P : (c + 1) * P], gate_cols[:, col : col + 1].to_broadcast([P, P]), identity[:]
-                )
+            for lo in range(0, CELL, P):
+                c = (j * CELL + lo) // P
+                nc.tensor.transpose(bank[:, lo : lo + P], gate_cols[:, c : c + 1].to_broadcast([P, P]), identity[:])
             gate_banks.append(bank)
 
         codes = [keep.tile([P, S], U32, align_bytes=64, name=f"codes{a}") for a in range(PASSES)]
         scale_of = {}
         sums_of = {}
+        result_banks = {}
 
-        def gather(engine, a, lo, hi, raw, rows=range(PACK)):
+        def staging(n, width):
+            return keep.tile([P, PACK, width], F32, align_bytes=64, tag=f"staging{n}", name=f"staging{n}")
+
+        def picked(a, r, lo, hi):
+            return planes[a * PACK + r][:].indirect(slot_tokens[:, lo // LIST : hi // LIST])
+
+        def vector_gather(a, lo, hi, raw, rows=range(PACK)):
             for r in rows:
-                picked = planes[a * PACK + r][:].indirect(slot_tokens[:, lo // LIST : hi // LIST])
-                if engine is nc.vector:
-                    nc.vector.tensor_copy(raw[:, r], picked)
-                else:
-                    nc.scalar.activation(raw[:, r], picked, COPY)
+                nc.vector.tensor_copy(raw[:, r], picked(a, r, lo, hi))
             return raw
 
-        def staging(tag, lo, hi):
-            return keep.tile([P, PACK, hi - lo], F32, align_bytes=64, tag=tag, name=tag)
+        def scalar_gather(a, lo, hi, raw, rows=range(PACK)):
+            for r in rows:
+                nc.scalar.activation(raw[:, r], picked(a, r, lo, hi), COPY)
+            return raw
 
-        def weave(engine, woven, raw, weights, run):
-            width = weights.shape[1]
-            engine.tensor_tensor(
-                woven.rearrange("p (c i) r -> p c r i", i=run),
-                raw.rearrange("p r (c i) -> p c r i", i=run),
-                weights.rearrange("p (c i) -> p c i", i=run).unsqueeze(2).to_broadcast([P, width // run, PACK, run]),
+        def vector_weave(woven, raw, lo):
+            width = raw.shape[2]
+            weights = gate_banks[lo // CELL][:, lo % CELL : lo % CELL + width].rearrange("p (c i) -> p c i", i=PAIR)
+            nc.vector.tensor_tensor(
+                woven.rearrange("p (c i) r -> p c r i", i=PAIR),
+                raw.rearrange("p r (c i) -> p c r i", i=PAIR),
+                weights.unsqueeze(2).to_broadcast([P, width // PAIR, PACK, PAIR]),
                 MULT,
             )
-
-        def multiply(e):
-            j, col = divmod(e * C, CELL)
-            if e == E - 1:
-                sums_of[e] = psum.tile([N, C], F32, tag="bank0", name="last_sums")[:]
-            elif col == 0:
-                bank = psum.tile([N, CELL], F32, tag=f"bank{j}", name=f"sums{j}")
-                sums_of[e], sums_of[e + 1] = bank[:, :C], bank[:, C:]
-            for a in range(PASSES):
-                g = e * PASSES + a
-                nc.tensor.matmul_mx(
-                    out=sums_of[e],
-                    lhsT=w_codes[:, g, :].bitcast(FP8X4),
-                    lhsT_scale=w_scale[4 * (g % 4) :, g // 4, :],
-                    rhs=codes[a][:, e * C : (e + 1) * C].bitcast(FP8X4),
-                    rhs_scale=scale_of[a, e],
-                    start=(a == 0),
-                    stop=(a == PASSES - 1),
-                )
-
-        def quantise(a, lo, hi, woven, scales):
-            nc.vector.quantize_mx(
-                out=codes[a][:, lo:hi].bitcast(FP8X4), scales=scales, in_=woven.rearrange("p c r -> p (c r)")
-            )
-            for e in range(lo // C, hi // C):
-                scale_of[a, e] = scales[:, e * C - lo : (e + 1) * C - lo]
-                if (1 - a, e) in scale_of:
-                    multiply(e)
-
-        def vector_cells(cells):
-            woven = keep.tile([P, len(cells) * CELL, PACK], BF16, align_bytes=64, tag="woven_v")
-            for n, (lo, raw) in enumerate(cells):
-                weave(nc.vector, woven[:, n * CELL : (n + 1) * CELL], raw, gate_banks[lo // CELL][:], 2)
-            return woven
-
-        def batch(tag, pieces):
-            scales = keep.tile([P, sum(hi - lo for a, lo, hi, woven in pieces)], U8, align_bytes=64, tag=tag, name=tag)
-            col = 0
-            for a, lo, hi, woven in pieces:
-                quantise(a, lo, hi, woven, scales[:, col : col + hi - lo])
-                col = col + hi - lo
 
         def gpsimd_weave(woven, raw, weights):
             nc.gpsimd.tensor_tensor(
                 woven, raw.rearrange("p r c -> p c r"), weights.unsqueeze(2).to_broadcast(woven.shape), MULT
             )
 
-        def turn_tile(width):
-            return keep.tile([P, width, PACK], BF16, align_bytes=64, tag="woven_g", name="turn")
+        def woven_tile(owner, width):
+            return keep.tile([P, width, PACK], BF16, align_bytes=64, tag=f"woven_{owner}", name=f"woven_{owner}")
 
-        v1 = staging("raw0", 0, 768)
+        def vector_cells(cells):
+            woven = woven_tile("vector", len(cells) * CELL)
+            for n, (lo, raw) in enumerate(cells):
+                vector_weave(woven[:, n * CELL : (n + 1) * CELL], raw, lo)
+            return woven
+
+        def multiply(lo, hi, sums):
+            for a in range(PASSES):
+                matrix = lo // C * PASSES + a
+                first, scales = scale_of[a, lo // P]
+                nc.tensor.matmul_mx(
+                    out=sums,
+                    lhsT=w_codes[:, matrix, :].bitcast(FP8X4),
+                    lhsT_scale=w_scale[:, matrix, :],
+                    rhs=codes[a][:, lo:hi].bitcast(FP8X4),
+                    rhs_scale=scales[:, lo - first : hi - first],
+                    start=(a == 0),
+                    stop=(a == PASSES - 1),
+                )
+            sums_of[lo] = (hi, sums)
+
+        def quantise(a, lo, hi, woven, scales):
+            nc.vector.quantize_mx(
+                out=codes[a][:, lo:hi].bitcast(FP8X4), scales=scales, in_=woven.rearrange("p c r -> p (c r)")
+            )
+            for block in range(lo // P, hi // P):
+                scale_of[a, block] = (lo, scales)
+            for first in range(lo, hi, C):
+                if (1 - a, first // P) not in scale_of:
+                    continue
+                if first >= S - C:
+                    half = psum.tile([N, P], F32, tag=f"bank{(first - (S - C)) // P}", name="half")
+                    multiply(first, hi, half[:])
+                else:
+                    j, col = divmod(first, CELL)
+                    if col == 0:
+                        result_banks[j] = psum.tile([N, CELL], F32, tag=f"bank{j}", name=f"sums{j}")
+                    multiply(first, first + C, result_banks[j][:, col : col + C])
+
+        def batch_scales(turn, width):
+            return keep.tile([P, width], U8, align_bytes=64, tag=f"gate{turn}", name=f"scales{turn}")
+
+        def batch(turn, pieces):
+            scales = batch_scales(turn, sum(hi - lo for a, lo, hi, woven in pieces))
+            col = 0
+            for a, lo, hi, woven in pieces:
+                quantise(a, lo, hi, woven, scales[:, col : col + hi - lo])
+                col = col + hi - lo
+
+        v1 = staging(0, FUSED)
         for r in range(PACK):
-            for lo, hi in ((0, 256), (256, 768)) if r == 0 else ((0, 768),):
-                picked = planes[r][:].indirect(slot_tokens[:, lo // LIST : hi // LIST])
-                nc.vector.tensor_tensor(v1[:, r, lo:hi], picked, gate1[:, lo:hi], MULT)
-        s1 = gather(nc.scalar, 0, 768, 1792, staging("raw1", 768, 1792))
-        v2 = gather(nc.vector, 1, 0, 512, staging("raw4", 0, 512))
-        v3 = gather(nc.vector, 1, 1536, 2560, staging("raw3", 1536, 2560))
-        s2 = gather(nc.scalar, 1, 512, 1536, staging("raw2", 512, 1536))
-        s3 = gather(nc.scalar, 0, 1792, 2560, staging("rows", 1792, 2560))
-        turn = turn_tile(1792)
-        nc.gpsimd.tensor_scalar(turn[:, :768], v1[:].rearrange("p r c -> p c r"), 1.0, 0.0, MULT, ADD)
-        gpsimd_weave(turn[:, 768:], s1[:], gate2[:])
+            for lo, hi in ((0, FIRST_GATE), (FIRST_GATE, FUSED)) if r == 0 else ((0, FUSED),):
+                nc.vector.tensor_tensor(v1[:, r, lo:hi], picked(0, r, lo, hi), fused_gate[:, lo:hi], MULT)
+        s1 = scalar_gather(0, FUSED, SECOND, staging(1, RUN))
+        v2 = vector_gather(1, 0, B1, staging(4, CELL))
+        v3 = vector_gather(1, B3, B5, staging(3, RUN))
+        s2 = scalar_gather(1, B1, B3, staging(2, RUN))
+        s3 = scalar_gather(0, SECOND, B5, staging(5, B5 - SECOND))
+        turn = woven_tile("gpsimd", SECOND)
+        nc.gpsimd.tensor_scalar(turn[:, :FUSED], v1[:].rearrange("p r c -> p c r"), 1.0, 0.0, MULT, ADD)
+        gpsimd_weave(turn[:, FUSED:], s1[:], gate1[:])
         woven = vector_cells([(0, v2[:])])
-        s4 = gather(nc.scalar, 0, 2560, 3584, staging("raw4", 2560, 3584))
+        s4 = scalar_gather(0, B5, B7, staging(4, RUN))
         batch(
-            "gate2",
+            1,
             [
-                (1, 0, 512, woven[:]),
-                (0, 0, 1024, turn[:, :1024]),
-                (0, 1024, 1536, turn[:, 1024:1536]),
-                (0, 1536, 1792, turn[:, 1536:]),
+                (1, 0, B1, woven[:]),
+                (0, 0, RUN, turn[:, :RUN]),
+                (0, RUN, B3, turn[:, RUN:B3]),
+                (0, B3, SECOND, turn[:, B3:]),
             ],
         )
 
-        turn = turn_tile(1280)
-        gpsimd_weave(turn[:, :1024], v3[:], gate3[:])
-        gpsimd_weave(turn[:, 1024:], s3[:, :, :C], gate3[:, C:CELL])
-        v4 = staging("raw1", 3584, 4096)
-        gather(nc.vector, 0, 3584, 4096, v4, [1, 2, 3])
-        gather(nc.scalar, 0, 3584, 4096, v4, [0])
+        turn = woven_tile("gpsimd", RUN + B4 - SECOND)
+        gpsimd_weave(turn[:, :RUN], v3[:], gate2[:])
+        split = B4 - SECOND - SECOND_SHARE
+        gpsimd_weave(turn[:, RUN : RUN + split], s3[:, :, :split], gate2[:, SECOND - B3 : SECOND - B3 + split])
+        v4 = staging(1, CELL)
+        vector_gather(0, B7 + SCALAR_SHARE, S, v4[:, :, SCALAR_SHARE:], [1])
+        vector_gather(0, B7, S, v4, range(2, PACK))
+        scalar_gather(0, B7, S, v4, [0])
+        scalar_gather(0, B7, B7 + SCALAR_SHARE, v4[:, :, :SCALAR_SHARE], [1])
         woven = vector_cells(
             [
-                (512, s2[:, :, :CELL]),
-                (1024, s2[:, :, CELL:]),
-                (2048, s3[:, :, C:]),
-                (2560, s4[:, :, :CELL]),
-                (3072, s4[:, :, CELL:]),
+                (B1, s2[:, :, :CELL]),
+                (B1 + CELL, s2[:, :, CELL:]),
+                (B4, s3[:, :, B4 - SECOND :]),
+                (B5, s4[:, :, :CELL]),
+                (B6, s4[:, :, CELL:]),
             ]
         )
-        s5 = gather(nc.scalar, 1, 2560, 3584, staging("raw2", 2560, 3584))
-        s6 = staging("rows", 3584, 4096)
-        gather(nc.scalar, 1, 3584, 3840, s6[:, :, :C])
-        gather(nc.scalar, 1, 3840, 4096, s6[:, :, C:])
+        vector_weave(turn[:, RUN + split :], s3[:, :, split : B4 - SECOND], SECOND + split)
+        s5 = scalar_gather(1, B5, B7, staging(2, RUN))
+        s6 = staging(5, CELL)
+        scalar_gather(1, B7, B7 + C, s6[:, :, :C])
+        scalar_gather(1, B7 + C, S, s6[:, :, C:])
         batch(
-            "gate3",
+            2,
             [
-                (1, 512, 1536, woven[:, :1024]),
-                (0, 2048, 3072, woven[:, 1024:2048]),
-                (0, 3072, 3584, woven[:, 2048:]),
-                (0, 1792, 2048, turn[:, 1024:]),
-                (1, 1536, 2560, turn[:, :1024]),
+                (1, B1, B3, woven[:, :RUN]),
+                (0, B4, B6, woven[:, RUN : 2 * RUN]),
+                (0, B6, B7, woven[:, 2 * RUN :]),
+                (0, SECOND, B4, turn[:, RUN:]),
+                (1, B3, B5, turn[:, :RUN]),
             ],
         )
 
         y = keep.tile([N, S], F32, tag=f"plane{PASSES * PACK - 1}")
 
-        def activate(e):
-            nc.scalar.activation(y[:, e * C : (e + 1) * C], sums_of[e], SILU, bias=bias[:, e : e + 1])
+        def activate(lo):
+            hi, sums = sums_of[lo]
+            nc.scalar.activation(y[:, lo:hi], sums, SILU, bias=bias[:, lo // C : lo // C + 1])
 
-        for e in range(E - 6):
-            activate(e)
-        turn = turn_tile(CELL)
-        gpsimd_weave(turn[:, 64:], v4[:, :, 64:], gate4[:])
-        weave(nc.vector, turn[:, :64], v4[:, :, :64], gate_banks[7][:, :64], 2)
-        woven = keep.tile([P, 3 * CELL, PACK], BF16, align_bytes=64, tag="woven_v")
-        scales = keep.tile([P, 4 * CELL], U8, align_bytes=64, tag="gate4")
-        for n in range(2):
-            weave(nc.vector, woven[:, n * CELL : (n + 1) * CELL], s5[:, :, n * CELL : (n + 1) * CELL], gate_banks[5 + n][:], 2)
-        weave(nc.vector, woven[:, 1024:1280], s6[:, :, :C], gate_banks[7][:, :C], 2)
-        quantise(1, 2560, 3072, woven[:, :512], scales[:, :512])
-        quantise(1, 3072, 3584, woven[:, 512:1024], scales[:, 512:1024])
-        quantise(0, 3584, 4096, turn[:], scales[:, 1024:1536])
-        weave(nc.vector, woven[:, 1280:], s6[:, :, C:], gate_banks[7][:, C:], 2)
-        quantise(1, 3584, 3840, woven[:, 1024:1280], scales[:, 1536:1792])
-        quantise(1, 3840, 4096, woven[:, 1280:], scales[:, 1792:])
+        for lo in range(0, B5, C):
+            activate(lo)
 
-        for e in range(E - 6, E):
-            activate(e)
+        turn = woven_tile("gpsimd", CELL)
+        gpsimd_weave(turn[:, LAST_SHARE:], v4[:, :, LAST_SHARE:], gate3[:])
+        vector_weave(turn[:, :LAST_SHARE], v4[:, :, :LAST_SHARE], B7)
+        woven = woven_tile("vector", S - B5)
+        scales = batch_scales(3, S - B5 + CELL)
+        for lo in (B5, B6):
+            vector_weave(woven[:, lo - B5 : lo - B5 + CELL], s5[:, :, lo - B5 : lo - B5 + CELL], lo)
+        vector_weave(woven[:, RUN : RUN + C], s6[:, :, :C], B7)
+        for lo in (B5, B6):
+            quantise(1, lo, lo + CELL, woven[:, lo - B5 : lo - B5 + CELL], scales[:, lo - B5 : lo - B5 + CELL])
+        quantise(0, B7, S, turn[:], scales[:, RUN : RUN + CELL])
+        vector_weave(woven[:, RUN + C :], s6[:, :, C:], B7 + C)
+        for lo, hi in ((B7, S - C), (S - C, S - P), (S - P, S)):
+            quantise(1, lo, hi, woven[:, lo - B5 : hi - B5], scales[:, lo - B5 + CELL : hi - B5 + CELL])
 
-        def result(j, lo, hi):
-            return y[:].indirect(token_slots[j][:, lo // LIST : hi // LIST])
+        for lo in [*range(B5, S, C), S - P]:
+            activate(lo)
 
-        fetched = keep.tile([N, TOP - 1, T], F32, align_bytes=64, tag="raw1")
-        sums = keep.tile([N, TOP, T], F32, align_bytes=64, tag="raw2")
-        own, narrow, wide = slice(0, 256), slice(256, 512), slice(512, T)
+        def result(j, part):
+            return y[:].indirect(token_slots[j][:, part.start // LIST : part.stop // LIST])
+
+        fetched = keep.tile([N, TOP - 1, T], F32, align_bytes=64, tag="staging1")
+        totals = keep.tile([N, TOP, T], F32, align_bytes=64, tag="staging2")
         for j in range(TOP - 1):
-            for part in (narrow, wide) if j == 0 else (wide, narrow):
-                nc.scalar.activation(fetched[:, j, part], result(j, part.start, part.stop), COPY)
-
-        def own_step(j):
-            picked = result(j, own.start, own.stop)
-            if j == 0:
-                nc.vector.tensor_copy(sums[:, 0, own], picked)
-            else:
-                nc.vector.tensor_tensor(sums[:, j, own], picked, sums[:, j - 1, own], ADD)
-
-        def shared_step(j, part):
-            if j == 0:
-                picked = result(TOP - 1, part.start, part.stop)
-                nc.vector.tensor_tensor(sums[:, 0, part], picked, fetched[:, 0, part], ADD)
-            else:
-                nc.vector.tensor_tensor(sums[:, j, part], sums[:, j - 1, part], fetched[:, j, part], ADD)
-
-        own_step(0)
-        shared_step(0, narrow)
-        own_step(1)
-        shared_step(0, wide)
-        own_step(2)
-        shared_step(1, wide)
-        own_step(3)
-        nc.sync.dma_start(out[:, own], sums[:, TOP - 1, own])
-        shared_step(1, narrow)
-        shared_step(2, wide)
-        nc.sync.dma_start(out[:, wide], sums[:, TOP - 2, wide])
-        shared_step(2, narrow)
-        nc.sync.dma_start(out[:, narrow], sums[:, TOP - 2, narrow])
+            for part in (NARROW, MIDDLE, WIDE) if j == 0 else (WIDE, MIDDLE, NARROW):
+                nc.scalar.activation(fetched[:, j, part], result(j, part), COPY)
+        nc.vector.tensor_copy(totals[:, 0, OWN], result(0, OWN))
+        for j, part in enumerate((NARROW, MIDDLE, WIDE), start=1):
+            nc.vector.tensor_tensor(totals[:, 0, part], result(TOP - 1, part), fetched[:, 0, part], ADD)
+            nc.vector.tensor_tensor(totals[:, j, OWN], result(j, OWN), totals[:, j - 1, OWN], ADD)
+        nc.sync.dma_start(out[:, OWN], totals[:, TOP - 1, OWN])
+        for j in range(1, TOP - 1):
+            for part in (WIDE, MIDDLE, NARROW):
+                nc.vector.tensor_tensor(totals[:, j, part], totals[:, j - 1, part], fetched[:, j, part], ADD)
+                if j == TOP - 2:
+                    nc.sync.dma_start(out[:, part], totals[:, j, part])

@@ -37,7 +37,6 @@ B1, B3, B4, B5, B6, B7 = (j * CELL for j in (1, 3, 4, 5, 6, 7))
 FUSED = 3 * C
 FIRST_GATE = C
 SECOND = FUSED + RUN
-SECOND_SHARE, LAST_SHARE = 32, 64
 SCALAR_SHARE = 128
 OWN, WIDE, MIDDLE, NARROW = slice(0, 288), slice(288, 672), slice(672, 896), slice(896, T)
 
@@ -90,7 +89,7 @@ def tile_moe_pre_lin_silu_kernel(
         nc.sync.dma_start(gate_rows[:], gate[: P * P // S].rearrange("k (c q) -> (k c) q", q=P))
         gate1 = load_turn_gate(1, FUSED, SECOND)
         gate2 = load_turn_gate(2, B3, B5)
-        gate3 = load_turn_gate(3, B7 + LAST_SHARE, S)
+        gate3 = load_turn_gate(3, B7, S)
         scale_rows = w_scales.rearrange("e a (q r) n -> r q (e a) n", r=PACK)
         for r in range(PACK):
             nc.sync.dma_start(w_scale[r:P:QUAD].bitcast(I32), scale_rows[r].bitcast(I32))
@@ -150,8 +149,12 @@ def tile_moe_pre_lin_silu_kernel(
             )
 
         def gpsimd_weave(woven, raw, weights):
+            width = raw.shape[2]
             nc.gpsimd.tensor_tensor(
-                woven, raw.rearrange("p r c -> p c r"), weights.unsqueeze(2).to_broadcast(woven.shape), MULT
+                woven.rearrange("p (c i) r -> p c r i", i=PAIR),
+                raw.rearrange("p r (c i) -> p c r i", i=PAIR),
+                weights.rearrange("p (c i) -> p c i", i=PAIR).unsqueeze(2).to_broadcast([P, width // PAIR, PACK, PAIR]),
+                MULT,
             )
 
         def woven_tile(owner, width):
@@ -230,25 +233,21 @@ def tile_moe_pre_lin_silu_kernel(
             ],
         )
 
-        turn = woven_tile("gpsimd", RUN + B4 - SECOND)
+        turn = woven_tile("gpsimd", RUN + CELL)
         gpsimd_weave(turn[:, :RUN], v3[:], gate2[:])
-        split = B4 - SECOND - SECOND_SHARE
-        gpsimd_weave(turn[:, RUN : RUN + split], s3[:, :, :split], gate2[:, SECOND - B3 : SECOND - B3 + split])
+        gpsimd_weave(turn[:, RUN:], s3[:, :, :CELL], gate2[:, SECOND - B3 : SECOND - B3 + CELL])
         v4 = staging(1, CELL)
         vector_gather(0, B7 + SCALAR_SHARE, S, v4[:, :, SCALAR_SHARE:], [1])
         vector_gather(0, B7, S, v4, range(2, PACK))
         scalar_gather(0, B7, S, v4, [0])
         scalar_gather(0, B7, B7 + SCALAR_SHARE, v4[:, :, :SCALAR_SHARE], [1])
-        woven = vector_cells(
-            [
-                (B1, s2[:, :, :CELL]),
-                (B1 + CELL, s2[:, :, CELL:]),
-                (B4, s3[:, :, B4 - SECOND :]),
-                (B5, s4[:, :, :CELL]),
-                (B6, s4[:, :, CELL:]),
-            ]
-        )
-        vector_weave(turn[:, RUN + split :], s3[:, :, split : B4 - SECOND], SECOND + split)
+        woven = woven_tile("vector", 2 * RUN + C)
+        for n in range(2):
+            vector_weave(woven[:, n * CELL : (n + 1) * CELL], s2[:, :, n * CELL : (n + 1) * CELL], B1 + n * CELL)
+        vector_weave(woven[:, RUN : RUN + C], s3[:, :, CELL:], B5 - C)
+        for n in range(2):
+            lo = RUN + C + n * CELL
+            vector_weave(woven[:, lo : lo + CELL], s4[:, :, n * CELL : (n + 1) * CELL], B5 + n * CELL)
         s5 = scalar_gather(1, B5, B7, staging(2, RUN))
         s6 = staging(5, CELL)
         scalar_gather(1, B7, B7 + C, s6[:, :, :C])
@@ -257,9 +256,9 @@ def tile_moe_pre_lin_silu_kernel(
             2,
             [
                 (1, B1, B3, woven[:, :RUN]),
-                (0, B4, B6, woven[:, RUN : 2 * RUN]),
-                (0, B6, B7, woven[:, 2 * RUN :]),
-                (0, SECOND, B4, turn[:, RUN:]),
+                (0, B5 - C, B7 - C, woven[:, RUN : 2 * RUN]),
+                (0, B7 - C, B7, woven[:, 2 * RUN :]),
+                (0, SECOND, SECOND + CELL, turn[:, RUN:]),
                 (1, B3, B5, turn[:, :RUN]),
             ],
         )
@@ -274,8 +273,7 @@ def tile_moe_pre_lin_silu_kernel(
             activate(lo)
 
         turn = woven_tile("gpsimd", CELL)
-        gpsimd_weave(turn[:, LAST_SHARE:], v4[:, :, LAST_SHARE:], gate3[:])
-        vector_weave(turn[:, :LAST_SHARE], v4[:, :, :LAST_SHARE], B7)
+        gpsimd_weave(turn[:], v4[:], gate3[:])
         woven = woven_tile("vector", S - B5)
         scales = batch_scales(3, S - B5 + CELL)
         for lo in (B5, B6):

@@ -33,11 +33,9 @@ RUN = 2 * CELL
 PAIR = 2
 W_PART = 8
 
-B1, B3, B4, B5, B6, B7 = (j * CELL for j in (1, 3, 4, 5, 6, 7))
-FUSED = 3 * C
-FIRST_GATE = C
-SECOND = FUSED + RUN
-SCALAR_SHARE = 128
+B1, B2, B3, B4, B5, B6, B7 = (j * CELL for j in range(1, 8))
+LATE = B6 + C
+SUM_GROUPS = [(lo, lo + CELL) for lo in range(0, B7, CELL)] + [(B7, S - C), (S - C, S - P), (S - P, S)]
 OWN, WIDE, MIDDLE, NARROW = slice(0, 288), slice(288, 672), slice(672, 896), slice(896, T)
 
 
@@ -72,24 +70,26 @@ def tile_moe_pre_lin_silu_kernel(
             rows = xT[a * K_PASS : (a + 1) * K_PASS, :].rearrange("(p r) t -> p r t", r=PACK)
             nc.sync.dma_start(planes[i][:, :T], rows[:, r, :])
 
-        def load_turn_gate(turn, lo, hi):
-            tile = keep.tile([P, hi - lo], F32, align_bytes=64, tag=f"gate{turn}", name=f"gate{turn}")
-            nc.sync.dma_start(tile[:], gate[:P, lo:hi])
+        def load_gate(tag, cuts):
+            tile = keep.tile([P, cuts[-1] - cuts[0]], F32, align_bytes=64, tag=tag, name=tag)
+            for lo, hi in zip(cuts, cuts[1:]):
+                nc.sync.dma_start(tile[:, lo - cuts[0] : hi - cuts[0]], gate[:P, lo:hi])
             return tile
 
         slot_tokens = lists.tile([P, S // LIST], U16)
         nc.sync.dma_start(slot_tokens[:], offs)
-        load_plane(0)
-        fused_gate = keep.tile([P, FUSED], F32)
-        for lo, hi in ((0, FIRST_GATE), (FIRST_GATE, FUSED)):
-            nc.sync.dma_start(fused_gate[:, lo:hi], gate[:P, lo:hi])
-        for i in range(1, PASSES * PACK):
+        for i in range(PACK):
+            load_plane(i)
+        gate1 = load_gate("gate1", [0, B1])
+        for i in range(PACK, PACK + 2):
+            load_plane(i)
+        gate_s1 = load_gate("gate_s1", [B1, B3])
+        for i in range(PACK + 2, PASSES * PACK):
             load_plane(i)
         gate_rows = keep.tile([P, P], F32, align_bytes=64, tag="staging5")
         nc.sync.dma_start(gate_rows[:], gate[: P * P // S].rearrange("k (c q) -> (k c) q", q=P))
-        gate1 = load_turn_gate(1, FUSED, SECOND)
-        gate2 = load_turn_gate(2, B3, B5)
-        gate3 = load_turn_gate(3, B7, S)
+        gate2 = load_gate("gate2", [B3, B5, LATE])
+        gate3 = load_gate("gate3", [B6, B7])
         scale_rows = w_scales.rearrange("e a (q r) n -> r q (e a) n", r=PACK)
         for r in range(PACK):
             nc.sync.dma_start(w_scale[r:P:QUAD].bitcast(I32), scale_rows[r].bitcast(I32))
@@ -112,7 +112,7 @@ def tile_moe_pre_lin_silu_kernel(
         gate_banks = []
         for j in range(S // CELL):
             bank = psum.tile([P, CELL], F32, tag=f"bank{j}", name=f"gate_bank{j}")
-            for lo in range(0, CELL, P):
+            for lo in range(C if j in (0, 6) else 0, CELL, P):
                 c = (j * CELL + lo) // P
                 nc.tensor.transpose(bank[:, lo : lo + P], gate_cols[:, c : c + 1].to_broadcast([P, P]), identity[:])
             gate_banks.append(bank)
@@ -120,7 +120,6 @@ def tile_moe_pre_lin_silu_kernel(
         codes = [keep.tile([P, S], U32, align_bytes=64, name=f"codes{a}") for a in range(PASSES)]
         scale_of = {}
         sums_of = {}
-        result_banks = {}
 
         def staging(n, width):
             return keep.tile([P, PACK, width], F32, align_bytes=64, tag=f"staging{n}", name=f"staging{n}")
@@ -160,14 +159,16 @@ def tile_moe_pre_lin_silu_kernel(
         def woven_tile(owner, width):
             return keep.tile([P, width, PACK], BF16, align_bytes=64, tag=f"woven_{owner}", name=f"woven_{owner}")
 
-        def vector_cells(cells):
-            woven = woven_tile("vector", len(cells) * CELL)
-            for n, (lo, raw) in enumerate(cells):
-                vector_weave(woven[:, n * CELL : (n + 1) * CELL], raw, lo)
+        def vector_weaves(pieces):
+            woven = woven_tile("vector", sum(raw.shape[2] for lo, raw in pieces))
+            col = 0
+            for lo, raw in pieces:
+                vector_weave(woven[:, col : col + raw.shape[2]], raw, lo)
+                col = col + raw.shape[2]
             return woven
 
-        def multiply(lo, hi, sums):
-            for a in range(PASSES):
+        def multiply(lo, hi, sums, last):
+            for a in (1 - last, last):
                 matrix = lo // C * PASSES + a
                 first, scales = scale_of[a, lo // P]
                 nc.tensor.matmul_mx(
@@ -176,8 +177,8 @@ def tile_moe_pre_lin_silu_kernel(
                     lhsT_scale=w_scale[:, matrix, :],
                     rhs=codes[a][:, lo:hi].bitcast(FP8X4),
                     rhs_scale=scales[:, lo - first : hi - first],
-                    start=(a == 0),
-                    stop=(a == PASSES - 1),
+                    start=(a != last),
+                    stop=(a == last),
                 )
             sums_of[lo] = (hi, sums)
 
@@ -187,17 +188,14 @@ def tile_moe_pre_lin_silu_kernel(
             )
             for block in range(lo // P, hi // P):
                 scale_of[a, block] = (lo, scales)
-            for first in range(lo, hi, C):
-                if (1 - a, first // P) not in scale_of:
-                    continue
-                if first >= S - C:
-                    half = psum.tile([N, P], F32, tag=f"bank{(first - (S - C)) // P}", name="half")
-                    multiply(first, hi, half[:])
-                else:
-                    j, col = divmod(first, CELL)
-                    if col == 0:
-                        result_banks[j] = psum.tile([N, CELL], F32, tag=f"bank{j}", name=f"sums{j}")
-                    multiply(first, first + C, result_banks[j][:, col : col + C])
+            for first, end in SUM_GROUPS:
+                ready = all((n, block) in scale_of for n in range(PASSES) for block in range(first // P, end // P))
+                if ready and first not in sums_of:
+                    j = first // CELL if first < S - C else (first - (S - C)) // P
+                    bank = psum.tile([N, end - first], F32, tag=f"bank{j}", name=f"sums{first}")
+                    for start in range(first, end, C):
+                        stop = min(start + C, end)
+                        multiply(start, stop, bank[:, start - first : stop - first], a)
 
         def batch_scales(turn, width):
             return keep.tile([P, width], U8, align_bytes=64, tag=f"gate{turn}", name=f"scales{turn}")
@@ -209,59 +207,59 @@ def tile_moe_pre_lin_silu_kernel(
                 quantise(a, lo, hi, woven, scales[:, col : col + hi - lo])
                 col = col + hi - lo
 
-        v1 = staging(0, FUSED)
-        for r in range(PACK):
-            for lo, hi in ((0, FIRST_GATE), (FIRST_GATE, FUSED)) if r == 0 else ((0, FUSED),):
-                nc.vector.tensor_tensor(v1[:, r, lo:hi], picked(0, r, lo, hi), fused_gate[:, lo:hi], MULT)
-        s1 = scalar_gather(0, FUSED, SECOND, staging(1, RUN))
+        v1 = vector_gather(0, 0, B1, staging(0, CELL))
+        s1 = scalar_gather(0, B1, B3, staging(1, RUN))
         v2 = vector_gather(1, 0, B1, staging(4, CELL))
         v3 = vector_gather(1, B3, B5, staging(3, RUN))
         s2 = scalar_gather(1, B1, B3, staging(2, RUN))
-        s3 = scalar_gather(0, SECOND, B5, staging(5, B5 - SECOND))
-        turn = woven_tile("gpsimd", SECOND)
-        nc.gpsimd.tensor_scalar(turn[:, :FUSED], v1[:].rearrange("p r c -> p c r"), 1.0, 0.0, MULT, ADD)
-        gpsimd_weave(turn[:, FUSED:], s1[:], gate1[:])
-        woven = vector_cells([(0, v2[:])])
-        s4 = scalar_gather(0, B5, B7, staging(4, RUN))
+        s3 = scalar_gather(0, B3, B5, staging(5, RUN))
+        turn = woven_tile("gpsimd", B3 + C)
+        gpsimd_weave(turn[:, :B1], v1[:], gate1[:])
+        gpsimd_weave(turn[:, B1:B3], s1[:], gate_s1[:])
+        gpsimd_weave(turn[:, B3:], v2[:, :, :C], gate1[:, :C])
+        woven = vector_weaves([(C, v2[:, :, C:]), (B1, s2[:, :, :C])])
+        s4 = scalar_gather(0, B5, B7, staging(1, RUN))
         batch(
             1,
             [
-                (1, 0, B1, woven[:]),
-                (0, 0, RUN, turn[:, :RUN]),
-                (0, RUN, B3, turn[:, RUN:B3]),
-                (0, B3, SECOND, turn[:, B3:]),
+                (1, C, B1 + C, woven[:]),
+                (0, 0, B2, turn[:, :B2]),
+                (0, B2, B3, turn[:, B2:B3]),
+                (1, 0, C, turn[:, B3:]),
             ],
         )
 
-        turn = woven_tile("gpsimd", RUN + CELL)
-        gpsimd_weave(turn[:, :RUN], v3[:], gate2[:])
-        gpsimd_weave(turn[:, RUN:], s3[:, :, :CELL], gate2[:, SECOND - B3 : SECOND - B3 + CELL])
-        v4 = staging(1, CELL)
-        vector_gather(0, B7 + SCALAR_SHARE, S, v4[:, :, SCALAR_SHARE:], [1])
-        vector_gather(0, B7, S, v4, range(2, PACK))
-        scalar_gather(0, B7, S, v4, [0])
-        scalar_gather(0, B7, B7 + SCALAR_SHARE, v4[:, :, :SCALAR_SHARE], [1])
-        woven = woven_tile("vector", 2 * RUN + C)
-        for n in range(2):
-            vector_weave(woven[:, n * CELL : (n + 1) * CELL], s2[:, :, n * CELL : (n + 1) * CELL], B1 + n * CELL)
-        vector_weave(woven[:, RUN : RUN + C], s3[:, :, CELL:], B5 - C)
-        for n in range(2):
-            lo = RUN + C + n * CELL
-            vector_weave(woven[:, lo : lo + CELL], s4[:, :, n * CELL : (n + 1) * CELL], B5 + n * CELL)
-        s5 = scalar_gather(1, B5, B7, staging(2, RUN))
-        s6 = staging(5, CELL)
-        scalar_gather(1, B7, B7 + C, s6[:, :, :C])
-        scalar_gather(1, B7 + C, S, s6[:, :, C:])
+        turn = woven_tile("gpsimd", LATE - B3)
+        gpsimd_weave(turn[:, :RUN], v3[:], gate2[:, :RUN])
+        v4 = vector_gather(1, B5, LATE, staging(4, LATE - B5))
+        gpsimd_weave(turn[:, RUN:], v4[:], gate2[:, RUN:])
+        woven = vector_weaves(
+            [
+                (B1 + C, s2[:, :, C:CELL]),
+                (B2, s2[:, :, CELL:]),
+                (B3, s3[:, :, :CELL]),
+                (B4, s3[:, :, CELL:]),
+                (B5, s4[:, :, :CELL]),
+            ]
+        )
+        s5 = scalar_gather(1, LATE, S, staging(2, S - LATE))
+        s6 = scalar_gather(0, B7, S - C, staging(5, C))
         batch(
             2,
             [
-                (1, B1, B3, woven[:, :RUN]),
-                (0, B5 - C, B7 - C, woven[:, RUN : 2 * RUN]),
-                (0, B7 - C, B7, woven[:, 2 * RUN :]),
-                (0, SECOND, SECOND + CELL, turn[:, RUN:]),
+                (1, B1 + C, B2 + C, woven[:, :CELL]),
+                (1, B2 + C, B3, woven[:, CELL : CELL + C]),
+                (0, B3, B5, woven[:, CELL + C : 3 * CELL + C]),
+                (0, B5, B6, woven[:, 3 * CELL + C :]),
                 (1, B3, B5, turn[:, :RUN]),
+                (1, B5, B6, turn[:, RUN : RUN + CELL]),
+                (1, B6, LATE, turn[:, RUN + CELL :]),
             ],
         )
+
+        s7 = staging(4, C)
+        vector_gather(0, S - C, S, s7, [0])
+        scalar_gather(0, S - C, S, s7, range(1, PACK))
 
         y = keep.tile([N, S], F32, tag=f"plane{PASSES * PACK - 1}")
 
@@ -269,24 +267,25 @@ def tile_moe_pre_lin_silu_kernel(
             hi, sums = sums_of[lo]
             nc.scalar.activation(y[:, lo:hi], sums, SILU, bias=bias[:, lo // C : lo // C + 1])
 
-        for lo in range(0, B5, C):
+        for lo in range(0, B6, C):
             activate(lo)
 
         turn = woven_tile("gpsimd", CELL)
-        gpsimd_weave(turn[:], v4[:], gate3[:])
-        woven = woven_tile("vector", S - B5)
-        scales = batch_scales(3, S - B5 + CELL)
-        for lo in (B5, B6):
-            vector_weave(woven[:, lo - B5 : lo - B5 + CELL], s5[:, :, lo - B5 : lo - B5 + CELL], lo)
-        vector_weave(woven[:, RUN : RUN + C], s6[:, :, :C], B7)
-        for lo in (B5, B6):
-            quantise(1, lo, lo + CELL, woven[:, lo - B5 : lo - B5 + CELL], scales[:, lo - B5 : lo - B5 + CELL])
-        quantise(0, B7, S, turn[:], scales[:, RUN : RUN + CELL])
-        vector_weave(woven[:, RUN + C :], s6[:, :, C:], B7 + C)
+        gpsimd_weave(turn[:], s4[:, :, CELL:], gate3[:])
+        woven = woven_tile("vector", S - LATE + CELL)
+        late, last = woven[:, : S - LATE], woven[:, S - LATE :]
+        scales = batch_scales(3, S - LATE + RUN)
+        vector_weave(late[:, :C], s5[:, :, :C], LATE)
+        vector_weave(late[:, C:], s5[:, :, C:], B7)
+        vector_weave(last[:, :C], s6[:], B7)
+        quantise(1, LATE, S - C, late[:, :CELL], scales[:, :CELL])
+        quantise(0, B6, B7, turn[:], scales[:, CELL:RUN])
+        quantise(1, S - C, S, late[:, CELL:], scales[:, RUN : RUN + C])
+        vector_weave(last[:, C:], s7[:], S - C)
         for lo, hi in ((B7, S - C), (S - C, S - P), (S - P, S)):
-            quantise(1, lo, hi, woven[:, lo - B5 : hi - B5], scales[:, lo - B5 + CELL : hi - B5 + CELL])
+            quantise(0, lo, hi, last[:, lo - B7 : hi - B7], scales[:, RUN + C + lo - B7 : RUN + C + hi - B7])
 
-        for lo in [*range(B5, S, C), S - P]:
+        for lo in [*range(B6, S, C), S - P]:
             activate(lo)
 
         def result(j, part):

@@ -31,6 +31,7 @@ BYTES = K * T * 4 + E * K * N + E * K * N // 32 + N * E * 4 + S * 4 + P * (S + T
 CELL = 512
 RUN = 2 * CELL
 PAIR = 2
+LINE = 4
 W_PART = 8
 
 B1, B2, B3, B4, B5, B6, B7 = (j * CELL for j in range(1, 8))
@@ -150,9 +151,9 @@ def tile_moe_pre_lin_silu_kernel(
         def gpsimd_weave(woven, raw, weights):
             width = raw.shape[2]
             nc.gpsimd.tensor_tensor(
-                woven.rearrange("p (c i) r -> p c r i", i=PAIR),
-                raw.rearrange("p r (c i) -> p c r i", i=PAIR),
-                weights.rearrange("p (c i) -> p c i", i=PAIR).unsqueeze(2).to_broadcast([P, width // PAIR, PACK, PAIR]),
+                woven.rearrange("p (c i) r -> p c r i", i=LINE),
+                raw.rearrange("p r (c i) -> p c r i", i=LINE),
+                weights.rearrange("p (c i) -> p c i", i=LINE).unsqueeze(2).to_broadcast([P, width // LINE, PACK, LINE]),
                 MULT,
             )
 

@@ -32,12 +32,20 @@ CELL = 512
 RUN = 2 * CELL
 PAIR = 2
 LINE = 4
-W_PART = 8
+STAGE = PACK * RUN * 4
+LAP = 64
 
-B1, B2, B3, B4, B5, B6, B7 = (j * CELL for j in range(1, 8))
-LATE = B6 + C
-SUM_GROUPS = [(lo, lo + CELL) for lo in range(0, B7, CELL)] + [(B7, S - C), (S - C, S - P), (S - P, S)]
-OWN, WIDE, MIDDLE, NARROW = slice(0, 288), slice(288, 672), slice(672, 896), slice(896, T)
+FIRST = 768
+G0_END = FIRST + RUN
+G1_END = 2 * RUN
+LATE0, LATE1 = S - 2 * C, S - 3 * C
+LATE_G = LATE1 + 384
+LONG_G = G0_END + G1_END
+LONG_V = LATE0 - G0_END + LATE1 - G1_END
+SHORT = PASSES * S - LONG_G - LONG_V
+HELP = 768
+W_CUTS = (0, 4, 8, 11, 14, 16)
+OWN, SEED, WIDE, MIDDLE, NARROW = slice(0, 256), slice(256, 512), slice(256, 640), slice(640, 896), slice(896, T)
 
 
 def tile_moe_pre_lin_silu_kernel(
@@ -47,9 +55,29 @@ def tile_moe_pre_lin_silu_kernel(
     with ExitStack() as ctx:
         lists = ctx.enter_context(tc.tile_pool(name="lists", bufs=1))
         keep = ctx.enter_context(tc.tile_pool(name="keep", bufs=1))
+        shared = ctx.enter_context(tc.tile_pool(name="shared", bufs=1))
         psum = ctx.enter_context(tc.psum_pool(name="psum", bufs=1))
 
-        planes = [keep.tile([P, RUN + LIST], F32, tag=f"plane{i}", name=f"plane{i}") for i in range(PASSES * PACK)]
+        def placed(name, shape, dtype, offset):
+            return shared.tile(shape, dtype, align_bytes=64, tag=name, name=name, offset=offset)
+
+        at_e = 0
+        at_a = at_e + STAGE
+        at_d = at_a + STAGE + LAP
+        at_c = at_d + STAGE
+        at_woven_v = at_c + STAGE + LAP
+        at_b = at_woven_v + LONG_V * PACK * 2
+        at_plane = at_b + STAGE
+        at_gate = at_plane + (RUN + LIST) * 4
+        at_gate2 = at_gate + G1_END * 4
+
+        last_plane = PACK - 1
+        planes = [
+            placed("plane_last", [P, RUN + LIST], F32, at_plane)
+            if i == last_plane
+            else keep.tile([P, RUN + LIST], F32, tag=f"plane{i}", name=f"plane{i}")
+            for i in range(PASSES * PACK)
+        ]
         w_scale = keep.tile([P, E * PASSES, N], U8, align_bytes=64)
         nc.vector.memset(w_scale[:].bitcast(I32), 0)
         ones = keep.tile([P, QUAD], F32)
@@ -71,33 +99,28 @@ def tile_moe_pre_lin_silu_kernel(
             rows = xT[a * K_PASS : (a + 1) * K_PASS, :].rearrange("(p r) t -> p r t", r=PACK)
             nc.sync.dma_start(planes[i][:, :T], rows[:, r, :])
 
-        def load_gate(tag, cuts):
-            tile = keep.tile([P, cuts[-1] - cuts[0]], F32, align_bytes=64, tag=tag, name=tag)
-            for lo, hi in zip(cuts, cuts[1:]):
-                nc.sync.dma_start(tile[:, lo - cuts[0] : hi - cuts[0]], gate[:P, lo:hi])
-            return tile
-
+        gate_long = placed("gate_long", [P, G1_END], F32, at_gate)
+        gate_late = placed("gate_late", [P, LATE_G - LATE1], F32, at_gate2)
         slot_tokens = lists.tile([P, S // LIST], U16)
         nc.sync.dma_start(slot_tokens[:], offs)
-        for i in range(PACK):
+        for i in range(3):
             load_plane(i)
-        gate1 = load_gate("gate1", [0, B1])
-        for i in range(PACK, PACK + 2):
+        nc.sync.dma_start(gate_long[:, :FIRST], gate[:P, :FIRST])
+        for i in range(3, PASSES * PACK):
             load_plane(i)
-        gate_s1 = load_gate("gate_s1", [B1, B3])
-        for i in range(PACK + 2, PASSES * PACK):
-            load_plane(i)
-        gate_rows = keep.tile([P, P], F32, align_bytes=64, tag="staging5")
+        nc.sync.dma_start(gate_long[:, FIRST:G0_END], gate[:P, FIRST:G0_END])
+        gate_rows = placed("gate_rows", [P, P], F32, at_a + LAP - P * 2)
         nc.sync.dma_start(gate_rows[:], gate[: P * P // S].rearrange("k (c q) -> (k c) q", q=P))
-        gate2 = load_gate("gate2", [B3, B5, LATE])
-        gate3 = load_gate("gate3", [B6, B7])
+        nc.sync.dma_start(gate_long[:, G0_END:], gate[:P, G0_END:G1_END])
+        nc.sync.dma_start(gate_late[:], gate[:P, LATE1:LATE_G])
         scale_rows = w_scales.rearrange("e a (q r) n -> r q (e a) n", r=PACK)
         for r in range(PACK):
             nc.sync.dma_start(w_scale[r:P:QUAD].bitcast(I32), scale_rows[r].bitcast(I32))
         w_codes = keep.tile([P, E * PASSES, N * PACK], U8, align_bytes=64)
         words = w_words.rearrange("e a p n r -> p (e a) (n r)")
-        for lo in range(0, E * PASSES, W_PART):
-            nc.sync.dma_start(w_codes[:, lo : lo + W_PART].bitcast(I32), words[:, lo : lo + W_PART].bitcast(I32))
+        for lo, hi in zip(W_CUTS, W_CUTS[1:]):
+            part = slice(lo * PASSES, hi * PASSES)
+            nc.sync.dma_start(w_codes[:, part].bitcast(I32), words[:, part].bitcast(I32))
         bias = keep.tile([N, E], F32)
         nc.sync.dma_start(bias[:], b)
         token_slots = []
@@ -106,24 +129,20 @@ def tile_moe_pre_lin_silu_kernel(
             nc.sync.dma_start(slots[:], pos)
             token_slots.append(slots)
 
-        turned = psum.tile([P, P], F32, tag=f"bank{S // CELL - 1}")
+        turned = psum.tile([P, P], F32, tag="bank0")
         nc.tensor.transpose(turned[:], gate_rows[:], identity[:])
         gate_cols = keep.tile([P, S // P], F32)
         nc.vector.tensor_copy(gate_cols[:], turned[:, : S // P])
-        gate_banks = []
-        for j in range(S // CELL):
+        gate_banks = {}
+        for j in [*range(G1_END // CELL, S // CELL), G0_END // CELL]:
             bank = psum.tile([P, CELL], F32, tag=f"bank{j}", name=f"gate_bank{j}")
-            for lo in range(C if j in (0, 6) else 0, CELL, P):
+            for lo in range(max(G0_END - j * CELL, 0), CELL, P):
                 c = (j * CELL + lo) // P
                 nc.tensor.transpose(bank[:, lo : lo + P], gate_cols[:, c : c + 1].to_broadcast([P, P]), identity[:])
-            gate_banks.append(bank)
+            gate_banks[j] = bank
 
-        codes = [keep.tile([P, S], U32, align_bytes=64, name=f"codes{a}") for a in range(PASSES)]
-        scale_of = {}
-        sums_of = {}
-
-        def staging(n, width):
-            return keep.tile([P, PACK, width], F32, align_bytes=64, tag=f"staging{n}", name=f"staging{n}")
+        def staging(name, width, offset):
+            return placed(name, [P, PACK, width], F32, offset)
 
         def picked(a, r, lo, hi):
             return planes[a * PACK + r][:].indirect(slot_tokens[:, lo // LIST : hi // LIST])
@@ -131,179 +150,165 @@ def tile_moe_pre_lin_silu_kernel(
         def vector_gather(a, lo, hi, raw, rows=range(PACK)):
             for r in rows:
                 nc.vector.tensor_copy(raw[:, r], picked(a, r, lo, hi))
-            return raw
 
         def scalar_gather(a, lo, hi, raw, rows=range(PACK)):
             for r in rows:
                 nc.scalar.activation(raw[:, r], picked(a, r, lo, hi), COPY)
-            return raw
 
         def vector_weave(woven, raw, lo):
-            width = raw.shape[2]
-            weights = gate_banks[lo // CELL][:, lo % CELL : lo % CELL + width].rearrange("p (c i) -> p c i", i=PAIR)
-            nc.vector.tensor_tensor(
-                woven.rearrange("p (c i) r -> p c r i", i=PAIR),
-                raw.rearrange("p r (c i) -> p c r i", i=PAIR),
-                weights.unsqueeze(2).to_broadcast([P, width // PAIR, PACK, PAIR]),
-                MULT,
-            )
+            hi = lo + raw.shape[2]
+            cuts = [lo, *range((lo // CELL + 1) * CELL, hi, CELL), hi]
+            for first, end in zip(cuts, cuts[1:]):
+                cols = slice(first - lo, end - lo)
+                weights = gate_banks[first // CELL][:, first % CELL : first % CELL + end - first]
+                nc.vector.tensor_tensor(
+                    woven[:, cols].rearrange("p (c i) r -> p c r i", i=PAIR),
+                    raw[:, :, cols].rearrange("p r (c i) -> p c r i", i=PAIR),
+                    weights.rearrange("p (c i) -> p c i", i=PAIR)
+                    .unsqueeze(2)
+                    .to_broadcast([P, (end - first) // PAIR, PACK, PAIR]),
+                    MULT,
+                )
 
         def gpsimd_weave(woven, raw, weights):
-            width = raw.shape[2]
+            rows, width = raw.shape[1:]
             nc.gpsimd.tensor_tensor(
                 woven.rearrange("p (c i) r -> p c r i", i=LINE),
                 raw.rearrange("p r (c i) -> p c r i", i=LINE),
-                weights.rearrange("p (c i) -> p c i", i=LINE).unsqueeze(2).to_broadcast([P, width // LINE, PACK, LINE]),
+                weights.rearrange("p (c i) -> p c i", i=LINE).unsqueeze(2).to_broadcast([P, width // LINE, rows, LINE]),
                 MULT,
             )
 
-        def woven_tile(owner, width):
-            return keep.tile([P, width, PACK], BF16, align_bytes=64, tag=f"woven_{owner}", name=f"woven_{owner}")
+        g0 = staging("g0", FIRST, at_a + LAP + STAGE - FIRST * PACK * 4)
+        g1 = staging("g1", RUN, at_b - LAP)
+        g2 = staging("g2", RUN, at_c)
+        v0 = staging("v0", RUN, at_d)
+        woven_g = keep.tile([P, LONG_G, PACK], BF16, align_bytes=64)
+        vector_gather(0, 0, FIRST, g0)
+        scalar_gather(0, FIRST, G0_END, g1, range(PACK - 1))
+        vector_gather(0, FIRST, G0_END, g1, [PACK - 1])
+        vector_gather(1, 0, RUN, g2)
+        scalar_gather(1, G1_END, G1_END + RUN, v0)
+        for half in (slice(0, PACK // 2), slice(PACK // 2, PACK)):
+            gpsimd_weave(woven_g[:, G1_END : G1_END + FIRST, half], g0[:, half], gate_long[:, :FIRST])
+        gpsimd_weave(woven_g[:, G1_END + FIRST :], g1[:], gate_long[:, FIRST:G0_END])
+        gpsimd_weave(woven_g[:, :RUN], g2[:], gate_long[:, :RUN])
+        v1 = staging("v1", RUN, at_e + LAP)
+        scalar_gather(0, G0_END, G0_END + RUN, v1)
+        g3 = staging("g3", RUN, at_a + LAP)
+        vector_gather(1, RUN, G1_END, g3, range(PACK - 1))
+        vector_gather(1, RUN, G1_END - HELP, g3[:, :, : RUN - HELP], [PACK - 1])
+        scalar_gather(1, G1_END - HELP, G1_END, g3[:, :, RUN - HELP :], [PACK - 1])
+        gpsimd_weave(woven_g[:, RUN:G1_END], g3[:], gate_long[:, RUN:])
+        woven_v = placed("woven_v", [P, LONG_V, PACK], BF16, at_woven_v)
+        woven_v0, woven_v1 = woven_v[:, : LATE0 - G0_END], woven_v[:, LATE0 - G0_END :]
+        vector_weave(woven_v1[:, :RUN], v0[:], G1_END)
+        vector_weave(woven_v0[:, :RUN], v1[:], G0_END)
+        v2 = staging("v2", RUN - C, at_b)
+        v3 = staging("v3", C, at_b + (RUN - C) * PACK * 4)
+        scalar_gather(0, G0_END + RUN, LATE0, v2)
+        scalar_gather(1, G1_END + RUN, LATE1, v3)
+        vector_weave(woven_v0[:, RUN:], v2[:], G0_END + RUN)
+        vector_weave(woven_v1[:, RUN:], v3[:], G1_END + RUN)
+        l0 = staging("l0", S - LATE1, at_c + LAP)
+        l1 = staging("l1", C, at_c + LAP + (S - LATE1) * PACK * 4)
+        l2 = staging("l2", C, at_c + LAP - C * PACK * 4)
+        scalar_gather(1, LATE1, S, l0)
+        scalar_gather(0, LATE0, S - C, l1)
+        scalar_gather(0, S - C, S, l2)
 
-        def vector_weaves(pieces):
-            woven = woven_tile("vector", sum(raw.shape[2] for lo, raw in pieces))
-            col = 0
-            for lo, raw in pieces:
-                vector_weave(woven[:, col : col + raw.shape[2]], raw, lo)
-                col = col + raw.shape[2]
-            return woven
+        spans = [(1, 0, G1_END), (0, 0, G0_END), (0, G0_END, LATE0), (1, G1_END, LATE1), (1, LATE1, S), (0, LATE0, S)]
+        column_of = {}
+        for a, lo, hi in spans:
+            for slot in range(lo, hi, P):
+                column_of[a, slot] = len(column_of) * P
+        codes = placed("codes", [P, PASSES * S], U32, at_e + LAP)
+        scale_of = {}
+        sums_of = {}
+        groups = [(lo, min(lo + CELL, LATE1), lo // CELL) for lo in range(0, LATE1, CELL)]
+        groups = groups + [(lo, hi, j) for j, (lo, hi) in enumerate(((LATE1, LATE0), (LATE0, S - C), (S - C, S - P), (S - P, S)))]
 
-        def multiply(lo, hi, sums, last):
-            for a in (1 - last, last):
+        def multiply(lo, hi, sums):
+            for n, a in enumerate(sorted(range(PASSES), key=lambda a: scale_of[column_of[a, lo]][0])):
                 matrix = lo // C * PASSES + a
-                first, scales = scale_of[a, lo // P]
+                col = column_of[a, lo]
+                order, first, scales = scale_of[col]
                 nc.tensor.matmul_mx(
                     out=sums,
                     lhsT=w_codes[:, matrix, :].bitcast(FP8X4),
                     lhsT_scale=w_scale[:, matrix, :],
-                    rhs=codes[a][:, lo:hi].bitcast(FP8X4),
-                    rhs_scale=scales[:, lo - first : hi - first],
-                    start=(a != last),
-                    stop=(a == last),
+                    rhs=codes[:, col : col + hi - lo].bitcast(FP8X4),
+                    rhs_scale=scales[:, col - first : col - first + hi - lo],
+                    start=(n == 0),
+                    stop=(n == PASSES - 1),
                 )
             sums_of[lo] = (hi, sums)
 
-        def quantise(a, lo, hi, woven, scales):
+        def quantise(woven, woven_first, scales, scales_first, lo, hi):
             nc.vector.quantize_mx(
-                out=codes[a][:, lo:hi].bitcast(FP8X4), scales=scales, in_=woven.rearrange("p c r -> p (c r)")
+                out=codes[:, lo:hi].bitcast(FP8X4),
+                scales=scales[:, lo - scales_first : hi - scales_first],
+                in_=woven[:, lo - woven_first : hi - woven_first].rearrange("p c r -> p (c r)"),
             )
-            for block in range(lo // P, hi // P):
-                scale_of[a, block] = (lo, scales)
-            for first, end in SUM_GROUPS:
-                ready = all((n, block) in scale_of for n in range(PASSES) for block in range(first // P, end // P))
+            for col in range(lo, hi, P):
+                scale_of[col] = (len(scale_of), scales_first, scales)
+            for first, end, j in groups:
+                ready = all(column_of[a, slot] in scale_of for a in range(PASSES) for slot in range(first, end, P))
                 if ready and first not in sums_of:
-                    j = first // CELL if first < S - C else (first - (S - C)) // P
                     bank = psum.tile([N, end - first], F32, tag=f"bank{j}", name=f"sums{first}")
                     for start in range(first, end, C):
                         stop = min(start + C, end)
-                        multiply(start, stop, bank[:, start - first : stop - first], a)
+                        multiply(start, stop, bank[:, start - first : stop - first])
 
-        def batch_scales(turn, width):
-            return keep.tile([P, width], U8, align_bytes=64, tag=f"gate{turn}", name=f"scales{turn}")
+        scales_long = placed("scales_long", [P, LONG_G + LONG_V], U8, at_gate)
+        for lo, hi in ((2 * RUN, 3 * RUN), (0, RUN), (3 * RUN, 3 * RUN + CELL), (3 * RUN + CELL, LONG_G)):
+            quantise(woven_g, 0, scales_long, 0, lo, hi)
+        quantise(woven_v, LONG_G, scales_long, 0, LONG_G, LONG_G + RUN)
+        quantise(woven_g, 0, scales_long, 0, RUN, 2 * RUN)
+        for lo in range(LONG_G + RUN, LONG_G + LONG_V, RUN):
+            quantise(woven_v, LONG_G, scales_long, 0, lo, lo + RUN)
 
-        def batch(turn, pieces):
-            scales = batch_scales(turn, sum(hi - lo for a, lo, hi, woven in pieces))
-            col = 0
-            for a, lo, hi, woven in pieces:
-                quantise(a, lo, hi, woven, scales[:, col : col + hi - lo])
-                col = col + hi - lo
-
-        v1 = vector_gather(0, 0, B1, staging(0, CELL))
-        s1 = scalar_gather(0, B1, B3, staging(1, RUN))
-        v2 = vector_gather(1, 0, B1, staging(4, CELL))
-        v3 = vector_gather(1, B3, B5, staging(3, RUN))
-        s2 = scalar_gather(1, B1, B3, staging(2, RUN))
-        s3 = scalar_gather(0, B3, B5, staging(5, RUN))
-        turn = woven_tile("gpsimd", B3 + C)
-        gpsimd_weave(turn[:, :B1], v1[:], gate1[:])
-        gpsimd_weave(turn[:, B1:B3], s1[:], gate_s1[:])
-        gpsimd_weave(turn[:, B3:], v2[:, :, :C], gate1[:, :C])
-        woven = vector_weaves([(C, v2[:, :, C:]), (B1, s2[:, :, :C])])
-        s4 = scalar_gather(0, B5, B7, staging(1, RUN))
-        batch(
-            1,
-            [
-                (1, C, B1 + C, woven[:]),
-                (0, 0, B2, turn[:, :B2]),
-                (0, B2, B3, turn[:, B2:B3]),
-                (1, 0, C, turn[:, B3:]),
-            ],
-        )
-
-        turn = woven_tile("gpsimd", LATE - B3)
-        gpsimd_weave(turn[:, :RUN], v3[:], gate2[:, :RUN])
-        v4 = vector_gather(1, B5, LATE, staging(4, LATE - B5))
-        gpsimd_weave(turn[:, RUN:], v4[:], gate2[:, RUN:])
-        woven = vector_weaves(
-            [
-                (B1 + C, s2[:, :, C:CELL]),
-                (B2, s2[:, :, CELL:]),
-                (B3, s3[:, :, :CELL]),
-                (B4, s3[:, :, CELL:]),
-                (B5, s4[:, :, :CELL]),
-            ]
-        )
-        s5 = scalar_gather(1, LATE, S, staging(2, S - LATE))
-        s6 = scalar_gather(0, B7, S - C, staging(5, C))
-        batch(
-            2,
-            [
-                (1, B1 + C, B2 + C, woven[:, :CELL]),
-                (1, B2 + C, B3, woven[:, CELL : CELL + C]),
-                (0, B3, B5, woven[:, CELL + C : 3 * CELL + C]),
-                (0, B5, B6, woven[:, 3 * CELL + C :]),
-                (1, B3, B5, turn[:, :RUN]),
-                (1, B5, B6, turn[:, RUN : RUN + CELL]),
-                (1, B6, LATE, turn[:, RUN + CELL :]),
-            ],
-        )
-
-        s7 = staging(4, C)
-        vector_gather(0, S - C, S, s7, [0])
-        scalar_gather(0, S - C, S, s7, range(1, PACK))
-
-        y = keep.tile([N, S], F32, tag=f"plane{PASSES * PACK - 1}")
+        y = placed("y", [N, S], F32, at_plane + RUN * 4 - S * 4)
 
         def activate(lo):
             hi, sums = sums_of[lo]
             nc.scalar.activation(y[:, lo:hi], sums, SILU, bias=bias[:, lo // C : lo // C + 1])
 
-        for lo in range(0, B6, C):
+        for lo in range(0, LATE1, C):
             activate(lo)
 
-        turn = woven_tile("gpsimd", CELL)
-        gpsimd_weave(turn[:], s4[:, :, CELL:], gate3[:])
-        woven = woven_tile("vector", S - LATE + CELL)
-        late, last = woven[:, : S - LATE], woven[:, S - LATE :]
-        scales = batch_scales(3, S - LATE + RUN)
-        vector_weave(late[:, :C], s5[:, :, :C], LATE)
-        vector_weave(late[:, C:], s5[:, :, C:], B7)
-        vector_weave(last[:, :C], s6[:], B7)
-        quantise(1, LATE, S - C, late[:, :CELL], scales[:, :CELL])
-        quantise(0, B6, B7, turn[:], scales[:, CELL:RUN])
-        quantise(1, S - C, S, late[:, CELL:], scales[:, RUN : RUN + C])
-        vector_weave(last[:, C:], s7[:], S - C)
-        for lo, hi in ((B7, S - C), (S - C, S - P), (S - P, S)):
-            quantise(0, lo, hi, last[:, lo - B7 : hi - B7], scales[:, RUN + C + lo - B7 : RUN + C + hi - B7])
-
-        for lo in [*range(B6, S, C), S - P]:
+        woven_l = placed("woven_l", [P, SHORT, PACK], BF16, at_woven_v)
+        late1, late0 = woven_l[:, : S - LATE1], woven_l[:, S - LATE1 :]
+        gpsimd_weave(late1[:, : LATE_G - LATE1], l0[:, :, : LATE_G - LATE1], gate_late[:])
+        vector_weave(late1[:, LATE_G - LATE1 :], l0[:, :, LATE_G - LATE1 :], LATE_G)
+        vector_weave(late0[:, :C], l1[:], LATE0)
+        vector_weave(late0[:, C:], l2[:], S - C)
+        scales_late = placed("scales_late", [P, SHORT], U8, at_gate2)
+        for a, lo, hi in ((1, LATE1, S - C), (0, LATE0, S - C), (1, S - C, S), (0, S - C, S - P), (0, S - P, S)):
+            col = column_of[a, lo]
+            quantise(woven_l, LONG_G + LONG_V, scales_late, LONG_G + LONG_V, col, col + hi - lo)
+        for lo in [*range(LATE1, S, C), S - P]:
             activate(lo)
 
         def result(j, part):
             return y[:].indirect(token_slots[j][:, part.start // LIST : part.stop // LIST])
 
-        fetched = keep.tile([N, TOP - 1, T], F32, align_bytes=64, tag="staging1")
-        totals = keep.tile([N, TOP, T], F32, align_bytes=64, tag="staging2")
-        for j in range(TOP - 1):
-            for part in (NARROW, MIDDLE, WIDE) if j == 0 else (WIDE, MIDDLE, NARROW):
+        fetched = keep.tile([N, TOP - 1, T], F32, align_bytes=64)
+        totals = keep.tile([N, TOP, T], F32, align_bytes=64)
+        rest = slice(SEED.stop, T)
+        shared_tokens = slice(OWN.stop, T)
+        for j, parts in enumerate(((SEED, rest), (shared_tokens,), (WIDE, MIDDLE, NARROW))):
+            for part in parts:
                 nc.scalar.activation(fetched[:, j, part], result(j, part), COPY)
         nc.vector.tensor_copy(totals[:, 0, OWN], result(0, OWN))
-        for j, part in enumerate((NARROW, MIDDLE, WIDE), start=1):
+        for j, part in enumerate((SEED, rest), start=1):
             nc.vector.tensor_tensor(totals[:, 0, part], result(TOP - 1, part), fetched[:, 0, part], ADD)
             nc.vector.tensor_tensor(totals[:, j, OWN], result(j, OWN), totals[:, j - 1, OWN], ADD)
+        nc.vector.tensor_tensor(
+            totals[:, 1, shared_tokens], totals[:, 0, shared_tokens], fetched[:, 1, shared_tokens], ADD
+        )
+        nc.vector.tensor_tensor(totals[:, 3, OWN], result(3, OWN), totals[:, 2, OWN], ADD)
         nc.sync.dma_start(out[:, OWN], totals[:, TOP - 1, OWN])
-        for j in range(1, TOP - 1):
-            for part in (WIDE, MIDDLE, NARROW):
-                nc.vector.tensor_tensor(totals[:, j, part], totals[:, j - 1, part], fetched[:, j, part], ADD)
-                if j == TOP - 2:
-                    nc.sync.dma_start(out[:, part], totals[:, j, part])
+        for part in (WIDE, MIDDLE, NARROW):
+            nc.vector.tensor_tensor(totals[:, 2, part], totals[:, 1, part], fetched[:, 2, part], ADD)
+            nc.sync.dma_start(out[:, part], totals[:, 2, part])

@@ -40,12 +40,15 @@ G0_END = FIRST + RUN
 G1_END = 2 * RUN
 LATE0, LATE1 = S - 2 * C, S - 3 * C
 LATE_G = LATE1 + 384
-LONG_G = G0_END + G1_END
-LONG_V = LATE0 - G0_END + LATE1 - G1_END
-SHORT = PASSES * S - LONG_G - LONG_V
+SPANS = [(0, 0, 3 * RUN), (1, 0, RUN), (0, 3 * RUN, LATE0), (1, 3 * RUN, LATE1), (1, RUN, 3 * RUN)]
+SPANS = SPANS + [(0, LATE0, S), (1, LATE1, S)]
+LONG_CALLS = [(0, 0, RUN), (1, 0, RUN), (0, RUN, 2 * RUN), (0, 2 * RUN, 3 * RUN)]
+LONG_CALLS = LONG_CALLS + [(0, 3 * RUN, LATE0), (1, 3 * RUN, LATE1), (1, RUN, 2 * RUN), (1, 2 * RUN, 3 * RUN)]
+SHORT_CALLS = [(0, LATE0, S - C), (1, LATE1, S - C), (1, S - C, S), (0, S - C, S - P), (0, S - P, S)]
+LONG = LATE0 + LATE1
 HELP = 768
 W_CUTS = (0, 4, 8, 11, 14, 16)
-OWN, SEED, WIDE, MIDDLE, NARROW = slice(0, 256), slice(256, 512), slice(256, 640), slice(640, 896), slice(896, T)
+OWN, WIDE, MIDDLE, NARROW = slice(0, 256), slice(256, 640), slice(640, 896), slice(896, T)
 
 
 def tile_moe_pre_lin_silu_kernel(
@@ -65,11 +68,9 @@ def tile_moe_pre_lin_silu_kernel(
         at_a = at_e + STAGE
         at_d = at_a + STAGE + LAP
         at_c = at_d + STAGE
-        at_woven_v = at_c + STAGE + LAP
-        at_b = at_woven_v + LONG_V * PACK * 2
+        at_woven = at_c + STAGE + LAP
+        at_b = at_woven + LONG * PACK * 2
         at_plane = at_b + STAGE
-        at_gate = at_plane + (RUN + LIST) * 4
-        at_gate2 = at_gate + G1_END * 4
 
         last_plane = PACK - 1
         planes = [
@@ -99,8 +100,8 @@ def tile_moe_pre_lin_silu_kernel(
             rows = xT[a * K_PASS : (a + 1) * K_PASS, :].rearrange("(p r) t -> p r t", r=PACK)
             nc.sync.dma_start(planes[i][:, :T], rows[:, r, :])
 
-        gate_long = placed("gate_long", [P, G1_END], F32, at_gate)
-        gate_late = placed("gate_late", [P, LATE_G - LATE1], F32, at_gate2)
+        gate_long = keep.tile([P, G1_END], F32, align_bytes=64)
+        gate_late = keep.tile([P, LATE_G - LATE1], F32, align_bytes=64)
         slot_tokens = lists.tile([P, S // LIST], U16)
         nc.sync.dma_start(slot_tokens[:], offs)
         for i in range(3):
@@ -155,14 +156,29 @@ def tile_moe_pre_lin_silu_kernel(
             for r in rows:
                 nc.scalar.activation(raw[:, r], picked(a, r, lo, hi), COPY)
 
-        def vector_weave(woven, raw, lo):
+        column_of = {}
+        for a, lo, hi in SPANS:
+            for slot in range(lo, hi, LIST):
+                column_of[a, slot] = len(column_of) * LIST
+
+        def columns(parts, a, lo, hi):
+            col = column_of[a, lo]
+            first, tile = [part for part in parts if part[0] <= col][-1]
+            return tile[:, col - first : col - first + hi - lo]
+
+        woven = [
+            (0, placed("woven_long", [P, LONG - RUN, PACK], BF16, at_woven)),
+            (LONG - RUN, placed("woven_last", [P, RUN, PACK], BF16, at_woven + (LONG - RUN) * PACK * 2)),
+        ]
+
+        def vector_weave(a, lo, raw):
             hi = lo + raw.shape[2]
             cuts = [lo, *range((lo // CELL + 1) * CELL, hi, CELL), hi]
             for first, end in zip(cuts, cuts[1:]):
                 cols = slice(first - lo, end - lo)
                 weights = gate_banks[first // CELL][:, first % CELL : first % CELL + end - first]
                 nc.vector.tensor_tensor(
-                    woven[:, cols].rearrange("p (c i) r -> p c r i", i=PAIR),
+                    columns(woven, a, first, end).rearrange("p (c i) r -> p c r i", i=PAIR),
                     raw[:, :, cols].rearrange("p r (c i) -> p c r i", i=PAIR),
                     weights.rearrange("p (c i) -> p c i", i=PAIR)
                     .unsqueeze(2)
@@ -180,36 +196,33 @@ def tile_moe_pre_lin_silu_kernel(
             )
 
         g0 = staging("g0", FIRST, at_a + LAP + STAGE - FIRST * PACK * 4)
-        g1 = staging("g1", RUN, at_b - LAP)
+        g1 = staging("g1", G0_END - FIRST, at_b)
         g2 = staging("g2", RUN, at_c)
         v0 = staging("v0", RUN, at_d)
-        woven_g = keep.tile([P, LONG_G, PACK], BF16, align_bytes=64)
         vector_gather(0, 0, FIRST, g0)
         scalar_gather(0, FIRST, G0_END, g1, range(PACK - 1))
         vector_gather(0, FIRST, G0_END, g1, [PACK - 1])
         vector_gather(1, 0, RUN, g2)
         scalar_gather(1, G1_END, G1_END + RUN, v0)
         for half in (slice(0, PACK // 2), slice(PACK // 2, PACK)):
-            gpsimd_weave(woven_g[:, G1_END : G1_END + FIRST, half], g0[:, half], gate_long[:, :FIRST])
-        gpsimd_weave(woven_g[:, G1_END + FIRST :], g1[:], gate_long[:, FIRST:G0_END])
-        gpsimd_weave(woven_g[:, :RUN], g2[:], gate_long[:, :RUN])
+            gpsimd_weave(columns(woven, 0, 0, FIRST)[:, :, half], g0[:, half], gate_long[:, :FIRST])
+        gpsimd_weave(columns(woven, 0, FIRST, G0_END), g1[:], gate_long[:, FIRST:G0_END])
+        gpsimd_weave(columns(woven, 1, 0, RUN), g2[:], gate_long[:, :RUN])
         v1 = staging("v1", RUN, at_e + LAP)
         scalar_gather(0, G0_END, G0_END + RUN, v1)
         g3 = staging("g3", RUN, at_a + LAP)
         vector_gather(1, RUN, G1_END, g3, range(PACK - 1))
         vector_gather(1, RUN, G1_END - HELP, g3[:, :, : RUN - HELP], [PACK - 1])
         scalar_gather(1, G1_END - HELP, G1_END, g3[:, :, RUN - HELP :], [PACK - 1])
-        gpsimd_weave(woven_g[:, RUN:G1_END], g3[:], gate_long[:, RUN:])
-        woven_v = placed("woven_v", [P, LONG_V, PACK], BF16, at_woven_v)
-        woven_v0, woven_v1 = woven_v[:, : LATE0 - G0_END], woven_v[:, LATE0 - G0_END :]
-        vector_weave(woven_v1[:, :RUN], v0[:], G1_END)
-        vector_weave(woven_v0[:, :RUN], v1[:], G0_END)
-        v2 = staging("v2", RUN - C, at_b)
-        v3 = staging("v3", C, at_b + (RUN - C) * PACK * 4)
+        gpsimd_weave(columns(woven, 1, RUN, G1_END), g3[:], gate_long[:, RUN:])
+        vector_weave(1, G1_END, v0[:])
+        vector_weave(0, G0_END, v1[:])
+        v2 = staging("v2", LATE0 - G0_END - RUN, at_b)
+        v3 = staging("v3", C, at_b + STAGE - C * PACK * 4)
         scalar_gather(0, G0_END + RUN, LATE0, v2)
         scalar_gather(1, G1_END + RUN, LATE1, v3)
-        vector_weave(woven_v0[:, RUN:], v2[:], G0_END + RUN)
-        vector_weave(woven_v1[:, RUN:], v3[:], G1_END + RUN)
+        vector_weave(0, G0_END + RUN, v2[:])
+        vector_weave(1, G1_END + RUN, v3[:])
         l0 = staging("l0", S - LATE1, at_c + LAP)
         l1 = staging("l1", C, at_c + LAP + (S - LATE1) * PACK * 4)
         l2 = staging("l2", C, at_c + LAP - C * PACK * 4)
@@ -217,56 +230,46 @@ def tile_moe_pre_lin_silu_kernel(
         scalar_gather(0, LATE0, S - C, l1)
         scalar_gather(0, S - C, S, l2)
 
-        spans = [(1, 0, G1_END), (0, 0, G0_END), (0, G0_END, LATE0), (1, G1_END, LATE1), (1, LATE1, S), (0, LATE0, S)]
-        column_of = {}
-        for a, lo, hi in spans:
-            for slot in range(lo, hi, P):
-                column_of[a, slot] = len(column_of) * P
-        codes = placed("codes", [P, PASSES * S], U32, at_e + LAP)
-        scale_of = {}
+        codes = [(0, placed("codes0", [P, S], U32, at_e + LAP)), (S, placed("codes1", [P, S], U32, at_a + LAP))]
+        scale_bytes = keep.tile([P, PASSES * S], U8, align_bytes=64)
+        scales = [(0, scale_bytes)]
+        done = []
         sums_of = {}
         groups = [(lo, min(lo + CELL, LATE1), lo // CELL) for lo in range(0, LATE1, CELL)]
-        groups = groups + [(lo, hi, j) for j, (lo, hi) in enumerate(((LATE1, LATE0), (LATE0, S - C), (S - C, S - P), (S - P, S)))]
+        late_groups = ((LATE1, LATE0), (LATE0, S - C), (S - C, S - P), (S - P, S))
+        groups = groups + [(lo, hi, j) for j, (lo, hi) in enumerate(late_groups)]
 
         def multiply(lo, hi, sums):
-            for n, a in enumerate(sorted(range(PASSES), key=lambda a: scale_of[column_of[a, lo]][0])):
+            for n, a in enumerate(sorted(range(PASSES), key=lambda a: done.index((a, lo)))):
                 matrix = lo // C * PASSES + a
-                col = column_of[a, lo]
-                order, first, scales = scale_of[col]
                 nc.tensor.matmul_mx(
                     out=sums,
                     lhsT=w_codes[:, matrix, :].bitcast(FP8X4),
                     lhsT_scale=w_scale[:, matrix, :],
-                    rhs=codes[:, col : col + hi - lo].bitcast(FP8X4),
-                    rhs_scale=scales[:, col - first : col - first + hi - lo],
+                    rhs=columns(codes, a, lo, hi).bitcast(FP8X4),
+                    rhs_scale=columns(scales, a, lo, hi),
                     start=(n == 0),
                     stop=(n == PASSES - 1),
                 )
             sums_of[lo] = (hi, sums)
 
-        def quantise(woven, woven_first, scales, scales_first, lo, hi):
+        def quantise(a, lo, hi):
             nc.vector.quantize_mx(
-                out=codes[:, lo:hi].bitcast(FP8X4),
-                scales=scales[:, lo - scales_first : hi - scales_first],
-                in_=woven[:, lo - woven_first : hi - woven_first].rearrange("p c r -> p (c r)"),
+                out=columns(codes, a, lo, hi).bitcast(FP8X4),
+                scales=columns(scales, a, lo, hi),
+                in_=columns(woven, a, lo, hi).rearrange("p c r -> p (c r)"),
             )
-            for col in range(lo, hi, P):
-                scale_of[col] = (len(scale_of), scales_first, scales)
+            done.extend((a, slot) for slot in range(lo, hi, P))
             for first, end, j in groups:
-                ready = all(column_of[a, slot] in scale_of for a in range(PASSES) for slot in range(first, end, P))
+                ready = all((n, slot) in done for n in range(PASSES) for slot in range(first, end, P))
                 if ready and first not in sums_of:
                     bank = psum.tile([N, end - first], F32, tag=f"bank{j}", name=f"sums{first}")
                     for start in range(first, end, C):
                         stop = min(start + C, end)
                         multiply(start, stop, bank[:, start - first : stop - first])
 
-        scales_long = placed("scales_long", [P, LONG_G + LONG_V], U8, at_gate)
-        for lo, hi in ((2 * RUN, 3 * RUN), (0, RUN), (3 * RUN, 3 * RUN + CELL), (3 * RUN + CELL, LONG_G)):
-            quantise(woven_g, 0, scales_long, 0, lo, hi)
-        quantise(woven_v, LONG_G, scales_long, 0, LONG_G, LONG_G + RUN)
-        quantise(woven_g, 0, scales_long, 0, RUN, 2 * RUN)
-        for lo in range(LONG_G + RUN, LONG_G + LONG_V, RUN):
-            quantise(woven_v, LONG_G, scales_long, 0, lo, lo + RUN)
+        for call in LONG_CALLS:
+            quantise(*call)
 
         y = placed("y", [N, S], F32, at_plane + RUN * 4 - S * 4)
 
@@ -277,16 +280,13 @@ def tile_moe_pre_lin_silu_kernel(
         for lo in range(0, LATE1, C):
             activate(lo)
 
-        woven_l = placed("woven_l", [P, SHORT, PACK], BF16, at_woven_v)
-        late1, late0 = woven_l[:, : S - LATE1], woven_l[:, S - LATE1 :]
-        gpsimd_weave(late1[:, : LATE_G - LATE1], l0[:, :, : LATE_G - LATE1], gate_late[:])
-        vector_weave(late1[:, LATE_G - LATE1 :], l0[:, :, LATE_G - LATE1 :], LATE_G)
-        vector_weave(late0[:, :C], l1[:], LATE0)
-        vector_weave(late0[:, C:], l2[:], S - C)
-        scales_late = placed("scales_late", [P, SHORT], U8, at_gate2)
-        for a, lo, hi in ((1, LATE1, S - C), (0, LATE0, S - C), (1, S - C, S), (0, S - C, S - P), (0, S - P, S)):
-            col = column_of[a, lo]
-            quantise(woven_l, LONG_G + LONG_V, scales_late, LONG_G + LONG_V, col, col + hi - lo)
+        woven.append((LONG, placed("woven_short", [P, PASSES * S - LONG, PACK], BF16, at_woven)))
+        gpsimd_weave(columns(woven, 1, LATE1, LATE_G), l0[:, :, : LATE_G - LATE1], gate_late[:])
+        vector_weave(1, LATE_G, l0[:, :, LATE_G - LATE1 :])
+        vector_weave(0, LATE0, l1[:])
+        vector_weave(0, S - C, l2[:])
+        for call in SHORT_CALLS:
+            quantise(*call)
         for lo in [*range(LATE1, S, C), S - P]:
             activate(lo)
 
@@ -295,20 +295,16 @@ def tile_moe_pre_lin_silu_kernel(
 
         fetched = keep.tile([N, TOP - 1, T], F32, align_bytes=64)
         totals = keep.tile([N, TOP, T], F32, align_bytes=64)
-        rest = slice(SEED.stop, T)
-        shared_tokens = slice(OWN.stop, T)
-        for j, parts in enumerate(((SEED, rest), (shared_tokens,), (WIDE, MIDDLE, NARROW))):
+        for j, parts in enumerate(((NARROW, MIDDLE, WIDE), (slice(OWN.stop, T),), (WIDE, MIDDLE, NARROW))):
             for part in parts:
                 nc.scalar.activation(fetched[:, j, part], result(j, part), COPY)
         nc.vector.tensor_copy(totals[:, 0, OWN], result(0, OWN))
-        for j, part in enumerate((SEED, rest), start=1):
+        for j, part in enumerate((NARROW, MIDDLE, WIDE), start=1):
             nc.vector.tensor_tensor(totals[:, 0, part], result(TOP - 1, part), fetched[:, 0, part], ADD)
             nc.vector.tensor_tensor(totals[:, j, OWN], result(j, OWN), totals[:, j - 1, OWN], ADD)
-        nc.vector.tensor_tensor(
-            totals[:, 1, shared_tokens], totals[:, 0, shared_tokens], fetched[:, 1, shared_tokens], ADD
-        )
-        nc.vector.tensor_tensor(totals[:, 3, OWN], result(3, OWN), totals[:, 2, OWN], ADD)
         nc.sync.dma_start(out[:, OWN], totals[:, TOP - 1, OWN])
+        for part in (WIDE, slice(WIDE.stop, T)):
+            nc.vector.tensor_tensor(totals[:, 1, part], totals[:, 0, part], fetched[:, 1, part], ADD)
         for part in (WIDE, MIDDLE, NARROW):
             nc.vector.tensor_tensor(totals[:, 2, part], totals[:, 1, part], fetched[:, 2, part], ADD)
             nc.sync.dma_start(out[:, part], totals[:, 2, part])

@@ -44,7 +44,7 @@ SPANS = [(0, 0, 3 * RUN), (1, 0, RUN), (0, 3 * RUN, LATE0), (1, 3 * RUN, LATE1),
 SPANS = SPANS + [(0, LATE0, S), (1, LATE1, S)]
 LONG_CALLS = [(0, 0, RUN), (1, 0, RUN), (0, RUN, 2 * RUN), (0, 2 * RUN, 3 * RUN)]
 LONG_CALLS = LONG_CALLS + [(0, 3 * RUN, LATE0), (1, 3 * RUN, LATE1), (1, RUN, 2 * RUN), (1, 2 * RUN, 3 * RUN)]
-SHORT_CALLS = [(0, LATE0, S - C), (1, LATE1, S - C), (1, S - C, S), (0, S - C, S - P), (0, S - P, S)]
+SHORT_CALLS = [(1, LATE1, S - C), (0, LATE0, S - C), (1, S - C, S), (0, S - C, S - P), (0, S - P, S)]
 LONG = LATE0 + LATE1
 HELP = 768
 W_CUTS = (0, 4, 8, 11, 14, 16)
@@ -71,6 +71,8 @@ def tile_moe_pre_lin_silu_kernel(
         at_woven = at_c + STAGE + LAP
         at_b = at_woven + LONG * PACK * 2
         at_plane = at_b + STAGE
+        at_gate = at_plane + (RUN + LIST) * 4
+        at_gate_late = at_gate + G1_END * 4
 
         last_plane = PACK - 1
         planes = [
@@ -100,8 +102,8 @@ def tile_moe_pre_lin_silu_kernel(
             rows = xT[a * K_PASS : (a + 1) * K_PASS, :].rearrange("(p r) t -> p r t", r=PACK)
             nc.sync.dma_start(planes[i][:, :T], rows[:, r, :])
 
-        gate_long = keep.tile([P, G1_END], F32, align_bytes=64)
-        gate_late = keep.tile([P, LATE_G - LATE1], F32, align_bytes=64)
+        gate_long = placed("gate_long", [P, G1_END], F32, at_gate)
+        gate_late = placed("gate_late", [P, LATE_G - LATE1], F32, at_gate_late)
         slot_tokens = lists.tile([P, S // LIST], U16)
         nc.sync.dma_start(slot_tokens[:], offs)
         for i in range(3):
@@ -231,8 +233,7 @@ def tile_moe_pre_lin_silu_kernel(
         scalar_gather(0, S - C, S, l2)
 
         codes = [(0, placed("codes0", [P, S], U32, at_e + LAP)), (S, placed("codes1", [P, S], U32, at_a + LAP))]
-        scale_bytes = keep.tile([P, PASSES * S], U8, align_bytes=64)
-        scales = [(0, scale_bytes)]
+        scales = [(0, placed("scales_long", [P, LONG], U8, at_gate))]
         done = []
         sums_of = {}
         groups = [(lo, min(lo + CELL, LATE1), lo // CELL) for lo in range(0, LATE1, CELL)]
@@ -285,6 +286,7 @@ def tile_moe_pre_lin_silu_kernel(
         vector_weave(1, LATE_G, l0[:, :, LATE_G - LATE1 :])
         vector_weave(0, LATE0, l1[:])
         vector_weave(0, S - C, l2[:])
+        scales.append((LONG, placed("scales_short", [P, PASSES * S - LONG], U8, at_gate_late)))
         for call in SHORT_CALLS:
             quantise(*call)
         for lo in [*range(LATE1, S, C), S - P]:

@@ -238,7 +238,7 @@ def tile_moe_pre_lin_silu_kernel(
         sums_of = {}
         groups = [(lo, min(lo + CELL, LATE1), lo // CELL) for lo in range(0, LATE1, CELL)]
         late_groups = ((LATE1, LATE0), (LATE0, S - C), (S - C, S - P), (S - P, S))
-        groups = groups + [(lo, hi, j) for j, (lo, hi) in enumerate(late_groups)]
+        groups = groups + [(lo, hi, (j - 1) % (S // CELL)) for j, (lo, hi) in enumerate(late_groups)]
 
         def multiply(lo, hi, sums):
             for n, a in enumerate(sorted(range(PASSES), key=lambda a: done.index((a, lo)))):

@@ -35,8 +35,9 @@ LINE = 4
 STAGE = PACK * RUN * 4
 LAP = 64
 
-FIRST = 768
-G0_END = FIRST + RUN
+WINDOW = RUN + P
+FIRST = 640
+G0_END = FIRST + WINDOW
 G1_END = 2 * RUN
 LATE0, LATE1 = S - 2 * C, S - 3 * C
 LATE_G = LATE1 + 384
@@ -46,7 +47,7 @@ LONG_CALLS = [(0, 0, RUN), (1, 0, RUN), (0, RUN, 2 * RUN), (0, 2 * RUN, 3 * RUN)
 LONG_CALLS = LONG_CALLS + [(0, 3 * RUN, LATE0), (1, 3 * RUN, LATE1), (1, RUN, 2 * RUN), (1, 2 * RUN, 3 * RUN)]
 SHORT_CALLS = [(1, LATE1, S - C), (0, LATE0, S - C), (1, S - C, S), (0, S - C, S - P), (0, S - P, S)]
 LONG = LATE0 + LATE1
-HELP = 768
+HELP = 192
 W_CUTS = (0, 4, 8, 11, 14, 16)
 OWN, WIDE, MIDDLE, NARROW = slice(0, 256), slice(256, 640), slice(640, 896), slice(896, T)
 
@@ -70,15 +71,15 @@ def tile_moe_pre_lin_silu_kernel(
         at_c = at_d + STAGE
         at_woven = at_c + STAGE + LAP
         at_b = at_woven + LONG * PACK * 2
-        at_plane = at_b + STAGE
-        at_gate = at_plane + (RUN + LIST) * 4
+        at_plane = at_b + WINDOW * PACK * 4
+        at_gate = at_plane + (WINDOW + LIST) * 4
         at_gate_late = at_gate + G1_END * 4
 
         last_plane = PACK - 1
         planes = [
-            placed("plane_last", [P, RUN + LIST], F32, at_plane)
+            placed("plane_last", [P, WINDOW + LIST], F32, at_plane)
             if i == last_plane
-            else keep.tile([P, RUN + LIST], F32, tag=f"plane{i}", name=f"plane{i}")
+            else keep.tile([P, WINDOW + LIST], F32, tag=f"plane{i}", name=f"plane{i}")
             for i in range(PASSES * PACK)
         ]
         w_scale = keep.tile([P, E * PASSES, N], U8, align_bytes=64)
@@ -109,9 +110,11 @@ def tile_moe_pre_lin_silu_kernel(
         for i in range(3):
             load_plane(i)
         nc.sync.dma_start(gate_long[:, :FIRST], gate[:P, :FIRST])
-        for i in range(3, PASSES * PACK):
+        for i in range(3, 5):
             load_plane(i)
         nc.sync.dma_start(gate_long[:, FIRST:G0_END], gate[:P, FIRST:G0_END])
+        for i in range(5, PASSES * PACK):
+            load_plane(i)
         gate_rows = placed("gate_rows", [P, P], F32, at_a + LAP - P * 2)
         nc.sync.dma_start(gate_rows[:], gate[: P * P // S].rearrange("k (c q) -> (k c) q", q=P))
         nc.sync.dma_start(gate_long[:, G0_END:], gate[:P, G0_END:G1_END])

@@ -40,12 +40,12 @@ FIRST = 640
 G0_END = FIRST + WINDOW
 G1_END = 2 * RUN
 LATE0, LATE1 = S - 2 * C, S - 3 * C
-LATE_G = LATE1 + 384
+LATE_G = LATE1 + 416
 SPANS = [(0, 0, 3 * RUN), (1, 0, RUN), (0, 3 * RUN, LATE0), (1, 3 * RUN, LATE1), (1, RUN, 3 * RUN)]
 SPANS = SPANS + [(0, LATE0, S), (1, LATE1, S)]
 LONG_CALLS = [(0, 0, RUN), (1, 0, RUN), (0, RUN, 2 * RUN), (0, 2 * RUN, 3 * RUN)]
 LONG_CALLS = LONG_CALLS + [(0, 3 * RUN, LATE0), (1, 3 * RUN, LATE1), (1, RUN, 2 * RUN), (1, 2 * RUN, 3 * RUN)]
-SHORT_CALLS = [(1, LATE1, S - C), (0, LATE0, S - C), (1, S - C, S), (0, S - C, S - P), (0, S - P, S)]
+SHORT_CALLS = [(0, LATE0, S - C), (1, LATE1, S - C), (1, S - C, S), (0, S - C, S - P), (0, S - P, S)]
 LONG = LATE0 + LATE1
 HELP = 192
 W_CUTS = (0, 4, 8, 11, 14, 16)
@@ -72,8 +72,6 @@ def tile_moe_pre_lin_silu_kernel(
         at_woven = at_c + STAGE + LAP
         at_b = at_woven + LONG * PACK * 2
         at_plane = at_b + WINDOW * PACK * 4
-        at_gate = at_plane + (WINDOW + LIST) * 4
-        at_gate_late = at_gate + G1_END * 4
 
         last_plane = PACK - 1
         planes = [
@@ -103,8 +101,8 @@ def tile_moe_pre_lin_silu_kernel(
             rows = xT[a * K_PASS : (a + 1) * K_PASS, :].rearrange("(p r) t -> p r t", r=PACK)
             nc.sync.dma_start(planes[i][:, :T], rows[:, r, :])
 
-        gate_long = placed("gate_long", [P, G1_END], F32, at_gate)
-        gate_late = placed("gate_late", [P, LATE_G - LATE1], F32, at_gate_late)
+        gate_long = keep.tile([P, G1_END], F32, align_bytes=64)
+        gate_late = keep.tile([P, LATE_G - LATE1], F32, align_bytes=64)
         slot_tokens = lists.tile([P, S // LIST], U16)
         nc.sync.dma_start(slot_tokens[:], offs)
         for i in range(3):
@@ -236,7 +234,8 @@ def tile_moe_pre_lin_silu_kernel(
         scalar_gather(0, S - C, S, l2)
 
         codes = [(0, placed("codes0", [P, S], U32, at_e + LAP)), (S, placed("codes1", [P, S], U32, at_a + LAP))]
-        scales = [(0, placed("scales_long", [P, LONG], U8, at_gate))]
+        scale_bytes = keep.tile([P, PASSES * S], U8, align_bytes=64)
+        scales = [(0, scale_bytes)]
         done = []
         sums_of = {}
         groups = [(lo, min(lo + CELL, LATE1), lo // CELL) for lo in range(0, LATE1, CELL)]
@@ -289,7 +288,6 @@ def tile_moe_pre_lin_silu_kernel(
         vector_weave(1, LATE_G, l0[:, :, LATE_G - LATE1 :])
         vector_weave(0, LATE0, l1[:])
         vector_weave(0, S - C, l2[:])
-        scales.append((LONG, placed("scales_short", [P, PASSES * S - LONG], U8, at_gate_late)))
         for call in SHORT_CALLS:
             quantise(*call)
         for lo in [*range(LATE1, S, C), S - P]:
@@ -298,7 +296,7 @@ def tile_moe_pre_lin_silu_kernel(
         def result(j, part):
             return y[:].indirect(token_slots[j][:, part.start // LIST : part.stop // LIST])
 
-        fetched = keep.tile([N, TOP - 1, T], F32, align_bytes=64)
+        fetched = placed("fetched", [N, TOP - 1, T], F32, at_d)
         totals = keep.tile([N, TOP, T], F32, align_bytes=64)
         for j, parts in enumerate(((NARROW, MIDDLE, WIDE), (slice(OWN.stop, T),), (WIDE, MIDDLE, NARROW))):
             for part in parts:

@@ -45,8 +45,9 @@ SPANS = [(0, 0, 3 * RUN), (1, 0, RUN), (0, 3 * RUN, LATE0), (1, 3 * RUN, LATE1),
 SPANS = SPANS + [(0, LATE0, S), (1, LATE1, S)]
 LONG_CALLS = [(0, 0, RUN), (1, 0, RUN), (0, RUN, 2 * RUN), (0, 2 * RUN, 3 * RUN)]
 LONG_CALLS = LONG_CALLS + [(0, 3 * RUN, LATE0), (1, 3 * RUN, LATE1), (1, RUN, 2 * RUN), (1, 2 * RUN, 3 * RUN)]
-SHORT_CALLS = [(0, LATE0, S - C), (1, LATE1, S - C), (1, S - C, S), (0, S - C, S - P), (0, S - P, S)]
+SHORT_CALLS = [(0, LATE0, S - C), (1, LATE1, LATE0), (1, LATE0, S - C), (1, S - C, S), (0, S - C, S - P), (0, S - P, S)]
 LONG = LATE0 + LATE1
+HELD = 3 * RUN - CELL
 HELP = 192
 W_CUTS = (0, 4, 8, 11, 14, 16)
 OWN, WIDE, MIDDLE, NARROW = slice(0, 256), slice(256, 640), slice(640, 896), slice(896, T)
@@ -238,12 +239,11 @@ def tile_moe_pre_lin_silu_kernel(
         scales = [(0, scale_bytes)]
         done = []
         sums_of = {}
-        groups = [(lo, min(lo + CELL, LATE1), lo // CELL) for lo in range(0, LATE1, CELL)]
-        late_groups = ((LATE1, LATE0), (LATE0, S - C), (S - C, S - P), (S - P, S))
-        groups = groups + [(lo, hi, (j - 1) % (S // CELL)) for j, (lo, hi) in enumerate(late_groups)]
+        groups = [(lo, min(lo + CELL, LATE1), 0 if lo == HELD else lo // CELL) for lo in range(0, LATE1, CELL)]
+        groups = groups + [(LATE1, LATE0, 7), (LATE0, S - C, HELD // CELL), (S - C, S - P, 1), (S - P, S, 2)]
 
         def multiply(lo, hi, sums):
-            for n, a in enumerate(sorted(range(PASSES), key=lambda a: done.index((a, lo)))):
+            for n, a in enumerate(sorted(range(PASSES), key=lambda a: done.index((a, lo)), reverse=lo == HELD)):
                 matrix = lo // C * PASSES + a
                 nc.tensor.matmul_mx(
                     out=sums,

@@ -28,29 +28,31 @@ COPY = mybir.ActivationFunctionType.Copy
 FLOPS = 2 * K * S * N
 BYTES = K * T * 4 + E * K * N + E * K * N // 32 + N * E * 4 + S * 4 + P * (S + TOP * T) // LIST * 2 + N * T * 4
 
-CELL = 512
-RUN = 2 * CELL
+BANK = 512
+CALL = 1024
 PAIR = 2
 LINE = 4
-STAGE = PACK * RUN * 4
-LAP = 64
 
-WINDOW = RUN + P
-FIRST = 640
-G0_END = FIRST + WINDOW
-G1_END = 2 * RUN
-LATE0, LATE1 = S - 2 * C, S - 3 * C
-LATE_G = LATE1 + 416
-SPANS = [(0, 0, 3 * RUN), (1, 0, RUN), (0, 3 * RUN, LATE0), (1, 3 * RUN, LATE1), (1, RUN, 3 * RUN)]
-SPANS = SPANS + [(0, LATE0, S), (1, LATE1, S)]
-LONG_CALLS = [(0, 0, RUN), (1, 0, RUN), (0, RUN, 2 * RUN), (0, 2 * RUN, 3 * RUN)]
-LONG_CALLS = LONG_CALLS + [(0, 3 * RUN, LATE0), (1, 3 * RUN, LATE1), (1, RUN, 2 * RUN), (1, 2 * RUN, 3 * RUN)]
-SHORT_CALLS = [(0, LATE0, S - C), (1, LATE1, LATE0), (1, LATE0, S - C), (1, S - C, S), (0, S - C, S - P), (0, S - P, S)]
-LONG = LATE0 + LATE1
-HELD = 3 * RUN - CELL
-HELP = 192
-W_CUTS = (0, 4, 8, 11, 14, 16)
+FIRST = 608
+POOL_END = (1856, 1824)
+LONG_END = (11 * C, 14 * C)
+SHORT_POOL = (LONG_END[0] + BANK, LONG_END[0] + BANK + 576)
+GATE_BANKS = [(7 * C, 9 * C, 4), (9 * C, 11 * C, 5), (11 * C, 13 * C, 6), (13 * C, 14 * C, 3), (14 * C, S, 7)]
+LONG = sum(LONG_END)
+W_CUTS = (0, 3, 6, 9, 12, 14, 16)
 OWN, WIDE, MIDDLE, NARROW = slice(0, 256), slice(256, 640), slice(640, 896), slice(896, T)
+
+
+SPANS = [(0, 0, LONG_END[0]), (1, 0, 9 * C), (1, 13 * C, LONG_END[1]), (1, 9 * C, 13 * C)]
+SPANS = SPANS + [(0, LONG_END[0], S), (1, LONG_END[1], S)]
+
+
+def column(a, slot):
+    first = 0
+    for span_pass, lo, hi in SPANS:
+        if span_pass == a and lo <= slot < hi:
+            return first + slot - lo
+        first = first + hi - lo
 
 
 def tile_moe_pre_lin_silu_kernel(
@@ -66,58 +68,58 @@ def tile_moe_pre_lin_silu_kernel(
         def placed(name, shape, dtype, offset):
             return shared.tile(shape, dtype, align_bytes=64, tag=name, name=name, offset=offset)
 
-        at_e = 0
-        at_a = at_e + STAGE
-        at_d = at_a + STAGE + LAP
-        at_c = at_d + STAGE
-        at_woven = at_c + STAGE + LAP
-        at_b = at_woven + LONG * PACK * 2
-        at_plane = at_b + WINDOW * PACK * 4
+        widths = [end + LIST for end in POOL_END]
+        at_planes = 0
+        at_wide = at_planes + PACK * 4 * sum(widths)
+        at_upper0 = at_wide + (LONG_END[1] - POOL_END[1]) * PACK * 4
+        at_rows = at_upper0 + POOL_END[0] * PAIR * 4
+        at_lower1 = max(at_rows + P * 4, at_upper0 + (LONG_END[0] - POOL_END[0]) * PACK * 4)
+        at_lower0 = at_lower1 + (S - LONG_END[0]) * PACK * 4
+        at_woven = at_lower0 + POOL_END[0] * PAIR * 4
 
-        last_plane = PACK - 1
-        planes = [
-            placed("plane_last", [P, WINDOW + LIST], F32, at_plane)
-            if i == last_plane
-            else keep.tile([P, WINDOW + LIST], F32, tag=f"plane{i}", name=f"plane{i}")
-            for i in range(PASSES * PACK)
-        ]
-        w_scale = keep.tile([P, E * PASSES, N], U8, align_bytes=64)
-        nc.vector.memset(w_scale[:].bitcast(I32), 0)
+        planes = {}
+        for a in range(PASSES):
+            for r in range(PACK):
+                offset = at_planes + (a * PACK * widths[0] + r * widths[a]) * 4
+                planes[a, r] = placed(f"plane{a}{r}", [P, widths[a]], F32, offset)
+
         ones = keep.tile([P, QUAD], F32)
         nc.vector.memset(ones[:], 1.0)
         warm = keep.tile([P, 1], F32)
         nc.scalar.activation(warm[:], ones[:, :1], SILU)
         identity = keep.tile([P, P], F32)
         nc.vector.memset(identity[:], 0.0)
-        column = keep.tile([P, QUAD], F32, align_bytes=64)
-        nc.vector.tensor_tensor_scan(column[:], ones[:], ones[:], 0.0, MULT, ADD)
-        row = keep.tile([P, QUAD], F32, align_bytes=64)
-        nc.vector.transpose(row[:], column[:])
+        counts = keep.tile([P, QUAD], F32, align_bytes=64)
+        nc.vector.tensor_tensor_scan(counts[:], ones[:], ones[:], 0.0, MULT, ADD)
+        w_scale = keep.tile([P, E * PASSES, N], U8, align_bytes=64)
+        nc.vector.memset(w_scale[:].bitcast(I32), 0)
+        turned_counts = keep.tile([P, QUAD], F32, align_bytes=64)
+        nc.vector.transpose(turned_counts[:], counts[:])
         for start in range(0, P, QUAD):
             quadrant = slice(start, start + QUAD)
-            nc.vector.tensor_tensor(identity[quadrant, quadrant], column[quadrant, :], row[quadrant, :], EQUAL)
+            nc.vector.tensor_tensor(identity[quadrant, quadrant], counts[quadrant, :], turned_counts[quadrant, :], EQUAL)
 
-        def load_plane(i):
-            a, r = divmod(i, PACK)
+        def load_plane(a, r):
             rows = xT[a * K_PASS : (a + 1) * K_PASS, :].rearrange("(p r) t -> p r t", r=PACK)
-            nc.sync.dma_start(planes[i][:, :T], rows[:, r, :])
+            nc.sync.dma_start(planes[a, r][:, :T], rows[:, r, :])
 
-        gate_long = keep.tile([P, G1_END], F32, align_bytes=64)
-        gate_late = keep.tile([P, LATE_G - LATE1], F32, align_bytes=64)
+        gate_long = keep.tile([P, max(POOL_END)], F32, align_bytes=64)
+        gate_short = keep.tile([P, SHORT_POOL[1] - SHORT_POOL[0]], F32, align_bytes=64)
         slot_tokens = lists.tile([P, S // LIST], U16)
         nc.sync.dma_start(slot_tokens[:], offs)
-        for i in range(3):
-            load_plane(i)
+        load_plane(0, 0)
+        load_plane(0, 1)
         nc.sync.dma_start(gate_long[:, :FIRST], gate[:P, :FIRST])
-        for i in range(3, 5):
-            load_plane(i)
-        nc.sync.dma_start(gate_long[:, FIRST:G0_END], gate[:P, FIRST:G0_END])
-        for i in range(5, PASSES * PACK):
-            load_plane(i)
-        gate_rows = placed("gate_rows", [P, P], F32, at_a + LAP - P * 2)
+        load_plane(0, 2)
+        nc.sync.dma_start(gate_long[:, FIRST:], gate[:P, FIRST : max(POOL_END)])
+        load_plane(0, 3)
+        load_plane(1, 0)
+        load_plane(1, 1)
+        gate_rows = placed("gate_rows", [P, P], F32, at_rows)
         nc.sync.dma_start(gate_rows[:], gate[: P * P // S].rearrange("k (c q) -> (k c) q", q=P))
-        nc.sync.dma_start(gate_long[:, G0_END:], gate[:P, G0_END:G1_END])
-        nc.sync.dma_start(gate_late[:], gate[:P, LATE1:LATE_G])
+        load_plane(1, 2)
+        load_plane(1, 3)
+        nc.sync.dma_start(gate_short[:], gate[:P, SHORT_POOL[0] : SHORT_POOL[1]])
         scale_rows = w_scales.rearrange("e a (q r) n -> r q (e a) n", r=PACK)
         for r in range(PACK):
             nc.sync.dma_start(w_scale[r:P:QUAD].bitcast(I32), scale_rows[r].bitcast(I32))
@@ -139,165 +141,167 @@ def tile_moe_pre_lin_silu_kernel(
         gate_cols = keep.tile([P, S // P], F32)
         nc.vector.tensor_copy(gate_cols[:], turned[:, : S // P])
         gate_banks = {}
-        for j in [*range(G1_END // CELL, S // CELL), G0_END // CELL]:
-            bank = psum.tile([P, CELL], F32, tag=f"bank{j}", name=f"gate_bank{j}")
-            for lo in range(max(G0_END - j * CELL, 0), CELL, P):
-                c = (j * CELL + lo) // P
-                nc.tensor.transpose(bank[:, lo : lo + P], gate_cols[:, c : c + 1].to_broadcast([P, P]), identity[:])
+        for first, end, j in GATE_BANKS:
+            bank = psum.tile([P, end - first], F32, tag=f"bank{j}", name=f"gate_bank{j}")
+            for lo in range(first, end, P):
+                spread = gate_cols[:, lo // P : lo // P + 1].to_broadcast([P, P])
+                nc.tensor.transpose(bank[:, lo - first : lo - first + P], spread, identity[:])
             gate_banks[j] = bank
 
-        def staging(name, width, offset):
-            return placed(name, [P, PACK, width], F32, offset)
-
         def picked(a, r, lo, hi):
-            return planes[a * PACK + r][:].indirect(slot_tokens[:, lo // LIST : hi // LIST])
+            return planes[a, r][:].indirect(slot_tokens[:, lo // LIST : hi // LIST])
 
-        def vector_gather(a, lo, hi, raw, rows=range(PACK)):
-            for r in rows:
-                nc.vector.tensor_copy(raw[:, r], picked(a, r, lo, hi))
+        def vector_gather(raw, a, r, lo, hi):
+            nc.vector.tensor_copy(raw, picked(a, r, lo, hi))
 
-        def scalar_gather(a, lo, hi, raw, rows=range(PACK)):
-            for r in rows:
-                nc.scalar.activation(raw[:, r], picked(a, r, lo, hi), COPY)
+        def scalar_gather(raw, a, r, lo, hi):
+            nc.scalar.activation(raw, picked(a, r, lo, hi), COPY)
 
-        column_of = {}
-        for a, lo, hi in SPANS:
-            for slot in range(lo, hi, LIST):
-                column_of[a, slot] = len(column_of) * LIST
-
-        def columns(parts, a, lo, hi):
-            col = column_of[a, lo]
-            first, tile = [part for part in parts if part[0] <= col][-1]
-            return tile[:, col - first : col - first + hi - lo]
+        def scalar_unit(name, a, lo, hi, offset):
+            raw = placed(name, [P, PACK, hi - lo], F32, offset)
+            for r in range(PACK):
+                scalar_gather(raw[:, r], a, r, lo, hi)
+            return raw
 
         woven = [
-            (0, placed("woven_long", [P, LONG - RUN, PACK], BF16, at_woven)),
-            (LONG - RUN, placed("woven_last", [P, RUN, PACK], BF16, at_woven + (LONG - RUN) * PACK * 2)),
+            (0, placed("woven_long", [P, LONG - CALL, PACK], BF16, at_woven)),
+            (LONG - CALL, placed("woven_last", [P, CALL, PACK], BF16, at_woven + (LONG - CALL) * PACK * 2)),
         ]
 
-        def vector_weave(a, lo, raw):
+        def columns(parts, lo, hi):
+            first, tile = [part for part in parts if part[0] <= lo][-1]
+            return tile[:, lo - first : hi - first]
+
+        def woven_slots(a, lo, hi):
+            return columns(woven, column(a, lo), column(a, lo) + hi - lo)
+
+        def vector_weave(raw, a, lo):
             hi = lo + raw.shape[2]
-            cuts = [lo, *range((lo // CELL + 1) * CELL, hi, CELL), hi]
-            for first, end in zip(cuts, cuts[1:]):
-                cols = slice(first - lo, end - lo)
-                weights = gate_banks[first // CELL][:, first % CELL : first % CELL + end - first]
+            for bank_first, bank_end, j in GATE_BANKS:
+                first, end = max(lo, bank_first), min(hi, bank_end)
+                if first >= end:
+                    continue
+                weights = gate_banks[j][:, first - bank_first : end - bank_first]
                 nc.vector.tensor_tensor(
-                    columns(woven, a, first, end).rearrange("p (c i) r -> p c r i", i=PAIR),
-                    raw[:, :, cols].rearrange("p r (c i) -> p c r i", i=PAIR),
+                    woven_slots(a, first, end).rearrange("p (c i) r -> p c r i", i=PAIR),
+                    raw[:, :, first - lo : end - lo].rearrange("p r (c i) -> p c r i", i=PAIR),
                     weights.rearrange("p (c i) -> p c i", i=PAIR)
                     .unsqueeze(2)
                     .to_broadcast([P, (end - first) // PAIR, PACK, PAIR]),
                     MULT,
                 )
 
-        def gpsimd_weave(woven, raw, weights):
-            rows, width = raw.shape[1:]
+        def gpsimd_weave(raw, a, rows, lo, weights):
+            count, width = raw.shape[1:]
             nc.gpsimd.tensor_tensor(
-                woven.rearrange("p (c i) r -> p c r i", i=LINE),
+                woven_slots(a, lo, lo + width)[:, :, rows].rearrange("p (c i) r -> p c r i", i=LINE),
                 raw.rearrange("p r (c i) -> p c r i", i=LINE),
-                weights.rearrange("p (c i) -> p c i", i=LINE).unsqueeze(2).to_broadcast([P, width // LINE, rows, LINE]),
+                weights.rearrange("p (c i) -> p c i", i=LINE).unsqueeze(2).to_broadcast([P, width // LINE, count, LINE]),
                 MULT,
             )
 
-        g0 = staging("g0", FIRST, at_a + LAP + STAGE - FIRST * PACK * 4)
-        g1 = staging("g1", G0_END - FIRST, at_b)
-        g2 = staging("g2", RUN, at_c)
-        v0 = staging("v0", RUN, at_d)
-        vector_gather(0, 0, FIRST, g0)
-        scalar_gather(0, FIRST, G0_END, g1, range(PACK - 1))
-        vector_gather(0, FIRST, G0_END, g1, [PACK - 1])
-        vector_gather(1, 0, RUN, g2)
-        scalar_gather(1, G1_END, G1_END + RUN, v0)
-        for half in (slice(0, PACK // 2), slice(PACK // 2, PACK)):
-            gpsimd_weave(columns(woven, 0, 0, FIRST)[:, :, half], g0[:, half], gate_long[:, :FIRST])
-        gpsimd_weave(columns(woven, 0, FIRST, G0_END), g1[:], gate_long[:, FIRST:G0_END])
-        gpsimd_weave(columns(woven, 1, 0, RUN), g2[:], gate_long[:, :RUN])
-        v1 = staging("v1", RUN, at_e + LAP)
-        scalar_gather(0, G0_END, G0_END + RUN, v1)
-        g3 = staging("g3", RUN, at_a + LAP)
-        vector_gather(1, RUN, G1_END, g3, range(PACK - 1))
-        vector_gather(1, RUN, G1_END - HELP, g3[:, :, : RUN - HELP], [PACK - 1])
-        scalar_gather(1, G1_END - HELP, G1_END, g3[:, :, RUN - HELP :], [PACK - 1])
-        gpsimd_weave(columns(woven, 1, RUN, G1_END), g3[:], gate_long[:, RUN:])
-        vector_weave(1, G1_END, v0[:])
-        vector_weave(0, G0_END, v1[:])
-        v2 = staging("v2", LATE0 - G0_END - RUN, at_b)
-        v3 = staging("v3", C, at_b + STAGE - C * PACK * 4)
-        scalar_gather(0, G0_END + RUN, LATE0, v2)
-        scalar_gather(1, G1_END + RUN, LATE1, v3)
-        vector_weave(0, G0_END + RUN, v2[:])
-        vector_weave(1, G1_END + RUN, v3[:])
-        l0 = staging("l0", S - LATE1, at_c + LAP)
-        l1 = staging("l1", C, at_c + LAP + (S - LATE1) * PACK * 4)
-        l2 = staging("l2", C, at_c + LAP - C * PACK * 4)
-        scalar_gather(1, LATE1, S, l0)
-        scalar_gather(0, LATE0, S - C, l1)
-        scalar_gather(0, S - C, S, l2)
+        lower, upper = slice(0, PAIR), slice(PAIR, PACK)
+        end0, end1 = POOL_END
 
-        codes = [(0, placed("codes0", [P, S], U32, at_e + LAP)), (S, placed("codes1", [P, S], U32, at_a + LAP))]
-        scale_bytes = keep.tile([P, PASSES * S], U8, align_bytes=64)
-        scales = [(0, scale_bytes)]
+        head = placed("head", [P, PAIR, FIRST], F32, at_lower0)
+        lower0 = placed("lower0", [P, PAIR, end0 - FIRST], F32, at_lower0 + FIRST * PAIR * 4)
+        upper0 = placed("upper0", [P, PAIR, end0], F32, at_upper0)
+        vector_gather(head[:, 0], 0, 0, 0, FIRST)
+        scalar_gather(lower0[:, 0], 0, 0, FIRST, end0)
+        vector_gather(head[:, 1], 0, 1, 0, FIRST)
+        vector_gather(lower0[:, 1], 0, 1, FIRST, end0)
+        scalar_gather(upper0[:, 0], 0, 2, 0, end0)
+        vector_gather(upper0[:, 1], 0, 3, 0, end0)
+        gpsimd_weave(head[:], 0, lower, 0, gate_long[:, :FIRST])
+        gpsimd_weave(lower0[:], 0, lower, FIRST, gate_long[:, FIRST:end0])
+        gpsimd_weave(upper0[:], 0, upper, 0, gate_long[:, :end0])
+        wide = scalar_unit("wide", 1, end1, LONG_END[1], at_wide)
+        for rows, name, offset in ((lower, "lower1", at_lower1), (upper, "upper1", at_lower0)):
+            raw = placed(name, [P, PAIR, end1], F32, offset)
+            for r in range(rows.start, rows.stop):
+                vector_gather(raw[:, r - rows.start], 1, r, 0, end1)
+            gpsimd_weave(raw[:], 1, rows, 0, gate_long[:, :end1])
+        narrow = scalar_unit("narrow", 0, end0, LONG_END[0], at_upper0)
+        vector_weave(wide[:], 1, end1)
+        vector_weave(narrow[:], 0, end0)
+        short0 = scalar_unit("short0", 0, LONG_END[0], S, at_lower1)
+        short1 = scalar_unit("short1", 1, LONG_END[1], S, at_lower0)
+
+        codes = [
+            (0, placed("codes_long", [P, LONG], U32, at_wide)),
+            (LONG, placed("codes_short", [P, PASSES * S - LONG], U32, at_upper0)),
+        ]
+        scales = keep.tile([P, PASSES * S], U8, align_bytes=64)
         done = []
         sums_of = {}
-        groups = [(lo, min(lo + CELL, LATE1), 0 if lo == HELD else lo // CELL) for lo in range(0, LATE1, CELL)]
-        groups = groups + [(LATE1, LATE0, 7), (LATE0, S - C, HELD // CELL), (S - C, S - P, 1), (S - P, S, 2)]
+        groups = [(lo, min(lo + BANK, LONG_END[0]), lo // BANK) for lo in range(0, LONG_END[0], BANK)]
+        late = [*range(LONG_END[0], S, C), S - P]
+        for lo, hi, j in zip(late, late[1:] + [S], (6, 7, 0, 1, 2, 3)):
+            groups.append((lo, hi, j))
 
-        def multiply(lo, hi, sums):
-            for n, a in enumerate(sorted(range(PASSES), key=lambda a: done.index((a, lo)), reverse=lo == HELD)):
+        def multiply(lo, hi, sums, later_first):
+            order = sorted(range(PASSES), key=lambda a: done.index(column(a, lo)), reverse=later_first)
+            for n, a in enumerate(order):
                 matrix = lo // C * PASSES + a
+                first, end = column(a, lo), column(a, lo) + hi - lo
                 nc.tensor.matmul_mx(
                     out=sums,
                     lhsT=w_codes[:, matrix, :].bitcast(FP8X4),
                     lhsT_scale=w_scale[:, matrix, :],
-                    rhs=columns(codes, a, lo, hi).bitcast(FP8X4),
-                    rhs_scale=columns(scales, a, lo, hi),
+                    rhs=columns(codes, first, end).bitcast(FP8X4),
+                    rhs_scale=scales[:, first:end],
                     start=(n == 0),
                     stop=(n == PASSES - 1),
                 )
             sums_of[lo] = (hi, sums)
 
-        def quantise(a, lo, hi):
+        def quantise(lo, hi):
             nc.vector.quantize_mx(
-                out=columns(codes, a, lo, hi).bitcast(FP8X4),
-                scales=columns(scales, a, lo, hi),
-                in_=columns(woven, a, lo, hi).rearrange("p c r -> p (c r)"),
+                out=columns(codes, lo, hi).bitcast(FP8X4),
+                scales=scales[:, lo:hi],
+                in_=columns(woven, lo, hi).rearrange("p c r -> p (c r)"),
             )
-            done.extend((a, slot) for slot in range(lo, hi, P))
+            done.extend(range(lo, hi, P))
             for first, end, j in groups:
-                ready = all((n, slot) in done for n in range(PASSES) for slot in range(first, end, P))
+                ready = all(column(a, slot) in done for a in range(PASSES) for slot in range(first, end, P))
                 if ready and first not in sums_of:
                     bank = psum.tile([N, end - first], F32, tag=f"bank{j}", name=f"sums{first}")
+                    waits_for_silu = LONG_END[0] <= first < LONG_END[1] and j not in gate_banks
                     for start in range(first, end, C):
                         stop = min(start + C, end)
-                        multiply(start, stop, bank[:, start - first : stop - first])
+                        multiply(start, stop, bank[:, start - first : stop - first], waits_for_silu)
 
-        for call in LONG_CALLS:
-            quantise(*call)
+        cuts = [*range(0, LONG - CALL, CALL), LONG - CALL, LONG]
+        for lo, hi in zip(cuts, cuts[1:]):
+            quantise(lo, hi)
 
-        y = placed("y", [N, S], F32, at_plane + RUN * 4 - S * 4)
+        y = placed("y", [N, S], F32, at_wide - S * 4)
 
         def activate(lo):
             hi, sums = sums_of[lo]
             nc.scalar.activation(y[:, lo:hi], sums, SILU, bias=bias[:, lo // C : lo // C + 1])
 
-        for lo in range(0, LATE1, C):
+        for lo in range(0, LONG_END[0], C):
             activate(lo)
 
         woven.append((LONG, placed("woven_short", [P, PASSES * S - LONG, PACK], BF16, at_woven)))
-        gpsimd_weave(columns(woven, 1, LATE1, LATE_G), l0[:, :, : LATE_G - LATE1], gate_late[:])
-        vector_weave(1, LATE_G, l0[:, :, LATE_G - LATE1 :])
-        vector_weave(0, LATE0, l1[:])
-        vector_weave(0, S - C, l2[:])
-        for call in SHORT_CALLS:
-            quantise(*call)
-        for lo in [*range(LATE1, S, C), S - P]:
+        first, end = SHORT_POOL[0] - LONG_END[0], SHORT_POOL[1] - LONG_END[0]
+        gpsimd_weave(short0[:, :, first:end], 0, slice(0, PACK), SHORT_POOL[0], gate_short[:])
+        vector_weave(short0[:, :, :first], 0, LONG_END[0])
+        vector_weave(short0[:, :, end:], 0, SHORT_POOL[1])
+        vector_weave(short1[:], 1, LONG_END[1])
+        short_calls = [(0, LONG_END[0], SHORT_POOL[0]), (0, SHORT_POOL[0], S - C), (1, LONG_END[1], S - C)]
+        short_calls = short_calls + [(0, S - C, S), (1, S - C, S - P), (1, S - P, S)]
+        for a, lo, hi in short_calls:
+            quantise(column(a, lo), column(a, lo) + hi - lo)
+        for lo in late:
             activate(lo)
 
         def result(j, part):
             return y[:].indirect(token_slots[j][:, part.start // LIST : part.stop // LIST])
 
-        fetched = placed("fetched", [N, TOP - 1, T], F32, at_d)
-        totals = keep.tile([N, TOP, T], F32, align_bytes=64)
+        fetched = placed("fetched", [N, TOP - 1, T], F32, at_planes)
+        totals = placed("totals", [N, TOP, T], F32, at_planes + (TOP - 1) * T * 4)
         for j, parts in enumerate(((NARROW, MIDDLE, WIDE), (slice(OWN.stop, T),), (WIDE, MIDDLE, NARROW))):
             for part in parts:
                 nc.scalar.activation(fetched[:, j, part], result(j, part), COPY)

@@ -33,8 +33,8 @@ CALL = 1024
 PAIR = 2
 LINE = 4
 
-FIRST = 608
-POOL_END = (1856, 1824)
+FIRST = 576
+POOL_END = (7 * C, 1952)
 LONG_END = (11 * C, 14 * C)
 SHORT_POOL = (LONG_END[0] + BANK, LONG_END[0] + BANK + 576)
 GATE_BANKS = [(7 * C, 9 * C, 4), (9 * C, 11 * C, 5), (11 * C, 13 * C, 6), (13 * C, 14 * C, 3), (14 * C, S, 7)]
@@ -68,14 +68,16 @@ def tile_moe_pre_lin_silu_kernel(
         def placed(name, shape, dtype, offset):
             return shared.tile(shape, dtype, align_bytes=64, tag=name, name=name, offset=offset)
 
-        widths = [end + LIST for end in POOL_END]
+        end0, end1 = POOL_END
+        widths = [S - LONG_END[0] + LIST, end1 + LIST]
         at_planes = 0
         at_wide = at_planes + PACK * 4 * sum(widths)
-        at_upper0 = at_wide + (LONG_END[1] - POOL_END[1]) * PACK * 4
-        at_rows = at_upper0 + POOL_END[0] * PAIR * 4
-        at_lower1 = max(at_rows + P * 4, at_upper0 + (LONG_END[0] - POOL_END[0]) * PACK * 4)
-        at_lower0 = at_lower1 + (S - LONG_END[0]) * PACK * 4
-        at_woven = at_lower0 + POOL_END[0] * PAIR * 4
+        at_narrow = at_wide + (LONG_END[1] - end1) * PACK * 4
+        at_rows = at_narrow - P * 2
+        at_second = at_rows + P * 4
+        at_short = at_second + (end0 - FIRST) * PACK * 4
+        at_third = at_short + (S - LONG_END[0]) * PACK * 4
+        at_woven = at_third + end1 * PACK * 4
 
         planes = {}
         for a in range(PASSES):
@@ -111,14 +113,12 @@ def tile_moe_pre_lin_silu_kernel(
         load_plane(0, 1)
         nc.sync.dma_start(gate_long[:, :FIRST], gate[:P, :FIRST])
         load_plane(0, 2)
-        nc.sync.dma_start(gate_long[:, FIRST:], gate[:P, FIRST : max(POOL_END)])
         load_plane(0, 3)
-        load_plane(1, 0)
-        load_plane(1, 1)
+        nc.sync.dma_start(gate_long[:, FIRST:], gate[:P, FIRST : max(POOL_END)])
+        for r in range(PACK):
+            load_plane(1, r)
         gate_rows = placed("gate_rows", [P, P], F32, at_rows)
         nc.sync.dma_start(gate_rows[:], gate[: P * P // S].rearrange("k (c q) -> (k c) q", q=P))
-        load_plane(1, 2)
-        load_plane(1, 3)
         nc.sync.dma_start(gate_short[:], gate[:P, SHORT_POOL[0] : SHORT_POOL[1]])
         scale_rows = w_scales.rearrange("e a (q r) n -> r q (e a) n", r=PACK)
         for r in range(PACK):
@@ -138,7 +138,7 @@ def tile_moe_pre_lin_silu_kernel(
 
         turned = psum.tile([P, P], F32, tag="bank0")
         nc.tensor.transpose(turned[:], gate_rows[:], identity[:])
-        gate_cols = keep.tile([P, S // P], F32)
+        gate_cols = placed("gate_cols", [P, S // P], F32, at_third - S // P * 4)
         nc.vector.tensor_copy(gate_cols[:], turned[:, : S // P])
         gate_banks = {}
         for first, end, j in GATE_BANKS:
@@ -157,10 +157,11 @@ def tile_moe_pre_lin_silu_kernel(
         def scalar_gather(raw, a, r, lo, hi):
             nc.scalar.activation(raw, picked(a, r, lo, hi), COPY)
 
-        def scalar_unit(name, a, lo, hi, offset):
+        def unit(name, a, lo, hi, offset, by_vector=()):
             raw = placed(name, [P, PACK, hi - lo], F32, offset)
             for r in range(PACK):
-                scalar_gather(raw[:, r], a, r, lo, hi)
+                gather = vector_gather if r in by_vector else scalar_gather
+                gather(raw[:, r], a, r, lo, hi)
             return raw
 
         woven = [
@@ -200,60 +201,49 @@ def tile_moe_pre_lin_silu_kernel(
                 MULT,
             )
 
-        lower, upper = slice(0, PAIR), slice(PAIR, PACK)
-        end0, end1 = POOL_END
-
-        head = placed("head", [P, PAIR, FIRST], F32, at_lower0)
-        lower0 = placed("lower0", [P, PAIR, end0 - FIRST], F32, at_lower0 + FIRST * PAIR * 4)
-        upper0 = placed("upper0", [P, PAIR, end0], F32, at_upper0)
-        vector_gather(head[:, 0], 0, 0, 0, FIRST)
-        scalar_gather(lower0[:, 0], 0, 0, FIRST, end0)
-        vector_gather(head[:, 1], 0, 1, 0, FIRST)
-        vector_gather(lower0[:, 1], 0, 1, FIRST, end0)
-        scalar_gather(upper0[:, 0], 0, 2, 0, end0)
-        vector_gather(upper0[:, 1], 0, 3, 0, end0)
-        gpsimd_weave(head[:], 0, lower, 0, gate_long[:, :FIRST])
-        gpsimd_weave(lower0[:], 0, lower, FIRST, gate_long[:, FIRST:end0])
-        gpsimd_weave(upper0[:], 0, upper, 0, gate_long[:, :end0])
-        wide = scalar_unit("wide", 1, end1, LONG_END[1], at_wide)
-        for rows, name, offset in ((lower, "lower1", at_lower1), (upper, "upper1", at_lower0)):
-            raw = placed(name, [P, PAIR, end1], F32, offset)
+        for rows in (slice(0, PAIR), slice(PAIR, PACK)):
+            head = placed(f"head{rows.start}", [P, PAIR, FIRST], F32, at_short + rows.start * FIRST * 4)
             for r in range(rows.start, rows.stop):
-                vector_gather(raw[:, r - rows.start], 1, r, 0, end1)
-            gpsimd_weave(raw[:], 1, rows, 0, gate_long[:, :end1])
-        narrow = scalar_unit("narrow", 0, end0, LONG_END[0], at_upper0)
+                vector_gather(head[:, r - rows.start], 0, r, 0, FIRST)
+            gpsimd_weave(head[:], 0, rows, 0, gate_long[:, :FIRST])
+        second = unit("second", 0, FIRST, end0, at_second, (3,))
+        gpsimd_weave(second[:], 0, slice(0, PACK), FIRST, gate_long[:, FIRST:end0])
+        third = unit("third", 1, 0, end1, at_third, (0, 2))
+        gpsimd_weave(third[:], 1, slice(0, PACK), 0, gate_long[:, :end1])
+        wide = unit("wide", 1, end1, LONG_END[1], at_wide, (1, 3))
+        narrow = unit("narrow", 0, end0, LONG_END[0], at_narrow, (3,))
         vector_weave(wide[:], 1, end1)
         vector_weave(narrow[:], 0, end0)
-        short0 = scalar_unit("short0", 0, LONG_END[0], S, at_lower1)
-        short1 = scalar_unit("short1", 1, LONG_END[1], S, at_lower0)
+        short0 = unit("short0", 0, LONG_END[0], S, at_short)
+        short1 = unit("short1", 1, LONG_END[1], S, at_third)
 
         codes = [
             (0, placed("codes_long", [P, LONG], U32, at_wide)),
-            (LONG, placed("codes_short", [P, PASSES * S - LONG], U32, at_upper0)),
+            (LONG, placed("codes_short", [P, PASSES * S - LONG], U32, at_narrow)),
         ]
         scales = keep.tile([P, PASSES * S], U8, align_bytes=64)
         done = []
-        sums_of = {}
-        groups = [(lo, min(lo + BANK, LONG_END[0]), lo // BANK) for lo in range(0, LONG_END[0], BANK)]
-        late = [*range(LONG_END[0], S, C), S - P]
-        for lo, hi, j in zip(late, late[1:] + [S], (6, 7, 0, 1, 2, 3)):
-            groups.append((lo, hi, j))
+        banks = {}
+        bank_of = {}
 
-        def multiply(lo, hi, sums, later_first):
-            order = sorted(range(PASSES), key=lambda a: done.index(column(a, lo)), reverse=later_first)
-            for n, a in enumerate(order):
-                matrix = lo // C * PASSES + a
-                first, end = column(a, lo), column(a, lo) + hi - lo
-                nc.tensor.matmul_mx(
-                    out=sums,
-                    lhsT=w_codes[:, matrix, :].bitcast(FP8X4),
-                    lhsT_scale=w_scale[:, matrix, :],
-                    rhs=columns(codes, first, end).bitcast(FP8X4),
-                    rhs_scale=scales[:, first:end],
-                    start=(n == 0),
-                    stop=(n == PASSES - 1),
-                )
-            sums_of[lo] = (hi, sums)
+        def multiply(a, lo, hi, start, stop):
+            first, j = bank_of[lo]
+            matrix = lo // C * PASSES + a
+            col = column(a, lo)
+            nc.tensor.matmul_mx(
+                out=banks[first, j][:, lo - first : hi - first],
+                lhsT=w_codes[:, matrix, :].bitcast(FP8X4),
+                lhsT_scale=w_scale[:, matrix, :],
+                rhs=columns(codes, col, col + hi - lo).bitcast(FP8X4),
+                rhs_scale=scales[:, col : col + hi - lo],
+                start=start,
+                stop=stop,
+            )
+
+        def open_bank(j, first, end):
+            banks[first, j] = psum.tile([N, end - first], F32, tag=f"bank{j}", name=f"sums{first}")
+            for lo in range(first, end, P):
+                bank_of[lo] = (first, j)
 
         def quantise(lo, hi):
             nc.vector.quantize_mx(
@@ -262,27 +252,28 @@ def tile_moe_pre_lin_silu_kernel(
                 in_=columns(woven, lo, hi).rearrange("p c r -> p (c r)"),
             )
             done.extend(range(lo, hi, P))
-            for first, end, j in groups:
-                ready = all(column(a, slot) in done for a in range(PASSES) for slot in range(first, end, P))
-                if ready and first not in sums_of:
-                    bank = psum.tile([N, end - first], F32, tag=f"bank{j}", name=f"sums{first}")
-                    waits_for_silu = LONG_END[0] <= first < LONG_END[1] and j not in gate_banks
-                    for start in range(first, end, C):
-                        stop = min(start + C, end)
-                        multiply(start, stop, bank[:, start - first : stop - first], waits_for_silu)
 
         cuts = [*range(0, LONG - CALL, CALL), LONG - CALL, LONG]
         for lo, hi in zip(cuts, cuts[1:]):
             quantise(lo, hi)
+            for first in range(0, LONG_END[0], BANK):
+                end = min(first + BANK, LONG_END[0])
+                ready = all(column(a, slot) in done for a in range(PASSES) for slot in range(first, end, P))
+                if ready and first not in bank_of:
+                    open_bank(first // BANK, first, end)
+                    for expert_first in range(first, end, C):
+                        for a in range(PASSES):
+                            multiply(a, expert_first, expert_first + C, a == 0, a == PASSES - 1)
 
         y = placed("y", [N, S], F32, at_wide - S * 4)
 
-        def activate(lo):
-            hi, sums = sums_of[lo]
+        def activate(lo, hi):
+            first, j = bank_of[lo]
+            sums = banks[first, j][:, lo - first : hi - first]
             nc.scalar.activation(y[:, lo:hi], sums, SILU, bias=bias[:, lo // C : lo // C + 1])
 
         for lo in range(0, LONG_END[0], C):
-            activate(lo)
+            activate(lo, lo + C)
 
         woven.append((LONG, placed("woven_short", [P, PASSES * S - LONG, PACK], BF16, at_woven)))
         first, end = SHORT_POOL[0] - LONG_END[0], SHORT_POOL[1] - LONG_END[0]
@@ -290,12 +281,27 @@ def tile_moe_pre_lin_silu_kernel(
         vector_weave(short0[:, :, :first], 0, LONG_END[0])
         vector_weave(short0[:, :, end:], 0, SHORT_POOL[1])
         vector_weave(short1[:], 1, LONG_END[1])
-        short_calls = [(0, LONG_END[0], SHORT_POOL[0]), (0, SHORT_POOL[0], S - C), (1, LONG_END[1], S - C)]
-        short_calls = short_calls + [(0, S - C, S), (1, S - C, S - P), (1, S - P, S)]
-        for a, lo, hi in short_calls:
-            quantise(column(a, lo), column(a, lo) + hi - lo)
-        for lo in late:
-            activate(lo)
+        e11, e12, e13, e14, e15, half = 11 * C, 12 * C, 13 * C, 14 * C, 15 * C, S - P
+        for j, first, end in ((6, e11, e13), (7, e13, e14), (0, e14, e15), (1, e15, half), (2, half, S)):
+            open_bank(j, first, end)
+        multiply(1, e11, e12, True, False)
+        multiply(1, e12, e13, False, False)
+        multiply(1, e13, e14, True, False)
+        for lo in (e11, e12, e13):
+            quantise(column(0, lo), column(0, lo) + C)
+            multiply(0, lo, lo + C, False, lo != e11)
+        for a in range(PASSES):
+            quantise(column(a, e14), column(a, e14) + C)
+            multiply(a, e14, e15, a == 0, a == 1)
+        quantise(column(0, e15), column(0, e15) + C)
+        for lo, hi in ((e15, half), (half, S)):
+            multiply(0, lo, hi, True, False)
+        for lo, hi in ((e15, half), (half, S)):
+            quantise(column(1, lo), column(1, lo) + P)
+            multiply(1, lo, hi, False, True)
+        late = (e11, e12, e13, e14, e15, half, S)
+        for lo, hi in zip(late, late[1:]):
+            activate(lo, hi)
 
         def result(j, part):
             return y[:].indirect(token_slots[j][:, part.start // LIST : part.stop // LIST])

@@ -33,10 +33,11 @@ CALL = 1024
 PAIR = 2
 LINE = 4
 
-FIRST = 576
-POOL_END = (7 * C, 1952)
+FIRST = 640
+HELP = 320
+POOL_END = (7 * C, 1824)
 LONG_END = (11 * C, 14 * C)
-SHORT_POOL = (LONG_END[0] + BANK, LONG_END[0] + BANK + 576)
+SHORT_POOL = (LONG_END[0] + BANK, LONG_END[0] + BANK + 544)
 GATE_BANKS = [(7 * C, 9 * C, 4), (9 * C, 11 * C, 5), (11 * C, 13 * C, 6), (13 * C, 14 * C, 3), (14 * C, S, 7)]
 LONG = sum(LONG_END)
 W_CUTS = (0, 3, 6, 9, 12, 14, 16)
@@ -111,8 +112,8 @@ def tile_moe_pre_lin_silu_kernel(
         nc.sync.dma_start(slot_tokens[:], offs)
         load_plane(0, 0)
         load_plane(0, 1)
-        nc.sync.dma_start(gate_long[:, :FIRST], gate[:P, :FIRST])
         load_plane(0, 2)
+        nc.sync.dma_start(gate_long[:, :FIRST], gate[:P, :FIRST])
         load_plane(0, 3)
         nc.sync.dma_start(gate_long[:, FIRST:], gate[:P, FIRST : max(POOL_END)])
         for r in range(PACK):
@@ -211,7 +212,12 @@ def tile_moe_pre_lin_silu_kernel(
         third = unit("third", 1, 0, end1, at_third, (0, 2))
         gpsimd_weave(third[:], 1, slice(0, PACK), 0, gate_long[:, :end1])
         wide = unit("wide", 1, end1, LONG_END[1], at_wide, (1, 3))
-        narrow = unit("narrow", 0, end0, LONG_END[0], at_narrow, (3,))
+        narrow = placed("narrow", [P, PACK, LONG_END[0] - end0], F32, at_narrow)
+        cut = LONG_END[0] - HELP
+        for r in range(PACK - 1):
+            scalar_gather(narrow[:, r], 0, r, end0, LONG_END[0])
+        vector_gather(narrow[:, PACK - 1, : cut - end0], 0, PACK - 1, end0, cut)
+        scalar_gather(narrow[:, PACK - 1, cut - end0 :], 0, PACK - 1, cut, LONG_END[0])
         vector_weave(wide[:], 1, end1)
         vector_weave(narrow[:], 0, end0)
         short0 = unit("short0", 0, LONG_END[0], S, at_short)

@@ -34,11 +34,11 @@ PAIR = 2
 LINE = 4
 
 FIRST = 640
-HELP = 320
-POOL_END = (7 * C, 1824)
-LONG_END = (11 * C, 14 * C)
-SHORT_POOL = (LONG_END[0] + BANK, LONG_END[0] + BANK + 544)
-GATE_BANKS = [(7 * C, 9 * C, 4), (9 * C, 11 * C, 5), (11 * C, 13 * C, 6), (13 * C, 14 * C, 3), (14 * C, S, 7)]
+HELP = 608
+POOL_END = (7 * C, 1856)
+LONG_END = (11 * C, S - 3 * P)
+SHORT_POOL = (LONG_END[0] + BANK, LONG_END[0] + 2 * BANK)
+GATE_BANKS = [(7 * C, 9 * C, 4), (9 * C, 11 * C, 5), (11 * C, 13 * C, 6), (13 * C, LONG_END[1], 3), (LONG_END[1], S, 7)]
 LONG = sum(LONG_END)
 W_CUTS = (0, 3, 6, 9, 12, 14, 16)
 OWN, WIDE, MIDDLE, NARROW = slice(0, 256), slice(256, 640), slice(640, 896), slice(896, T)
@@ -115,9 +115,11 @@ def tile_moe_pre_lin_silu_kernel(
         load_plane(0, 2)
         nc.sync.dma_start(gate_long[:, :FIRST], gate[:P, :FIRST])
         load_plane(0, 3)
+        load_plane(1, 0)
+        load_plane(1, 1)
         nc.sync.dma_start(gate_long[:, FIRST:], gate[:P, FIRST : max(POOL_END)])
-        for r in range(PACK):
-            load_plane(1, r)
+        load_plane(1, 2)
+        load_plane(1, 3)
         gate_rows = placed("gate_rows", [P, P], F32, at_rows)
         nc.sync.dma_start(gate_rows[:], gate[: P * P // S].rearrange("k (c q) -> (k c) q", q=P))
         nc.sync.dma_start(gate_short[:], gate[:P, SHORT_POOL[0] : SHORT_POOL[1]])
@@ -266,10 +268,11 @@ def tile_moe_pre_lin_silu_kernel(
                 end = min(first + BANK, LONG_END[0])
                 ready = all(column(a, slot) in done for a in range(PASSES) for slot in range(first, end, P))
                 if ready and first not in bank_of:
-                    open_bank(first // BANK, first, end)
+                    held = end == LONG_END[0]
+                    open_bank(0 if held else first // BANK, first, end)
                     for expert_first in range(first, end, C):
-                        for a in range(PASSES):
-                            multiply(a, expert_first, expert_first + C, a == 0, a == PASSES - 1)
+                        for n, a in enumerate(sorted(range(PASSES), reverse=held)):
+                            multiply(a, expert_first, expert_first + C, n == 0, n == PASSES - 1)
 
         y = placed("y", [N, S], F32, at_wide - S * 4)
 
@@ -288,23 +291,24 @@ def tile_moe_pre_lin_silu_kernel(
         vector_weave(short0[:, :, end:], 0, SHORT_POOL[1])
         vector_weave(short1[:], 1, LONG_END[1])
         e11, e12, e13, e14, e15, half = 11 * C, 12 * C, 13 * C, 14 * C, 15 * C, S - P
-        for j, first, end in ((6, e11, e13), (7, e13, e14), (0, e14, e15), (1, e15, half), (2, half, S)):
+        both = LONG_END[1]
+        for j, first, end in ((6, e11, e13), (7, e13, e14), (5, e14, e15), (1, e15, half), (2, half, S)):
             open_bank(j, first, end)
+        multiply(1, e14, both, True, False)
         multiply(1, e11, e12, True, False)
         multiply(1, e12, e13, False, False)
         multiply(1, e13, e14, True, False)
         for lo in (e11, e12, e13):
             quantise(column(0, lo), column(0, lo) + C)
             multiply(0, lo, lo + C, False, lo != e11)
-        for a in range(PASSES):
-            quantise(column(a, e14), column(a, e14) + C)
-            multiply(a, e14, e15, a == 0, a == 1)
-        quantise(column(0, e15), column(0, e15) + C)
-        for lo, hi in ((e15, half), (half, S)):
-            multiply(0, lo, hi, True, False)
-        for lo, hi in ((e15, half), (half, S)):
-            quantise(column(1, lo), column(1, lo) + P)
-            multiply(1, lo, hi, False, True)
+        for first in (e14, e15):
+            quantise(column(0, first), column(0, first) + C)
+            for lo in (first, first + P):
+                multiply(0, lo, lo + P, first == e15, False)
+        for first, end in ((both, half), (half, S)):
+            quantise(column(1, first), column(1, first) + end - first)
+            for lo in range(first, end, P):
+                multiply(1, lo, lo + P, False, True)
         late = (e11, e12, e13, e14, e15, half, S)
         for lo, hi in zip(late, late[1:]):
             activate(lo, hi)

@@ -34,8 +34,8 @@ PAIR = 2
 LINE = 4
 
 FIRST = 640
-HELP = 608
-POOL_END = (7 * C, 1856)
+HELP = 544
+POOL_END = (7 * C, 1888)
 LONG_END = (11 * C, S - 3 * P)
 SHORT_POOL = (LONG_END[0] + BANK, LONG_END[0] + 2 * BANK)
 GATE_BANKS = [(7 * C, 9 * C, 4), (9 * C, 11 * C, 5), (11 * C, 13 * C, 6), (13 * C, LONG_END[1], 3), (LONG_END[1], S, 7)]
@@ -274,7 +274,7 @@ def tile_moe_pre_lin_silu_kernel(
                         for n, a in enumerate(sorted(range(PASSES), reverse=held)):
                             multiply(a, expert_first, expert_first + C, n == 0, n == PASSES - 1)
 
-        y = placed("y", [N, S], F32, at_wide - S * 4)
+        y = placed("y", [N, S], F32, at_wide - (widths[1] + S) * 4)
 
         def activate(lo, hi):
             first, j = bank_of[lo]
@@ -317,7 +317,7 @@ def tile_moe_pre_lin_silu_kernel(
             return y[:].indirect(token_slots[j][:, part.start // LIST : part.stop // LIST])
 
         fetched = placed("fetched", [N, TOP - 1, T], F32, at_planes)
-        totals = placed("totals", [N, TOP, T], F32, at_planes + (TOP - 1) * T * 4)
+        totals = placed("totals", [N, TOP, T], F32, at_third)
         for j, parts in enumerate(((NARROW, MIDDLE, WIDE), (slice(OWN.stop, T),), (WIDE, MIDDLE, NARROW))):
             for part in parts:
                 nc.scalar.activation(fetched[:, j, part], result(j, part), COPY)

@@ -34,8 +34,8 @@ PAIR = 2
 LINE = 4
 
 FIRST = 640
-HELP = 544
-POOL_END = (7 * C, 1888)
+HELP = 672
+POOL_END = (7 * C, 1920)
 LONG_END = (11 * C, S - 3 * P)
 SHORT_POOL = (LONG_END[0] + BANK, LONG_END[0] + 2 * BANK)
 GATE_BANKS = [(7 * C, 9 * C, 4), (9 * C, 11 * C, 5), (11 * C, 13 * C, 6), (13 * C, LONG_END[1], 3), (LONG_END[1], S, 7)]
@@ -301,13 +301,12 @@ def tile_moe_pre_lin_silu_kernel(
         for lo in (e11, e12, e13):
             quantise(column(0, lo), column(0, lo) + C)
             multiply(0, lo, lo + C, False, lo != e11)
-        for first in (e14, e15):
+        for first, pieces in ((e14, (both,)), (e15, (e15, half))):
             quantise(column(0, first), column(0, first) + C)
             for lo in (first, first + P):
                 multiply(0, lo, lo + P, first == e15, False)
-        for first, end in ((both, half), (half, S)):
-            quantise(column(1, first), column(1, first) + end - first)
-            for lo in range(first, end, P):
+            for lo in pieces:
+                quantise(column(1, lo), column(1, lo) + P)
                 multiply(1, lo, lo + P, False, True)
         late = (e11, e12, e13, e14, e15, half, S)
         for lo, hi in zip(late, late[1:]):

@@ -34,7 +34,7 @@ PAIR = 2
 LINE = 4
 
 FIRST = 640
-HELP = 672
+HELP = 544
 POOL_END = (7 * C, 1920)
 LONG_END = (11 * C, S - 3 * P)
 SHORT_POOL = (LONG_END[0] + BANK, LONG_END[0] + 2 * BANK)

@@ -38,7 +38,10 @@ HELP = 544
 POOL_END = (7 * C, 1920)
 LONG_END = (11 * C, S - 3 * P)
 SHORT_POOL = (LONG_END[0] + BANK, LONG_END[0] + 2 * BANK)
-GATE_BANKS = [(7 * C, 9 * C, 4), (9 * C, 11 * C, 5), (11 * C, 13 * C, 6), (13 * C, LONG_END[1], 3), (LONG_END[1], S, 7)]
+GATE_BANKS = [(7 * C, 9 * C, 2), (9 * C, 11 * C, 3), (11 * C, 13 * C, 6), (13 * C, LONG_END[1], 4), (LONG_END[1], S, 7)]
+SPARE_BANK = (SHORT_POOL[1], S, 5)
+LONG_SUMS = [(0, 2 * C, 0), (2 * C, 4 * C, 1), (4 * C, 6 * C, 2), (6 * C, 7 * C, 3)]
+HELD_SUMS = [(7 * C, 9 * C, 6), (9 * C, 11 * C, 5)]
 LONG = sum(LONG_END)
 W_CUTS = (0, 3, 6, 9, 12, 14, 16)
 OWN, WIDE, MIDDLE, NARROW = slice(0, 256), slice(256, 640), slice(640, 896), slice(896, T)
@@ -144,7 +147,7 @@ def tile_moe_pre_lin_silu_kernel(
         gate_cols = placed("gate_cols", [P, S // P], F32, at_third - S // P * 4)
         nc.vector.tensor_copy(gate_cols[:], turned[:, : S // P])
         gate_banks = {}
-        for first, end, j in GATE_BANKS:
+        for first, end, j in GATE_BANKS + [SPARE_BANK]:
             bank = psum.tile([P, end - first], F32, tag=f"bank{j}", name=f"gate_bank{j}")
             for lo in range(first, end, P):
                 spread = gate_cols[:, lo // P : lo // P + 1].to_broadcast([P, P])
@@ -179,9 +182,9 @@ def tile_moe_pre_lin_silu_kernel(
         def woven_slots(a, lo, hi):
             return columns(woven, column(a, lo), column(a, lo) + hi - lo)
 
-        def vector_weave(raw, a, lo):
+        def vector_weave(raw, a, lo, sources=GATE_BANKS):
             hi = lo + raw.shape[2]
-            for bank_first, bank_end, j in GATE_BANKS:
+            for bank_first, bank_end, j in sources:
                 first, end = max(lo, bank_first), min(hi, bank_end)
                 if first >= end:
                     continue
@@ -253,6 +256,12 @@ def tile_moe_pre_lin_silu_kernel(
             for lo in range(first, end, P):
                 bank_of[lo] = (first, j)
 
+        def multiply_whole(first, end, j):
+            open_bank(j, first, end)
+            for lo in range(first, end, C):
+                for a in range(PASSES):
+                    multiply(a, lo, lo + C, a == 0, a == PASSES - 1)
+
         def quantise(lo, hi):
             nc.vector.quantize_mx(
                 out=columns(codes, lo, hi).bitcast(FP8X4),
@@ -264,15 +273,10 @@ def tile_moe_pre_lin_silu_kernel(
         cuts = [*range(0, LONG - CALL, CALL), LONG - CALL, LONG]
         for lo, hi in zip(cuts, cuts[1:]):
             quantise(lo, hi)
-            for first in range(0, LONG_END[0], BANK):
-                end = min(first + BANK, LONG_END[0])
+            for first, end, j in LONG_SUMS:
                 ready = all(column(a, slot) in done for a in range(PASSES) for slot in range(first, end, P))
                 if ready and first not in bank_of:
-                    held = end == LONG_END[0]
-                    open_bank(0 if held else first // BANK, first, end)
-                    for expert_first in range(first, end, C):
-                        for n, a in enumerate(sorted(range(PASSES), reverse=held)):
-                            multiply(a, expert_first, expert_first + C, n == 0, n == PASSES - 1)
+                    multiply_whole(first, end, j)
 
         y = placed("y", [N, S], F32, at_wide - (widths[1] + S) * 4)
 
@@ -281,33 +285,41 @@ def tile_moe_pre_lin_silu_kernel(
             sums = banks[first, j][:, lo - first : hi - first]
             nc.scalar.activation(y[:, lo:hi], sums, SILU, bias=bias[:, lo // C : lo // C + 1])
 
-        for lo in range(0, LONG_END[0], C):
+        for lo in range(0, HELD_SUMS[0][0], C):
             activate(lo, lo + C)
 
         woven.append((LONG, placed("woven_short", [P, PASSES * S - LONG, PACK], BF16, at_woven)))
         first, end = SHORT_POOL[0] - LONG_END[0], SHORT_POOL[1] - LONG_END[0]
         gpsimd_weave(short0[:, :, first:end], 0, slice(0, PACK), SHORT_POOL[0], gate_short[:])
         vector_weave(short0[:, :, :first], 0, LONG_END[0])
-        vector_weave(short0[:, :, end:], 0, SHORT_POOL[1])
+        vector_weave(short0[:, :, end:], 0, SHORT_POOL[1], [SPARE_BANK])
         vector_weave(short1[:], 1, LONG_END[1])
         e11, e12, e13, e14, e15, half = 11 * C, 12 * C, 13 * C, 14 * C, 15 * C, S - P
         both = LONG_END[1]
-        for j, first, end in ((6, e11, e13), (7, e13, e14), (5, e14, e15), (1, e15, half), (2, half, S)):
-            open_bank(j, first, end)
-        multiply(1, e14, both, True, False)
+        open_bank(4, e11, e13)
         multiply(1, e11, e12, True, False)
         multiply(1, e12, e13, False, False)
+        for first, end, j in HELD_SUMS:
+            multiply_whole(first, end, j)
+            for lo in range(first, end, C):
+                activate(lo, lo + C)
+        for j, first, end in ((7, e13, e14), (0, e14, e15), (1, e15, half), (2, half, S)):
+            open_bank(j, first, end)
         multiply(1, e13, e14, True, False)
         for lo in (e11, e12, e13):
             quantise(column(0, lo), column(0, lo) + C)
             multiply(0, lo, lo + C, False, lo != e11)
-        for first, pieces in ((e14, (both,)), (e15, (e15, half))):
-            quantise(column(0, first), column(0, first) + C)
-            for lo in (first, first + P):
-                multiply(0, lo, lo + P, first == e15, False)
-            for lo in pieces:
-                quantise(column(1, lo), column(1, lo) + P)
-                multiply(1, lo, lo + P, False, True)
+        quantise(column(0, e14), column(0, e14) + C)
+        multiply(0, e14, e15, True, False)
+        multiply(1, e14, both, False, False)
+        quantise(column(1, both), column(1, both) + P)
+        multiply(1, both, e15, False, True)
+        quantise(column(0, e15), column(0, e15) + C)
+        for lo in (e15, half):
+            multiply(0, lo, lo + P, True, False)
+        for lo in (e15, half):
+            quantise(column(1, lo), column(1, lo) + P)
+            multiply(1, lo, lo + P, False, True)
         late = (e11, e12, e13, e14, e15, half, S)
         for lo, hi in zip(late, late[1:]):
             activate(lo, hi)

from contextlib import ExitStack

import concourse.mybir as mybir

K, T, E, C, N = 1024, 1024, 16, 256, 128
TOP = 4
S = E * C
P = 128
PACK = 4
K_PASS = P * PACK
PASSES = K // K_PASS
LIST = 16
QUAD = 32

F32 = mybir.dt.float32
BF16 = mybir.dt.bfloat16
I32 = mybir.dt.int32
U32 = mybir.dt.uint32
U16 = mybir.dt.uint16
U8 = mybir.dt.uint8
FP8X4 = mybir.dt.float8_e4m3fn_x4
MULT = mybir.AluOpType.mult
ADD = mybir.AluOpType.add
EQUAL = mybir.AluOpType.is_equal
SILU = mybir.ActivationFunctionType.Silu
COPY = mybir.ActivationFunctionType.Copy

FLOPS = 2 * K * S * N
BYTES = K * T * 4 + E * K * N + E * K * N // 32 + N * E * 4 + S * 4 + P * (S + TOP * T) // LIST * 2 + N * T * 4

BANK = 512
CALL = 1024
PAIR = 2
LINE = 4

FIRST = 640
HELP = 544
POOL_END = (7 * C, 1920)
LONG_END = (11 * C, S - 3 * P)
SHORT_POOL = (LONG_END[0] + BANK, LONG_END[0] + 2 * BANK)
GATE_BANKS = [(7 * C, 9 * C, 2), (9 * C, 11 * C, 3), (11 * C, 13 * C, 6), (13 * C, LONG_END[1], 4), (LONG_END[1], S, 7)]
SPARE_BANK = (SHORT_POOL[1], S, 5)
LONG_SUMS = [(0, 2 * C, 0), (2 * C, 4 * C, 1), (4 * C, 6 * C, 2), (6 * C, 7 * C, 3)]
HELD_SUMS = [(7 * C, 9 * C, 6), (9 * C, 11 * C, 5)]
LONG = sum(LONG_END)
W_CUTS = (0, 3, 6, 9, 12, 14, 16)
OWN, WIDE, MIDDLE, NARROW = slice(0, 256), slice(256, 640), slice(640, 896), slice(896, T)


SPANS = [(0, 0, LONG_END[0]), (1, 0, 9 * C), (1, 13 * C, LONG_END[1]), (1, 9 * C, 13 * C)]
SPANS = SPANS + [(0, LONG_END[0], S), (1, LONG_END[1], S)]


def column(a, slot):
    first = 0
    for span_pass, lo, hi in SPANS:
        if span_pass == a and lo <= slot < hi:
            return first + slot - lo
        first = first + hi - lo


def tile_moe_pre_lin_silu_kernel(
    tc, xT, w_words, w_scales, b, gate, offs, pos1, pos2, pos3, pos4, out
):
    nc = tc.nc
    with ExitStack() as ctx:
        lists = ctx.enter_context(tc.tile_pool(name="lists", bufs=1))
        keep = ctx.enter_context(tc.tile_pool(name="keep", bufs=1))
        shared = ctx.enter_context(tc.tile_pool(name="shared", bufs=1))
        psum = ctx.enter_context(tc.psum_pool(name="psum", bufs=1))

        def placed(name, shape, dtype, offset):
            return shared.tile(shape, dtype, align_bytes=64, tag=name, name=name, offset=offset)

        end0, end1 = POOL_END
        widths = [S - LONG_END[0] + LIST, end1 + LIST]
        at_planes = 0
        at_wide = at_planes + PACK * 4 * sum(widths)
        at_narrow = at_wide + (LONG_END[1] - end1) * PACK * 4
        at_rows = at_narrow - P * 2
        at_second = at_rows + P * 4
        at_short = at_second + (end0 - FIRST) * PACK * 4
        at_third = at_short + (S - LONG_END[0]) * PACK * 4
        at_woven = at_third + end1 * PACK * 4

        planes = {}
        for a in range(PASSES):
            for r in range(PACK):
                offset = at_planes + (a * PACK * widths[0] + r * widths[a]) * 4
                planes[a, r] = placed(f"plane{a}{r}", [P, widths[a]], F32, offset)

        ones = keep.tile([P, QUAD], F32)
        nc.vector.memset(ones[:], 1.0)
        warm = keep.tile([P, 1], F32)
        nc.scalar.activation(warm[:], ones[:, :1], SILU)
        identity = keep.tile([P, P], F32)
        nc.vector.memset(identity[:], 0.0)
        counts = keep.tile([P, QUAD], F32, align_bytes=64)
        nc.vector.tensor_tensor_scan(counts[:], ones[:], ones[:], 0.0, MULT, ADD)
        w_scale = keep.tile([P, E * PASSES, N], U8, align_bytes=64)
        nc.vector.memset(w_scale[:].bitcast(I32), 0)
        turned_counts = keep.tile([P, QUAD], F32, align_bytes=64)
        nc.vector.transpose(turned_counts[:], counts[:])
        for start in range(0, P, QUAD):
            quadrant = slice(start, start + QUAD)
            nc.vector.tensor_tensor(identity[quadrant, quadrant], counts[quadrant, :], turned_counts[quadrant, :], EQUAL)

        def load_plane(a, r):
            rows = xT[a * K_PASS : (a + 1) * K_PASS, :].rearrange("(p r) t -> p r t", r=PACK)
            nc.sync.dma_start(planes[a, r][:, :T], rows[:, r, :])

        gate_long = keep.tile([P, max(POOL_END)], F32, align_bytes=64)
        gate_short = keep.tile([P, SHORT_POOL[1] - SHORT_POOL[0]], F32, align_bytes=64)
        slot_tokens = lists.tile([P, S // LIST], U16)
        nc.sync.dma_start(slot_tokens[:], offs)
        load_plane(0, 0)
        load_plane(0, 1)
        load_plane(0, 2)
        nc.sync.dma_start(gate_long[:, :FIRST], gate[:P, :FIRST])
        load_plane(0, 3)
        load_plane(1, 0)
        load_plane(1, 1)
        nc.sync.dma_start(gate_long[:, FIRST:], gate[:P, FIRST : max(POOL_END)])
        load_plane(1, 2)
        load_plane(1, 3)
        gate_rows = placed("gate_rows", [P, P], F32, at_rows)
        nc.sync.dma_start(gate_rows[:], gate[: P * P // S].rearrange("k (c q) -> (k c) q", q=P))
        nc.sync.dma_start(gate_short[:], gate[:P, SHORT_POOL[0] : SHORT_POOL[1]])
        scale_rows = w_scales.rearrange("e a (q r) n -> r q (e a) n", r=PACK)
        for r in range(PACK):
            nc.sync.dma_start(w_scale[r:P:QUAD].bitcast(I32), scale_rows[r].bitcast(I32))
        w_codes = keep.tile([P, E * PASSES, N * PACK], U8, align_bytes=64)
        words = w_words.rearrange("e a p n r -> p (e a) (n r)")
        for lo, hi in zip(W_CUTS, W_CUTS[1:]):
            part = slice(lo * PASSES, hi * PASSES)
            nc.sync.dma_start(w_codes[:, part].bitcast(I32), words[:, part].bitcast(I32))
        bias = keep.tile([N, E], F32)
        nc.sync.dma_start(bias[:], b)
        token_slots = []
        for j, pos in enumerate((pos1, pos2, pos3, pos4)):
            slots = lists.tile([P, T // LIST], U16, name=f"pos{j}")
            nc.sync.dma_start(slots[:], pos)
            token_slots.append(slots)

        turned = psum.tile([P, P], F32, tag="bank0")
        nc.tensor.transpose(turned[:], gate_rows[:], identity[:])
        gate_cols = placed("gate_cols", [P, S // P], F32, at_third - S // P * 4)
        nc.vector.tensor_copy(gate_cols[:], turned[:, : S // P])
        gate_banks = {}
        for first, end, j in GATE_BANKS + [SPARE_BANK]:
            bank = psum.tile([P, end - first], F32, tag=f"bank{j}", name=f"gate_bank{j}")
            for lo in range(first, end, P):
                spread = gate_cols[:, lo // P : lo // P + 1].to_broadcast([P, P])
                nc.tensor.transpose(bank[:, lo - first : lo - first + P], spread, identity[:])
            gate_banks[j] = bank

        def picked(a, r, lo, hi):
            return planes[a, r][:].indirect(slot_tokens[:, lo // LIST : hi // LIST])

        def vector_gather(raw, a, r, lo, hi):
            nc.vector.tensor_copy(raw, picked(a, r, lo, hi))

        def scalar_gather(raw, a, r, lo, hi):
            nc.scalar.activation(raw, picked(a, r, lo, hi), COPY)

        def unit(name, a, lo, hi, offset, by_vector=()):
            raw = placed(name, [P, PACK, hi - lo], F32, offset)
            for r in range(PACK):
                gather = vector_gather if r in by_vector else scalar_gather
                gather(raw[:, r], a, r, lo, hi)
            return raw

        woven = [
            (0, placed("woven_long", [P, LONG - CALL, PACK], BF16, at_woven)),
            (LONG - CALL, placed("woven_last", [P, CALL, PACK], BF16, at_woven + (LONG - CALL) * PACK * 2)),
        ]

        def columns(parts, lo, hi):
            first, tile = [part for part in parts if part[0] <= lo][-1]
            return tile[:, lo - first : hi - first]

        def woven_slots(a, lo, hi):
            return columns(woven, column(a, lo), column(a, lo) + hi - lo)

        def vector_weave(raw, a, lo, sources=GATE_BANKS):
            hi = lo + raw.shape[2]
            for bank_first, bank_end, j in sources:
                first, end = max(lo, bank_first), min(hi, bank_end)
                if first >= end:
                    continue
                weights = gate_banks[j][:, first - bank_first : end - bank_first]
                nc.vector.tensor_tensor(
                    woven_slots(a, first, end).rearrange("p (c i) r -> p c r i", i=PAIR),
                    raw[:, :, first - lo : end - lo].rearrange("p r (c i) -> p c r i", i=PAIR),
                    weights.rearrange("p (c i) -> p c i", i=PAIR)
                    .unsqueeze(2)
                    .to_broadcast([P, (end - first) // PAIR, PACK, PAIR]),
                    MULT,
                )

        def gpsimd_weave(raw, a, rows, lo, weights):
            count, width = raw.shape[1:]
            nc.gpsimd.tensor_tensor(
                woven_slots(a, lo, lo + width)[:, :, rows].rearrange("p (c i) r -> p c r i", i=LINE),
                raw.rearrange("p r (c i) -> p c r i", i=LINE),
                weights.rearrange("p (c i) -> p c i", i=LINE).unsqueeze(2).to_broadcast([P, width // LINE, count, LINE]),
                MULT,
            )

        for rows in (slice(0, PAIR), slice(PAIR, PACK)):
            head = placed(f"head{rows.start}", [P, PAIR, FIRST], F32, at_short + rows.start * FIRST * 4)
            for r in range(rows.start, rows.stop):
                vector_gather(head[:, r - rows.start], 0, r, 0, FIRST)
            gpsimd_weave(head[:], 0, rows, 0, gate_long[:, :FIRST])
        second = unit("second", 0, FIRST, end0, at_second, (3,))
        gpsimd_weave(second[:], 0, slice(0, PACK), FIRST, gate_long[:, FIRST:end0])
        third = unit("third", 1, 0, end1, at_third, (0, 2))
        gpsimd_weave(third[:], 1, slice(0, PACK), 0, gate_long[:, :end1])
        wide = unit("wide", 1, end1, LONG_END[1], at_wide, (1, 3))
        narrow = placed("narrow", [P, PACK, LONG_END[0] - end0], F32, at_narrow)
        cut = LONG_END[0] - HELP
        for r in range(PACK - 1):
            scalar_gather(narrow[:, r], 0, r, end0, LONG_END[0])
        vector_gather(narrow[:, PACK - 1, : cut - end0], 0, PACK - 1, end0, cut)
        scalar_gather(narrow[:, PACK - 1, cut - end0 :], 0, PACK - 1, cut, LONG_END[0])
        vector_weave(wide[:], 1, end1)
        vector_weave(narrow[:], 0, end0)
        short0 = unit("short0", 0, LONG_END[0], S, at_short)
        short1 = unit("short1", 1, LONG_END[1], S, at_third)

        codes = [
            (0, placed("codes_long", [P, LONG], U32, at_wide)),
            (LONG, placed("codes_short", [P, PASSES * S - LONG], U32, at_narrow)),
        ]
        scales = keep.tile([P, PASSES * S], U8, align_bytes=64)
        done = []
        banks = {}
        bank_of = {}

        def multiply(a, lo, hi, start, stop):
            first, j = bank_of[lo]
            matrix = lo // C * PASSES + a
            col = column(a, lo)
            nc.tensor.matmul_mx(
                out=banks[first, j][:, lo - first : hi - first],
                lhsT=w_codes[:, matrix, :].bitcast(FP8X4),
                lhsT_scale=w_scale[:, matrix, :],
                rhs=columns(codes, col, col + hi - lo).bitcast(FP8X4),
                rhs_scale=scales[:, col : col + hi - lo],
                start=start,
                stop=stop,
            )

        def open_bank(j, first, end):
            banks[first, j] = psum.tile([N, end - first], F32, tag=f"bank{j}", name=f"sums{first}")
            for lo in range(first, end, P):
                bank_of[lo] = (first, j)

        def multiply_whole(first, end, j):
            open_bank(j, first, end)
            for lo in range(first, end, C):
                for a in range(PASSES):
                    multiply(a, lo, lo + C, a == 0, a == PASSES - 1)

        def quantise(lo, hi):
            nc.vector.quantize_mx(
                out=columns(codes, lo, hi).bitcast(FP8X4),
                scales=scales[:, lo:hi],
                in_=columns(woven, lo, hi).rearrange("p c r -> p (c r)"),
            )
            done.extend(range(lo, hi, P))

        cuts = [*range(0, LONG - CALL, CALL), LONG - CALL, LONG]
        for lo, hi in zip(cuts, cuts[1:]):
            quantise(lo, hi)
            for first, end, j in LONG_SUMS:
                ready = all(column(a, slot) in done for a in range(PASSES) for slot in range(first, end, P))
                if ready and first not in bank_of:
                    multiply_whole(first, end, j)

        y = placed("y", [N, S], F32, at_wide - (widths[1] + S) * 4)

        def activate(lo, hi):
            first, j = bank_of[lo]
            sums = banks[first, j][:, lo - first : hi - first]
            nc.scalar.activation(y[:, lo:hi], sums, SILU, bias=bias[:, lo // C : lo // C + 1])

        for lo in range(0, HELD_SUMS[0][0], C):
            activate(lo, lo + C)

        woven.append((LONG, placed("woven_short", [P, PASSES * S - LONG, PACK], BF16, at_woven)))
        first, end = SHORT_POOL[0] - LONG_END[0], SHORT_POOL[1] - LONG_END[0]
        gpsimd_weave(short0[:, :, first:end], 0, slice(0, PACK), SHORT_POOL[0], gate_short[:])
        vector_weave(short0[:, :, :first], 0, LONG_END[0])
        vector_weave(short0[:, :, end:], 0, SHORT_POOL[1], [SPARE_BANK])
        vector_weave(short1[:], 1, LONG_END[1])
        e11, e12, e13, e14, e15, half = 11 * C, 12 * C, 13 * C, 14 * C, 15 * C, S - P
        both = LONG_END[1]
        open_bank(4, e11, e13)
        multiply(1, e11, e12, True, False)
        multiply(1, e12, e13, False, False)
        for first, end, j in HELD_SUMS:
            multiply_whole(first, end, j)
            for lo in range(first, end, C):
                activate(lo, lo + C)
        for j, first, end in ((7, e13, e14), (0, e14, e15), (1, e15, half), (2, half, S)):
            open_bank(j, first, end)
        multiply(1, e13, e14, True, False)
        for lo in (e11, e12, e13):
            quantise(column(0, lo), column(0, lo) + C)
            multiply(0, lo, lo + C, False, lo != e11)
        quantise(column(0, e14), column(0, e14) + C)
        multiply(0, e14, e15, True, False)
        multiply(1, e14, both, False, False)
        quantise(column(1, both), column(1, both) + P)
        multiply(1, both, e15, False, True)
        quantise(column(0, e15), column(0, e15) + C)
        for lo in (e15, half):
            multiply(0, lo, lo + P, True, False)
        for lo in (e15, half):
            quantise(column(1, lo), column(1, lo) + P)
            multiply(1, lo, lo + P, False, True)
        late = (e11, e12, e13, e14, e15, half, S)
        for lo, hi in zip(late, late[1:]):
            activate(lo, hi)

        def result(j, part):
            return y[:].indirect(token_slots[j][:, part.start // LIST : part.stop // LIST])

        fetched = placed("fetched", [N, TOP - 1, T], F32, at_planes)
        totals = placed("totals", [N, TOP, T], F32, at_third)
        for j, parts in enumerate(((NARROW, MIDDLE, WIDE), (slice(OWN.stop, T),), (WIDE, MIDDLE, NARROW))):
            for part in parts:
                nc.scalar.activation(fetched[:, j, part], result(j, part), COPY)
        nc.vector.tensor_copy(totals[:, 0, OWN], result(0, OWN))
        for j, part in enumerate((NARROW, MIDDLE, WIDE), start=1):
            nc.vector.tensor_tensor(totals[:, 0, part], result(TOP - 1, part), fetched[:, 0, part], ADD)
            nc.vector.tensor_tensor(totals[:, j, OWN], result(j, OWN), totals[:, j - 1, OWN], ADD)
        nc.sync.dma_start(out[:, OWN], totals[:, TOP - 1, OWN])
        for part in (WIDE, slice(WIDE.stop, T)):
            nc.vector.tensor_tensor(totals[:, 1, part], totals[:, 0, part], fetched[:, 1, part], ADD)
        for part in (WIDE, MIDDLE, NARROW):
            nc.vector.tensor_tensor(totals[:, 2, part], totals[:, 1, part], fetched[:, 2, part], ADD)
            nc.sync.dma_start(out[:, part], totals[:, 2, part])
